import numpy as np
import ml_dtypes


def mxq(x, axis, fmt="e4m3"):
    dtype, down = {"e4m3": (ml_dtypes.float8_e4m3fn, 7), "e5m2": (ml_dtypes.float8_e5m2, 14)}[fmt]
    v = np.moveaxis(np.asarray(x, np.float32).astype(ml_dtypes.bfloat16).astype(np.float64), axis, -1)
    blocks = v.reshape(v.shape[:-1] + (-1, 32))
    amax = np.abs(blocks).max(-1, keepdims=True)
    byte = np.maximum(np.where(amax > 0, np.frexp(amax)[1] - 1 + 127, 0) - down, 1)
    scale = np.exp2(byte - 127.0)
    codes = (blocks / scale).astype(np.float32).astype(dtype).astype(np.float64)
    return np.moveaxis((codes * scale).reshape(v.shape), -1, axis)


WIDE = False


def mx_kscale(k):
    if not WIDE:
        return np.ones(k)
    levels = np.array([30, -30])
    if k % 512:
        return np.exp2(np.random.permutation(np.resize(levels, k // 32))).repeat(32)
    a = np.empty((k // 512, 16))
    for p in range(k // 512):
        a[p, :8] = np.random.permutation(np.resize(levels, 8))
        for g in range(8):
            far = levels[np.abs(levels - a[p, g]) >= 10]
            a[p, g + 8] = far[np.random.randint(len(far))]
    return np.exp2(a.ravel()).repeat(32)


BF16 = ml_dtypes.bfloat16


def bf(x):
    return np.asarray(x, np.float32).astype(BF16)


def f64(x):
    return np.asarray(x).astype(np.float64)


E2M1 = np.array([0.0, 0.5, 1.0, 1.5, 2.0, 3.0, 4.0, 6.0, -0.0, -0.5, -1.0, -1.5, -2.0, -3.0, -4.0, -6.0])


def pack_weight(w, fmt):
    k, n = w.shape
    w = f64(bf(w)).reshape(k // 32, 32, n)
    amax = np.abs(w).max(1)
    if fmt == "e4m3":
        byte = np.frexp(amax)[1] - 1 + 127 - 7
    else:
        mant, ex = np.frexp(amax / 6.0)
        byte = np.where(mant > 0.5, ex, ex - 1) + 127
    byte = np.clip(np.where(amax > 0, byte, 1), 1, 254)
    scaled = (w * np.exp2(127.0 - byte)[:, None, :]).reshape(k, n).astype(np.float32)
    by_word = np.ascontiguousarray(scaled.reshape(k // 512, 128, 4, n).transpose(0, 1, 3, 2))
    if fmt == "e4m3":
        words = by_word.astype(ml_dtypes.float8_e4m3fn).view(np.uint8)
    else:
        c = by_word.astype(ml_dtypes.float4_e2m1fn).view(np.uint8) & 0xF
        words = c[..., 0::2] | (c[..., 1::2] << 4)
    return np.ascontiguousarray(words), np.ascontiguousarray(byte.astype(np.uint8).reshape(k // 512, 16, n))


def unpack_weight(words, scales, fmt):
    g, p, n, _ = words.shape
    if fmt == "e4m3":
        vals = np.ascontiguousarray(words).view(ml_dtypes.float8_e4m3fn).astype(np.float64)
    else:
        nib = np.empty((g, p, n, 4), np.uint8)
        nib[..., 0::2] = words & 0xF
        nib[..., 1::2] = words >> 4
        vals = E2M1[nib]
    vals = vals * np.repeat(np.exp2(scales.astype(np.float64) - 127.0), 8, axis=1)[..., None]
    return vals.transpose(0, 1, 3, 2).reshape(g * 512, n)
def pack4(w):
    words, scales = pack_weight(w, "e2m1")
    return words.reshape(words.shape[0], 128, -1), scales


def unpack4(words, scales):
    return unpack_weight(words.reshape(words.shape[0], 128, -1, 2), scales, "e2m1")


M, K, N = 1024, 1024, 2048


def setup_inputs():
    s, t = mx_kscale(K), mx_kscale(N)
    taps = np.random.standard_normal(N) / np.sqrt(K)
    shift = np.arange(N)[None, :] - (N // K) * np.arange(K)[:, None]
    h = taps[shift % N]
    h_words, h_scales = pack4(h / s[:, None])
    return {"lam": bf(np.random.standard_normal((M, K))),
            "amp": bf((1 + 0.1 * np.random.standard_normal(K)) * s),
            "h_words": h_words,
            "h_scales": h_scales,
            "y": bf(np.random.standard_normal((M, N))),
            "v": bf((1 + 0.1 * np.random.standard_normal(N)) * t),
            "f": bf(np.random.standard_normal((N, K)) / np.sqrt(N) / t[:, None])}


def reference(lam, amp, h_words, h_scales, y, v, f):
    h = unpack4(h_words, h_scales)
    x = np.tanh(f64(lam)) * f64(amp)
    z = mxq(x, 1, "e4m3") @ h
    r = (f64(y) - z) * f64(v)
    d = mxq(r, 1, "e5m2") @ mxq(f64(f), 0, "e4m3")
    return f64(lam) + d

@@ -1,0 +1,312 @@
+from contextlib import ExitStack
+
+import concourse.mybir as mybir
+from concourse.masks import make_identity
+
+F32 = mybir.dt.float32
+BF16 = mybir.dt.bfloat16
+I32 = mybir.dt.int32
+U32 = mybir.dt.uint32
+U8 = mybir.dt.uint8
+E4M3X4 = mybir.dt.float8_e4m3fn_x4
+E5M2X4 = mybir.dt.float8_e5m2_x4
+E2M1X4 = mybir.dt.float4_e2m1fn_x4
+ALU = mybir.AluOpType
+COPY = mybir.ActivationFunctionType.Copy
+TANH = mybir.ActivationFunctionType.Tanh
+
+M, K, N = 1024, 1024, 2048
+P = 128
+FLOPS = 2 * M * K * N * 2
+TILES = M // P
+KG = K // 512
+NG = N // 512
+X_ON_V = 8
+F_ON_V = ()
+TURN, Z = 3, 3
+S_BLOCKS = {3: (1, 3), 4: (0, 1, 2, 3), 5: (0, 1, 2, 3), 6: (0, 1, 2, 3), 7: (0, 1, 2, 3)}
+F_STEPS = (1, 1, 1, 1)
+
+
+def tile_ftn_residual_turn_s9_kernel(tc, lam, amp, h_words, h_scales, y, v, f, out):
+    nc = tc.nc
+    with ExitStack() as ctx:
+        keep = ctx.enter_context(tc.tile_pool(name="keep", bufs=1))
+        work = ctx.enter_context(tc.tile_pool(name="work", bufs=2))
+        psum = ctx.enter_context(tc.psum_pool(name="psum", bufs=2))
+
+        warm = keep.tile([P, 1], F32)
+        nc.vector.memset(warm[:], 0.0)
+        warm_out = keep.tile([P, 1], F32)
+        nc.scalar.activation(out=warm_out[:], in_=warm[:], func=TANH)
+        hs = keep.tile([P, KG, N], U8, align_bytes=64)
+        nc.vector.memset(hs[:].rearrange("p g n -> p (g n)").bitcast(I32), 0)
+        ident = keep.tile([P, P], F32, align_bytes=64)
+        make_identity(nc, ident[:])
+
+        v_turned = keep.tile([P, NG, 4], BF16, align_bytes=64)
+        amp_sb = keep.tile([P, KG, 4], BF16, align_bytes=64)
+        hw = keep.tile([P, KG, 2 * N], U8, align_bytes=64)
+        lam_sb = keep.tile([P, TILES, K], BF16, align_bytes=64)
+        f_raw = keep.tile([P, 2, NG, 4, 512], BF16, align_bytes=64)
+
+        y_t = {}
+
+        def load_lam(i):
+            nc.sync.dma_start(out=lam_sb[:, i, :], in_=lam[P * i : P * (i + 1), :])
+
+        def load_y(i):
+            y_t[i] = work.tile([P, N], BF16, name="y_in", bufs=8, align_bytes=64)
+            nc.sync.dma_start(out=y_t[i][:], in_=y[P * i : P * (i + 1), :])
+
+        def load_f(kh, g):
+            cols = slice(512 * kh, 512 * (kh + 1))
+            nc.sync.dma_start(
+                out=f_raw[:, kh, g], in_=f[512 * g : 512 * (g + 1), cols].rearrange("(p j) k -> p j k", j=4)
+            )
+
+        def load_h(half):
+            cols = slice(N * half, N * (half + 1))
+            nc.sync.dma_start(
+                out=hw[:, :, cols].bitcast(I32), in_=h_words[:, :, cols].rearrange("g p c -> p g c").bitcast(I32)
+            )
+
+        nc.scalar.dma_start(out=amp_sb[:], in_=amp.rearrange("(g p t) -> p g t", g=KG, t=4))
+        load_lam(0)
+        load_lam(1)
+        for q in range(4):
+            nc.sync.dma_start(
+                out=hs[32 * q : 32 * q + 4].bitcast(I32),
+                in_=h_scales[:, 4 * q : 4 * q + 4, :].rearrange("g r n -> r g n").bitcast(I32),
+            )
+        load_h(0)
+        load_y(0)
+        load_h(1)
+        nc.sync.dma_start(out=v_turned[:], in_=v.rearrange("(g p t) -> p g t", g=NG, t=4))
+        load_lam(2)
+        load_y(1)
+        load_f(0, 0)
+        load_f(0, 1)
+        load_lam(3)
+        load_f(0, 2)
+        load_f(0, 3)
+        load_y(2)
+        load_lam(4)
+        for g in range(NG):
+            load_f(1, g)
+        load_y(3)
+        for i in range(5, TILES):
+            load_lam(i)
+            load_y(i - 1)
+        load_y(TILES - 1)
+
+        v_col = keep.tile([P, NG, 4], F32)
+        nc.vector.tensor_copy(out=v_col[:], in_=v_turned[:])
+        f_codes = keep.tile([P, 2, NG, 512], U32, align_bytes=64)
+        f_scales = keep.tile([P, 2, NG, 512], U8, align_bytes=64)
+
+        xt, xf_t, xb_t, xc_t, xs_t = {}, {}, {}, {}, {}
+        z_t, t_t, rn_t, rg_t, rc_t, rs_t, d_t, tr_t, fg_t = {}, {}, {}, {}, {}, {}, {}, {}, {}
+
+        def lam_turn(i):
+            bank = psum.tile([P, 4, P], F32, name="bank", tag="turn", bufs=TURN)
+            words = lam_sb[:, i, :].bitcast(F32)
+            for g in range(KG):
+                for u in range(2):
+                    nc.tensor.transpose(bank[:, 2 * g + u, :], words[:, 256 * g + u : 256 * (g + 1) : 2], ident[:])
+            xt[i] = bank
+
+        def lam_tanh(i):
+            xf = work.tile([P, KG, P, 4], F32, name="xf", bufs=2, align_bytes=64)
+            for g in range(KG):
+                nc.scalar.activation(
+                    out=xf[:, g].rearrange("p m (u e) -> p m u e", u=2),
+                    in_=xt[i][:, 2 * g : 2 * g + 2, :].bitcast(BF16).rearrange("p u (m e) -> p m u e", e=2),
+                    func=TANH,
+                )
+            xf_t[i] = xf
+
+        def x_mul(i):
+            engine = nc.vector if i < X_ON_V else nc.gpsimd
+            xb = work.tile([P, KG, P, 4], BF16, name="xb", bufs=1, align_bytes=64)
+            for g in range(KG):
+                engine.tensor_tensor(
+                    out=xb[:, g],
+                    in0=xf_t[i][:, g],
+                    in1=amp_sb[:, g, :].unsqueeze(1).to_broadcast([P, P, 4]),
+                    op=ALU.mult,
+                )
+            xb_t[i] = xb
+
+        def x_quant(i):
+            xc = work.tile([P, KG * P], U32, name="xc", bufs=3, align_bytes=64)
+            xs = work.tile([P, KG * P], U8, name="xs", bufs=3, align_bytes=64)
+            nc.vector.quantize_mx(
+                out=xc[:].bitcast(E4M3X4), scales=xs[:], in_=xb_t[i][:].rearrange("p g m t -> p (g m t)")
+            )
+            xc_t[i], xs_t[i] = xc, xs
+
+        def stage1(s):
+            i, b = divmod(s, NG)
+            z = psum.tile([P, 512], F32, name="z", tag="z", bufs=Z)
+            for g in range(KG):
+                nc.tensor.matmul_mx(
+                    out=z[:],
+                    lhsT=xc_t[i][:, P * g : P * (g + 1)].bitcast(E4M3X4),
+                    lhsT_scale=xs_t[i][:, P * g : P * (g + 1)],
+                    rhs=hw[:, g, 1024 * b : 1024 * (b + 1)].bitcast(E2M1X4),
+                    rhs_scale=hs[:, g, 512 * b : 512 * (b + 1)],
+                    start=(g == 0),
+                    stop=(g == KG - 1),
+                )
+            z_t[s] = z
+
+        def sub(s):
+            i, b = divmod(s, NG)
+            if b == 0:
+                t_t[i] = work.tile([P, N], F32, name="t", bufs=5, align_bytes=64)
+            cols = slice(512 * b, 512 * (b + 1))
+            nc.vector.tensor_sub(
+                out=t_t[i][:, cols].rearrange("p (t q) -> p t q", t=4),
+                in0=y_t[i][:, cols].rearrange("p (q t) -> p t q", t=4),
+                in1=z_t[s][:].rearrange("p (q t) -> p t q", t=4),
+            )
+
+        def t_turn(s):
+            i, b = divmod(s, NG)
+            bank = psum.tile([P, 4, P], F32, name="bank", tag="turn", bufs=TURN)
+            for t in range(4):
+                nc.tensor.transpose(bank[:, t, :], t_t[i][:, 512 * b + P * t : 512 * b + P * (t + 1)], ident[:])
+            tr_t[i, b] = bank
+
+        def t_scale(s):
+            i, b = divmod(s, NG)
+            if b in S_BLOCKS.get(i, ()):
+                rn = work.tile([P, 4, P], BF16, name="rn", bufs=3, align_bytes=64)
+                for t in range(4):
+                    nc.scalar.activation(out=rn[:, t, :], in_=tr_t[i, b][:, t, :], func=COPY, scale=v_col[:, b, t : t + 1])
+                rn_t[s] = rn
+
+        def t_mul(s):
+            i, b = divmod(s, NG)
+            if b == 0:
+                rg_t[i] = work.tile([P, NG, P, 4], BF16, name="rg", bufs=2, align_bytes=64)
+            if s in rn_t:
+                nc.vector.tensor_copy(
+                    out=rg_t[i][:, b].rearrange("p (c i) t -> p c t i", i=4),
+                    in_=rn_t[s][:].rearrange("p t (c i) -> p c t i", i=4),
+                )
+            else:
+                nc.vector.tensor_tensor(
+                    out=rg_t[i][:, b],
+                    in0=tr_t[i, b][:].rearrange("p t m -> p m t"),
+                    in1=v_turned[:, b, :].unsqueeze(1).to_broadcast([P, P, 4]),
+                    op=ALU.mult,
+                )
+
+        def r_quant(i):
+            rc = work.tile([P, NG * P], U32, name="rc", bufs=6, align_bytes=64)
+            rs = work.tile([P, NG * P], U8, name="rs", bufs=6, align_bytes=64)
+            nc.vector.quantize_mx(
+                out=rc[:].bitcast(E5M2X4), scales=rs[:], in_=rg_t[i][:].rearrange("p g m t -> p (g m t)")
+            )
+            rc_t[i], rs_t[i] = rc, rs
+
+        def f_copy(piece):
+            kg, q = divmod(piece, 2)
+            kh, g = divmod(kg, NG)
+            if q == 0:
+                fg_t[kg] = work.tile([P, 512, 4], BF16, name="fg", bufs=5, align_bytes=64)
+            dst = fg_t[kg][:, 256 * q : 256 * (q + 1), :].rearrange("p (c i) t -> p c t i", i=4)
+            src = f_raw[:, kh, g, :, 256 * q : 256 * (q + 1)].rearrange("p t (c i) -> p c t i", i=4)
+            if piece in F_ON_V:
+                nc.vector.tensor_copy(out=dst, in_=src)
+            else:
+                nc.scalar.copy(out=dst, in_=src)
+
+        def f_quant(kg):
+            kh, g = divmod(kg, NG)
+            nc.vector.quantize_mx(
+                out=f_codes[:, kh, g, :].bitcast(E4M3X4),
+                scales=f_scales[:, kh, g, :],
+                in_=fg_t[kg][:].rearrange("p c j -> p (c j)"),
+            )
+
+        def stage2(i, kh):
+            d = psum.tile([P, 512], F32, name="d", tag="d", bufs=2)
+            for g in range(NG):
+                nc.tensor.matmul_mx(
+                    out=d[:],
+                    lhsT=rc_t[i][:, P * g : P * (g + 1)].bitcast(E5M2X4),
+                    lhsT_scale=rs_t[i][:, P * g : P * (g + 1)],
+                    rhs=f_codes[:, kh, g, :].bitcast(E4M3X4),
+                    rhs_scale=f_scales[:, kh, g, :],
+                    start=(g == 0),
+                    stop=(g == NG - 1),
+                )
+            d_t[i, kh] = d
+
+        def add(i, kh):
+            o = work.tile([P, 512], F32, name="o", bufs=4, align_bytes=64)
+            cols = slice(512 * kh, 512 * (kh + 1))
+            nc.vector.tensor_add(out=o[:], in0=d_t[i, kh][:], in1=lam_sb[:, i, cols])
+            nc.sync.dma_start(out=out[P * i : P * (i + 1), cols], in_=o[:])
+
+        pending = []
+        todo = [(i, kh) for i in range(TILES) for kh in range(2)]
+        f_ready = [0]
+
+        def second():
+            for x in todo:
+                if x[0] in rc_t and f_ready[0] >= NG * (x[1] + 1):
+                    if len(pending) == 2:
+                        add(*pending.pop(0))
+                    stage2(*x)
+                    pending.append(x)
+                    todo.remove(x)
+                    break
+
+        S = NG * TILES
+        for j in range(2):
+            lam_turn(j)
+            lam_tanh(j)
+        x_mul(0)
+        x_quant(0)
+        for s in range(-Z, S + 9):
+            if 0 <= s < S:
+                sub(s)
+            if 0 <= s + Z < S:
+                stage1(s + Z)
+            for j in range(1, TILES):
+                if s == NG * j + -10 or (s == -Z and j > 1 and NG * j + -10 < -Z):
+                    if j > 1:
+                        lam_turn(j)
+                        lam_tanh(j)
+                if s == max(NG * j + -8, -Z):
+                    x_mul(j)
+                if s == max(NG * j + -6, -Z + 1):
+                    x_quant(j)
+            if 0 <= s - 2 < S:
+                t_mul(s - 2)
+            if s % 2 == 1 and 0 < s < S:
+                t_turn(s - 1)
+                t_turn(s)
+                t_scale(s - 1)
+                t_scale(s)
+            for j in range(TILES):
+                if s == NG * j + 6:
+                    r_quant(j)
+            if s >= 0:
+                for kg in range(8):
+                    if s == 2 * kg + 3:
+                        f_quant(kg)
+                        f_ready[0] += 1
+                if pending:
+                    add(*pending.pop(0))
+                second()
+                if s >= S + 2:
+                    second()
+            if 0 <= s - 0 < 16:
+                f_copy(s - 0)
+        while pending:
+            add(*pending.pop(0))

@@ -12,7 +12,6 @@ E4M3X4 = mybir.dt.float8_e4m3fn_x4
 E5M2X4 = mybir.dt.float8_e5m2_x4
 E2M1X4 = mybir.dt.float4_e2m1fn_x4
 ALU = mybir.AluOpType
-COPY = mybir.ActivationFunctionType.Copy
 TANH = mybir.ActivationFunctionType.Tanh
 
 M, K, N = 1024, 1024, 2048
@@ -21,11 +20,8 @@ FLOPS = 2 * M * K * N * 2
 TILES = M // P
 KG = K // 512
 NG = N // 512
-X_ON_V = 8
-F_ON_V = ()
-TURN, Z = 3, 3
-S_BLOCKS = {3: (1, 3), 4: (0, 1, 2, 3), 5: (0, 1, 2, 3), 6: (0, 1, 2, 3), 7: (0, 1, 2, 3)}
-F_STEPS = (1, 1, 1, 1)
+F_PER_PERIOD = 3
+FIRST_SECOND = 2
 
 
 def tile_ftn_residual_turn_s9_kernel(tc, lam, amp, h_words, h_scales, y, v, f, out):
@@ -34,279 +30,301 @@ def tile_ftn_residual_turn_s9_kernel(tc, lam, amp, h_words, h_scales, y, v, f, o
         keep = ctx.enter_context(tc.tile_pool(name="keep", bufs=1))
         work = ctx.enter_context(tc.tile_pool(name="work", bufs=2))
         psum = ctx.enter_context(tc.psum_pool(name="psum", bufs=2))
+        ctx.enter_context(tc.manual_schedule())
 
-        warm = keep.tile([P, 1], F32)
+        warm = keep.tile([P, 1], F32, name="warm")
         nc.vector.memset(warm[:], 0.0)
-        warm_out = keep.tile([P, 1], F32)
-        nc.scalar.activation(out=warm_out[:], in_=warm[:], func=TANH)
-        hs = keep.tile([P, KG, N], U8, align_bytes=64)
+        warm_out = keep.tile([P, 1], F32, name="warm_out")
+        hs = keep.tile([P, KG, N], U8, name="hs", align_bytes=64)
         nc.vector.memset(hs[:].rearrange("p g n -> p (g n)").bitcast(I32), 0)
-        ident = keep.tile([P, P], F32, align_bytes=64)
+        ident = keep.tile([P, P], F32, name="ident", align_bytes=64)
         make_identity(nc, ident[:])
 
-        v_turned = keep.tile([P, NG, 4], BF16, align_bytes=64)
-        amp_sb = keep.tile([P, KG, 4], BF16, align_bytes=64)
-        hw = keep.tile([P, KG, 2 * N], U8, align_bytes=64)
-        lam_sb = keep.tile([P, TILES, K], BF16, align_bytes=64)
-        f_raw = keep.tile([P, 2, NG, 4, 512], BF16, align_bytes=64)
-
-        y_t = {}
+        amp_col = keep.tile([P, KG, 4], BF16, name="amp_col", align_bytes=64)
+        v_col = keep.tile([P, NG * 4], BF16, name="v_col", align_bytes=64)
+        lam_t, y_t, f_raw, hw = {}, {}, {}, {}
 
         def load_lam(i):
-            nc.sync.dma_start(out=lam_sb[:, i, :], in_=lam[P * i : P * (i + 1), :])
+            lam_t[i] = work.tile([P, K], BF16, name="lam_in", bufs=TILES, align_bytes=64)
+            nc.sync.dma_start(out=lam_t[i][:], in_=lam[P * i : P * (i + 1), :])
 
         def load_y(i):
-            y_t[i] = work.tile([P, N], BF16, name="y_in", bufs=8, align_bytes=64)
+            y_t[i] = work.tile([P, N], BF16, name="y_in", bufs=TILES, align_bytes=64)
             nc.sync.dma_start(out=y_t[i][:], in_=y[P * i : P * (i + 1), :])
 
-        def load_f(kh, g):
-            cols = slice(512 * kh, 512 * (kh + 1))
+        def load_f(c):
+            kh, g = divmod(c, NG)
+            f_raw[c] = work.tile([P, 4, 512], BF16, name="f_raw", bufs=2 * NG, align_bytes=64)
             nc.sync.dma_start(
-                out=f_raw[:, kh, g], in_=f[512 * g : 512 * (g + 1), cols].rearrange("(p j) k -> p j k", j=4)
+                out=f_raw[c][:],
+                in_=f[512 * g : 512 * (g + 1), 512 * kh : 512 * (kh + 1)].rearrange("(p j) k -> p j k", j=4),
             )
 
         def load_h(half):
-            cols = slice(N * half, N * (half + 1))
+            hw[half] = work.tile([P, KG, N], U8, name="hw", bufs=2, align_bytes=64)
             nc.sync.dma_start(
-                out=hw[:, :, cols].bitcast(I32), in_=h_words[:, :, cols].rearrange("g p c -> p g c").bitcast(I32)
+                out=hw[half][:].bitcast(I32),
+                in_=h_words[:, :, N * half : N * (half + 1)].rearrange("g p c -> p g c").bitcast(I32),
             )
 
-        nc.scalar.dma_start(out=amp_sb[:], in_=amp.rearrange("(g p t) -> p g t", g=KG, t=4))
         load_lam(0)
-        load_lam(1)
+        nc.scalar.dma_start(out=amp_col[:], in_=amp.rearrange("(g p t) -> p g t", g=KG, t=4))
+        nc.scalar.activation(out=warm_out[:], in_=warm[:], func=TANH)
+        nc.gpsimd.dma_start(
+            out=v_col[:].rearrange("p (g t) -> p g t", t=4), in_=v.rearrange("(g p t) -> p g t", g=NG, t=4)
+        )
         for q in range(4):
             nc.sync.dma_start(
                 out=hs[32 * q : 32 * q + 4].bitcast(I32),
                 in_=h_scales[:, 4 * q : 4 * q + 4, :].rearrange("g r n -> r g n").bitcast(I32),
             )
+        load_lam(1)
         load_h(0)
         load_y(0)
-        load_h(1)
-        nc.sync.dma_start(out=v_turned[:], in_=v.rearrange("(g p t) -> p g t", g=NG, t=4))
         load_lam(2)
-        load_y(1)
-        load_f(0, 0)
-        load_f(0, 1)
-        load_lam(3)
-        load_f(0, 2)
-        load_f(0, 3)
-        load_y(2)
-        load_lam(4)
-        for g in range(NG):
-            load_f(1, g)
-        load_y(3)
-        for i in range(5, TILES):
-            load_lam(i)
-            load_y(i - 1)
-        load_y(TILES - 1)
+        load_f(0)
+        load_h(1)
+        load_f(1)
+        for i in range(1, TILES):
+            if i + 2 < TILES:
+                load_lam(i + 2)
+            load_y(i)
+            for c in (2 * i, 2 * i + 1):
+                if c < 2 * NG:
+                    load_f(c)
 
-        v_col = keep.tile([P, NG, 4], F32)
-        nc.vector.tensor_copy(out=v_col[:], in_=v_turned[:])
-        f_codes = keep.tile([P, 2, NG, 512], U32, align_bytes=64)
-        f_scales = keep.tile([P, 2, NG, 512], U8, align_bytes=64)
+        xf_t, xt_t, xb_t, xc_t, xs_t = {}, {}, {}, {}, {}
+        z_t, t_t, r_t, rt_t, rg_t, rc_t, rs_t, d_t = {}, {}, {}, {}, {}, {}, {}, {}
+        fg_t, fc_t, fs_t = {}, {}, {}
 
-        xt, xf_t, xb_t, xc_t, xs_t = {}, {}, {}, {}, {}
-        z_t, t_t, rn_t, rg_t, rc_t, rs_t, d_t, tr_t, fg_t = {}, {}, {}, {}, {}, {}, {}, {}, {}
+        def x_tanh(i):
+            xf_t[i] = work.tile([P, KG, 4, P], F32, name="xf", bufs=2, align_bytes=64)
+            nc.scalar.activation(
+                out=xf_t[i][:].rearrange("p g t q -> p g q t"),
+                in_=lam_t[i][:].rearrange("p (g q t) -> p g q t", g=KG, t=4),
+                func=TANH,
+            )
 
-        def lam_turn(i):
-            bank = psum.tile([P, 4, P], F32, name="bank", tag="turn", bufs=TURN)
-            words = lam_sb[:, i, :].bitcast(F32)
+        def x_turn(i):
             for g in range(KG):
-                for u in range(2):
-                    nc.tensor.transpose(bank[:, 2 * g + u, :], words[:, 256 * g + u : 256 * (g + 1) : 2], ident[:])
-            xt[i] = bank
+                xt_t[i, g] = psum.tile([P, 4, P], F32, name="bank", tag="bank", bufs=8)
+                for t in range(4):
+                    nc.tensor.transpose(xt_t[i, g][:, t, :], xf_t[i][:, g, t, :], ident[:])
 
-        def lam_tanh(i):
-            xf = work.tile([P, KG, P, 4], F32, name="xf", bufs=2, align_bytes=64)
-            for g in range(KG):
-                nc.scalar.activation(
-                    out=xf[:, g].rearrange("p m (u e) -> p m u e", u=2),
-                    in_=xt[i][:, 2 * g : 2 * g + 2, :].bitcast(BF16).rearrange("p u (m e) -> p m u e", e=2),
-                    func=TANH,
-                )
-            xf_t[i] = xf
-
-        def x_mul(i):
-            engine = nc.vector if i < X_ON_V else nc.gpsimd
-            xb = work.tile([P, KG, P, 4], BF16, name="xb", bufs=1, align_bytes=64)
-            for g in range(KG):
-                engine.tensor_tensor(
-                    out=xb[:, g],
-                    in0=xf_t[i][:, g],
-                    in1=amp_sb[:, g, :].unsqueeze(1).to_broadcast([P, P, 4]),
-                    op=ALU.mult,
-                )
-            xb_t[i] = xb
+        def x_amp(i, g):
+            if g == 0:
+                xb_t[i] = work.tile([P, KG, P, 4], BF16, name="xb", bufs=2, align_bytes=64)
+            nc.vector.tensor_tensor(
+                out=xb_t[i][:, g],
+                in0=xt_t[i, g][:].rearrange("p t m -> p m t"),
+                in1=amp_col[:, g, :].unsqueeze(1).to_broadcast([P, P, 4]),
+                op=ALU.mult,
+            )
 
         def x_quant(i):
-            xc = work.tile([P, KG * P], U32, name="xc", bufs=3, align_bytes=64)
-            xs = work.tile([P, KG * P], U8, name="xs", bufs=3, align_bytes=64)
+            xc_t[i] = work.tile([P, KG * P], U32, name="xc", bufs=3, align_bytes=64)
+            xs_t[i] = work.tile([P, KG * P], U8, name="xs", bufs=3, align_bytes=64)
             nc.vector.quantize_mx(
-                out=xc[:].bitcast(E4M3X4), scales=xs[:], in_=xb_t[i][:].rearrange("p g m t -> p (g m t)")
+                out=xc_t[i][:].bitcast(E4M3X4), scales=xs_t[i][:], in_=xb_t[i][:].rearrange("p g m t -> p (g m t)")
             )
-            xc_t[i], xs_t[i] = xc, xs
 
-        def stage1(s):
-            i, b = divmod(s, NG)
-            z = psum.tile([P, 512], F32, name="z", tag="z", bufs=Z)
+        def first(i, b):
+            z_t[i, b] = psum.tile([P, 512], F32, name="z", tag="bank", bufs=8)
+            half, c = divmod(b, 2)
             for g in range(KG):
                 nc.tensor.matmul_mx(
-                    out=z[:],
+                    out=z_t[i, b][:],
                     lhsT=xc_t[i][:, P * g : P * (g + 1)].bitcast(E4M3X4),
                     lhsT_scale=xs_t[i][:, P * g : P * (g + 1)],
-                    rhs=hw[:, g, 1024 * b : 1024 * (b + 1)].bitcast(E2M1X4),
+                    rhs=hw[half][:, g, 1024 * c : 1024 * (c + 1)].bitcast(E2M1X4),
                     rhs_scale=hs[:, g, 512 * b : 512 * (b + 1)],
                     start=(g == 0),
                     stop=(g == KG - 1),
                 )
-            z_t[s] = z
 
-        def sub(s):
-            i, b = divmod(s, NG)
-            if b == 0:
-                t_t[i] = work.tile([P, N], F32, name="t", bufs=5, align_bytes=64)
-            cols = slice(512 * b, 512 * (b + 1))
+        def sub(i, b):
+            half, c = divmod(b, 2)
+            if c == 0:
+                t_t[i, half] = work.tile([P, 1024], F32, name="t", bufs=4, align_bytes=64)
             nc.vector.tensor_sub(
-                out=t_t[i][:, cols].rearrange("p (t q) -> p t q", t=4),
-                in0=y_t[i][:, cols].rearrange("p (q t) -> p t q", t=4),
-                in1=z_t[s][:].rearrange("p (q t) -> p t q", t=4),
+                out=t_t[i, half][:, 512 * c : 512 * (c + 1)].rearrange("p (u q e) -> p q u e", u=2, e=2),
+                in0=y_t[i][:, 512 * b : 512 * (b + 1)].rearrange("p (q u e) -> p q u e", u=2, e=2),
+                in1=z_t[i, b][:].rearrange("p (q u e) -> p q u e", u=2, e=2),
             )
 
-        def t_turn(s):
-            i, b = divmod(s, NG)
-            bank = psum.tile([P, 4, P], F32, name="bank", tag="turn", bufs=TURN)
-            for t in range(4):
-                nc.tensor.transpose(bank[:, t, :], t_t[i][:, 512 * b + P * t : 512 * b + P * (t + 1)], ident[:])
-            tr_t[i, b] = bank
+        def weigh(engine, i, b0, b1):
+            half, c = divmod(b0, 2)
+            if c == 0:
+                r_t[i, half] = work.tile([P, 1024], BF16, name="r", bufs=4, align_bytes=64)
+            cols = slice(512 * c, 512 * (c + b1 - b0))
+            engine.tensor_tensor(
+                out=r_t[i, half][:, cols],
+                in0=t_t[i, half][:, cols],
+                in1=v_rows[:, 256 * b0 : 256 * b1].bitcast(BF16),
+                op=ALU.mult,
+            )
 
-        def t_scale(s):
-            i, b = divmod(s, NG)
-            if b in S_BLOCKS.get(i, ()):
-                rn = work.tile([P, 4, P], BF16, name="rn", bufs=3, align_bytes=64)
-                for t in range(4):
-                    nc.scalar.activation(out=rn[:, t, :], in_=tr_t[i, b][:, t, :], func=COPY, scale=v_col[:, b, t : t + 1])
-                rn_t[s] = rn
+        def r_turn(i, half):
+            rt_t[i, half] = psum.tile([P, 4, P], F32, name="bank", tag="bank", bufs=8)
+            words = r_t[i, half][:].bitcast(F32)
+            for j in range(4):
+                nc.tensor.transpose(rt_t[i, half][:, j, :], words[:, P * j : P * (j + 1)], ident[:])
 
-        def t_mul(s):
-            i, b = divmod(s, NG)
-            if b == 0:
-                rg_t[i] = work.tile([P, NG, P, 4], BF16, name="rg", bufs=2, align_bytes=64)
-            if s in rn_t:
-                nc.vector.tensor_copy(
-                    out=rg_t[i][:, b].rearrange("p (c i) t -> p c t i", i=4),
-                    in_=rn_t[s][:].rearrange("p t (c i) -> p c t i", i=4),
-                )
-            else:
-                nc.vector.tensor_tensor(
-                    out=rg_t[i][:, b],
-                    in0=tr_t[i, b][:].rearrange("p t m -> p m t"),
-                    in1=v_turned[:, b, :].unsqueeze(1).to_broadcast([P, P, 4]),
-                    op=ALU.mult,
-                )
+        def r_copy(i, half):
+            if half == 0:
+                rg_t[i] = work.tile([P, 1024], F32, name="rg", bufs=2, align_bytes=64)
+            nc.scalar.copy(
+                out=rg_t[i][:, 512 * half : 512 * (half + 1)].rearrange("p (g m u) -> p g m u", g=2, u=2),
+                in_=rt_t[i, half][:].rearrange("p (g u) m -> p g m u", u=2),
+            )
 
         def r_quant(i):
-            rc = work.tile([P, NG * P], U32, name="rc", bufs=6, align_bytes=64)
-            rs = work.tile([P, NG * P], U8, name="rs", bufs=6, align_bytes=64)
-            nc.vector.quantize_mx(
-                out=rc[:].bitcast(E5M2X4), scales=rs[:], in_=rg_t[i][:].rearrange("p g m t -> p (g m t)")
-            )
-            rc_t[i], rs_t[i] = rc, rs
+            rc_t[i] = work.tile([P, NG * P], U32, name="rc", bufs=TILES, align_bytes=64)
+            rs_t[i] = work.tile([P, NG * P], U8, name="rs", bufs=TILES, align_bytes=64)
+            nc.vector.quantize_mx(out=rc_t[i][:].bitcast(E5M2X4), scales=rs_t[i][:], in_=rg_t[i][:].bitcast(BF16))
 
         def f_copy(piece):
-            kg, q = divmod(piece, 2)
-            kh, g = divmod(kg, NG)
-            if q == 0:
-                fg_t[kg] = work.tile([P, 512, 4], BF16, name="fg", bufs=5, align_bytes=64)
-            dst = fg_t[kg][:, 256 * q : 256 * (q + 1), :].rearrange("p (c i) t -> p c t i", i=4)
-            src = f_raw[:, kh, g, :, 256 * q : 256 * (q + 1)].rearrange("p t (c i) -> p c t i", i=4)
-            if piece in F_ON_V:
-                nc.vector.tensor_copy(out=dst, in_=src)
-            else:
-                nc.scalar.copy(out=dst, in_=src)
-
-        def f_quant(kg):
-            kh, g = divmod(kg, NG)
-            nc.vector.quantize_mx(
-                out=f_codes[:, kh, g, :].bitcast(E4M3X4),
-                scales=f_scales[:, kh, g, :],
-                in_=fg_t[kg][:].rearrange("p c j -> p (c j)"),
+            pair, rest = divmod(piece, 4)
+            c, q = divmod(rest, 2)
+            if rest == 0:
+                fg_t[pair] = work.tile([P, 2, 512, 4], BF16, name="fg", bufs=2, align_bytes=64)
+            nc.scalar.copy(
+                out=fg_t[pair][:, c, 256 * q : 256 * (q + 1), :].rearrange("p (c i) t -> p c t i", i=4),
+                in_=f_raw[2 * pair + c][:, :, 256 * q : 256 * (q + 1)].rearrange("p t (c i) -> p c t i", i=4),
             )
 
-        def stage2(i, kh):
-            d = psum.tile([P, 512], F32, name="d", tag="d", bufs=2)
+        def f_quant(pair):
+            fc_t[pair] = work.tile([P, 1024], U32, name="fc", bufs=NG, align_bytes=64)
+            fs_t[pair] = work.tile([P, 1024], U8, name="fs", bufs=NG, align_bytes=64)
+            nc.vector.quantize_mx(
+                out=fc_t[pair][:].bitcast(E4M3X4),
+                scales=fs_t[pair][:],
+                in_=fg_t[pair][:].rearrange("p g c j -> p (g c j)"),
+            )
+
+        def second(i, kh):
+            d_t[i, kh] = psum.tile([P, 512], F32, name="d", tag="bank", bufs=8)
             for g in range(NG):
                 nc.tensor.matmul_mx(
-                    out=d[:],
+                    out=d_t[i, kh][:],
                     lhsT=rc_t[i][:, P * g : P * (g + 1)].bitcast(E5M2X4),
                     lhsT_scale=rs_t[i][:, P * g : P * (g + 1)],
-                    rhs=f_codes[:, kh, g, :].bitcast(E4M3X4),
-                    rhs_scale=f_scales[:, kh, g, :],
+                    rhs=fc_t[2 * kh + g // 2][:, 512 * (g % 2) : 512 * (g % 2 + 1)].bitcast(E4M3X4),
+                    rhs_scale=fs_t[2 * kh + g // 2][:, 512 * (g % 2) : 512 * (g % 2 + 1)],
                     start=(g == 0),
                     stop=(g == NG - 1),
                 )
-            d_t[i, kh] = d
 
         def add(i, kh):
             o = work.tile([P, 512], F32, name="o", bufs=4, align_bytes=64)
             cols = slice(512 * kh, 512 * (kh + 1))
-            nc.vector.tensor_add(out=o[:], in0=d_t[i, kh][:], in1=lam_sb[:, i, cols])
+            nc.vector.tensor_add(out=o[:], in0=d_t[i, kh][:], in1=lam_t[i][:, cols])
             nc.sync.dma_start(out=out[P * i : P * (i + 1), cols], in_=o[:])
 
-        pending = []
+        v_rows = keep.tile([P, NG * 256], F32, name="v_rows", align_bytes=64)
+
+        def spread_v():
+            words = v_col[:].bitcast(F32)
+            for half in range(2):
+                bank = psum.tile([P, 4, P], F32, name="bank", tag="bank", bufs=8)
+                for j in range(4):
+                    w = 4 * half + j
+                    nc.tensor.transpose(bank[:, j, :], words[:, w : w + 1].to_broadcast([P, P]), ident[:])
+                nc.scalar.copy(out=v_rows[:, 512 * half : 512 * (half + 1)], in_=bank[:].rearrange("p j m -> p (j m)"))
+
         todo = [(i, kh) for i in range(TILES) for kh in range(2)]
-        f_ready = [0]
+        waiting = []
+        known_r, known_f = set(), set()
+        f_copied = []
+        f_quantised = []
 
-        def second():
-            for x in todo:
-                if x[0] in rc_t and f_ready[0] >= NG * (x[1] + 1):
-                    if len(pending) == 2:
-                        add(*pending.pop(0))
-                    stage2(*x)
-                    pending.append(x)
-                    todo.remove(x)
-                    break
+        def tile_ok(i):
+            return 0 <= i < TILES
 
-        S = NG * TILES
-        for j in range(2):
-            lam_turn(j)
-            lam_tanh(j)
-        x_mul(0)
+        def next_second(j):
+            ready = [x for x in todo if x[0] in known_r and 2 * x[1] + 1 in known_f]
+            if ready and j >= FIRST_SECOND:
+                todo.remove(ready[0])
+                second(*ready[0])
+                waiting.append(ready[0])
+
+        def next_add():
+            if waiting:
+                add(*waiting.pop(0))
+
+        def next_f_copy():
+            if len(f_copied) < 4 * NG:
+                f_copy(len(f_copied))
+                f_copied.append(0)
+
+        def next_f_quant():
+            if len(f_quantised) < len(f_copied) // 4:
+                f_quant(len(f_quantised))
+                f_quantised.append(0)
+
+        x_tanh(0)
+        x_turn(0)
+        x_tanh(1)
+        x_amp(0, 0)
+        x_amp(0, 1)
+        spread_v()
         x_quant(0)
-        for s in range(-Z, S + 9):
-            if 0 <= s < S:
-                sub(s)
-            if 0 <= s + Z < S:
-                stage1(s + Z)
-            for j in range(1, TILES):
-                if s == NG * j + -10 or (s == -Z and j > 1 and NG * j + -10 < -Z):
-                    if j > 1:
-                        lam_turn(j)
-                        lam_tanh(j)
-                if s == max(NG * j + -8, -Z):
-                    x_mul(j)
-                if s == max(NG * j + -6, -Z + 1):
-                    x_quant(j)
-            if 0 <= s - 2 < S:
-                t_mul(s - 2)
-            if s % 2 == 1 and 0 < s < S:
-                t_turn(s - 1)
-                t_turn(s)
-                t_scale(s - 1)
-                t_scale(s)
-            for j in range(TILES):
-                if s == NG * j + 6:
-                    r_quant(j)
-            if s >= 0:
-                for kg in range(8):
-                    if s == 2 * kg + 3:
-                        f_quant(kg)
-                        f_ready[0] += 1
-                if pending:
-                    add(*pending.pop(0))
-                second()
-                if s >= S + 2:
-                    second()
-            if 0 <= s - 0 < 16:
-                f_copy(s - 0)
-        while pending:
-            add(*pending.pop(0))
+        x_turn(1)
+        x_tanh(2)
+        x_amp(1, 0)
+        x_amp(1, 1)
+        x_quant(1)
+        for j in range(TILES + 2):
+            known_f = set(fc_t)
+            if tile_ok(j):
+                first(j, 0)
+                first(j, 1)
+                sub(j, 0)
+                sub(j, 1)
+            next_f_quant()
+            if tile_ok(j):
+                weigh(nc.gpsimd, j, 0, 2)
+            next_second(j)
+            next_f_copy()
+            next_f_copy()
+            if tile_ok(j + 2):
+                x_turn(j + 2)
+            if tile_ok(j - 1):
+                r_turn(j - 1, 0)
+                r_turn(j - 1, 1)
+                r_copy(j - 1, 0)
+                r_copy(j - 1, 1)
+            if tile_ok(j + 3):
+                x_tanh(j + 3)
+            known_r = set(rc_t)
+            if tile_ok(j):
+                first(j, 2)
+            next_add()
+            if tile_ok(j + 2):
+                x_amp(j + 2, 0)
+                x_amp(j + 2, 1)
+            if tile_ok(j):
+                sub(j, 2)
+            if tile_ok(j + 2):
+                x_quant(j + 2)
+            if tile_ok(j):
+                weigh(nc.gpsimd, j, 2, 3)
+            next_second(j)
+            if tile_ok(j):
+                first(j, 3)
+            next_add()
+            if tile_ok(j):
+                sub(j, 3)
+            if tile_ok(j - 1):
+                r_quant(j - 1)
+            if tile_ok(j):
+                weigh(nc.gpsimd, j, 3, 4)
+            for c in range(F_PER_PERIOD - 2 + (j < 1)):
+                next_f_copy()
+        known_r = set(rc_t)
+        while todo:
+            next_second(TILES)
+            if len(waiting) == 2:
+                next_add()
+        while waiting:
+            next_add()

@@ -20,8 +20,12 @@ FLOPS = 2 * M * K * N * 2
 TILES = M // P
 KG = K // 512
 NG = N // 512
-F_PER_PERIOD = 3
-FIRST_SECOND = 2
+F_COUNT = (2, 3, 3, 4, 2)
+A_TILES = (0, 1, 2, 3)
+S_AMP_FROM = 8
+THIRD_FROM = 5
+ORDER = 1
+V_COPY = ()
 
 
 def tile_ftn_residual_turn_s9_kernel(tc, lam, amp, h_words, h_scales, y, v, f, out):
@@ -44,13 +48,17 @@ def tile_ftn_residual_turn_s9_kernel(tc, lam, amp, h_words, h_scales, y, v, f, o
         v_col = keep.tile([P, NG * 4], BF16, name="v_col", align_bytes=64)
         lam_t, y_t, f_raw, hw = {}, {}, {}, {}
 
-        def load_lam(i):
+        def load_lam(i, parts=1):
             lam_t[i] = work.tile([P, K], BF16, name="lam_in", bufs=TILES, align_bytes=64)
-            nc.sync.dma_start(out=lam_t[i][:], in_=lam[P * i : P * (i + 1), :])
+            for c in range(parts):
+                cols = slice(K // parts * c, K // parts * (c + 1))
+                nc.sync.dma_start(out=lam_t[i][:, cols], in_=lam[P * i : P * (i + 1), cols])
 
-        def load_y(i):
-            y_t[i] = work.tile([P, N], BF16, name="y_in", bufs=TILES, align_bytes=64)
-            nc.sync.dma_start(out=y_t[i][:], in_=y[P * i : P * (i + 1), :])
+        def load_y(i, c0=0, c1=2):
+            if c0 == 0:
+                y_t[i] = work.tile([P, N], BF16, name="y_in", bufs=TILES, align_bytes=64)
+            cols = slice(1024 * c0, 1024 * c1)
+            nc.sync.dma_start(out=y_t[i][:, cols], in_=y[P * i : P * (i + 1), cols])
 
         def load_f(c):
             kh, g = divmod(c, NG)
@@ -67,46 +75,51 @@ def tile_ftn_residual_turn_s9_kernel(tc, lam, amp, h_words, h_scales, y, v, f, o
                 in_=h_words[:, :, N * half : N * (half + 1)].rearrange("g p c -> p g c").bitcast(I32),
             )
 
-        load_lam(0)
+        load_lam(0, 2)
         nc.scalar.dma_start(out=amp_col[:], in_=amp.rearrange("(g p t) -> p g t", g=KG, t=4))
-        nc.scalar.activation(out=warm_out[:], in_=warm[:], func=TANH)
-        nc.gpsimd.dma_start(
+        nc.scalar.dma_start(
             out=v_col[:].rearrange("p (g t) -> p g t", t=4), in_=v.rearrange("(g p t) -> p g t", g=NG, t=4)
         )
+        nc.scalar.activation(out=warm_out[:], in_=warm[:], func=TANH)
         for q in range(4):
             nc.sync.dma_start(
                 out=hs[32 * q : 32 * q + 4].bitcast(I32),
                 in_=h_scales[:, 4 * q : 4 * q + 4, :].rearrange("g r n -> r g n").bitcast(I32),
             )
-        load_lam(1)
         load_h(0)
-        load_y(0)
-        load_lam(2)
-        load_f(0)
+        load_y(0, 0, 1)
+        load_lam(1)
+        if ORDER == 1:
+            load_f(0)
         load_h(1)
+        load_y(0, 1, 2)
+        if ORDER == 0:
+            load_f(0)
+        load_lam(2)
         load_f(1)
         for i in range(1, TILES):
-            if i + 2 < TILES:
-                load_lam(i + 2)
             load_y(i)
             for c in (2 * i, 2 * i + 1):
                 if c < 2 * NG:
                     load_f(c)
+            if i + 2 < TILES:
+                load_lam(i + 2)
 
         xf_t, xt_t, xb_t, xc_t, xs_t = {}, {}, {}, {}, {}
         z_t, t_t, r_t, rt_t, rg_t, rc_t, rs_t, d_t = {}, {}, {}, {}, {}, {}, {}, {}
-        fg_t, fc_t, fs_t = {}, {}, {}
+        vt_t = {}
 
-        def x_tanh(i):
-            xf_t[i] = work.tile([P, KG, 4, P], F32, name="xf", bufs=2, align_bytes=64)
+        def x_tanh(i, g0=0, g1=KG):
+            if g0 == 0:
+                xf_t[i] = work.tile([P, KG, 4, P], F32, name="xf", bufs=2, align_bytes=64)
             nc.scalar.activation(
-                out=xf_t[i][:].rearrange("p g t q -> p g q t"),
-                in_=lam_t[i][:].rearrange("p (g q t) -> p g q t", g=KG, t=4),
+                out=xf_t[i][:, g0:g1].rearrange("p g t q -> p g q t"),
+                in_=lam_t[i][:, 512 * g0 : 512 * g1].rearrange("p (g q t) -> p g q t", q=P, t=4),
                 func=TANH,
             )
 
-        def x_turn(i):
-            for g in range(KG):
+        def x_turn(i, g0=0, g1=KG):
+            for g in range(g0, g1):
                 xt_t[i, g] = psum.tile([P, 4, P], F32, name="bank", tag="bank", bufs=8)
                 for t in range(4):
                     nc.tensor.transpose(xt_t[i, g][:, t, :], xf_t[i][:, g, t, :], ident[:])
@@ -121,11 +134,14 @@ def tile_ftn_residual_turn_s9_kernel(tc, lam, amp, h_words, h_scales, y, v, f, o
                 op=ALU.mult,
             )
 
-        def x_quant(i):
-            xc_t[i] = work.tile([P, KG * P], U32, name="xc", bufs=3, align_bytes=64)
-            xs_t[i] = work.tile([P, KG * P], U8, name="xs", bufs=3, align_bytes=64)
+        def x_quant(i, g0=0, g1=KG):
+            if g0 == 0:
+                xc_t[i] = work.tile([P, KG * P], U32, name="xc", bufs=3, align_bytes=64)
+                xs_t[i] = work.tile([P, KG * P], U8, name="xs", bufs=3, align_bytes=64)
             nc.vector.quantize_mx(
-                out=xc_t[i][:].bitcast(E4M3X4), scales=xs_t[i][:], in_=xb_t[i][:].rearrange("p g m t -> p (g m t)")
+                out=xc_t[i][:, P * g0 : P * g1].bitcast(E4M3X4),
+                scales=xs_t[i][:, P * g0 : P * g1],
+                in_=xb_t[i][:, g0:g1].rearrange("p g m t -> p (g m t)"),
             )
 
         def first(i, b):
@@ -154,7 +170,7 @@ def tile_ftn_residual_turn_s9_kernel(tc, lam, amp, h_words, h_scales, y, v, f, o
 
         def weigh(engine, i, b0, b1):
             half, c = divmod(b0, 2)
-            if c == 0:
+            if (i, half) not in r_t:
                 r_t[i, half] = work.tile([P, 1024], BF16, name="r", bufs=4, align_bytes=64)
             cols = slice(512 * c, 512 * (c + b1 - b0))
             engine.tensor_tensor(
@@ -164,42 +180,67 @@ def tile_ftn_residual_turn_s9_kernel(tc, lam, amp, h_words, h_scales, y, v, f, o
                 op=ALU.mult,
             )
 
-        def r_turn(i, half):
-            rt_t[i, half] = psum.tile([P, 4, P], F32, name="bank", tag="bank", bufs=8)
-            words = r_t[i, half][:].bitcast(F32)
-            for j in range(4):
-                nc.tensor.transpose(rt_t[i, half][:, j, :], words[:, P * j : P * (j + 1)], ident[:])
+        def r_turn(i, b0, b1):
+            rt_t[i, b0] = psum.tile([P, 4, P], F32, name="bank", tag="bank", bufs=8)
+            words = r_t[i, b0 // 2][:].bitcast(F32)
+            for j in range(2 * (b0 % 2), 2 * (b0 % 2 + b1 - b0)):
+                nc.tensor.transpose(rt_t[i, b0][:, j, :], words[:, P * j : P * (j + 1)], ident[:])
 
-        def r_copy(i, half):
-            if half == 0:
+        def r_tile(i):
+            if i not in rg_t:
                 rg_t[i] = work.tile([P, 1024], F32, name="rg", bufs=2, align_bytes=64)
-            nc.scalar.copy(
-                out=rg_t[i][:, 512 * half : 512 * (half + 1)].rearrange("p (g m u) -> p g m u", g=2, u=2),
-                in_=rt_t[i, half][:].rearrange("p (g u) m -> p g m u", u=2),
+            return rg_t[i]
+
+        def r_copy(i, b0, b1, on_vector=False):
+            copy = nc.vector.tensor_copy if on_vector else nc.scalar.copy
+            copy(
+                out=r_tile(i)[:, 256 * b0 : 256 * b1].rearrange("p (g m u) -> p g m u", m=P, u=2),
+                in_=rt_t[i, b0][:, 2 * (b0 % 2) : 2 * (b0 % 2 + b1 - b0)].rearrange("p (g u) m -> p g m u", u=2),
             )
 
-        def r_quant(i):
-            rc_t[i] = work.tile([P, NG * P], U32, name="rc", bufs=TILES, align_bytes=64)
-            rs_t[i] = work.tile([P, NG * P], U8, name="rs", bufs=TILES, align_bytes=64)
-            nc.vector.quantize_mx(out=rc_t[i][:].bitcast(E5M2X4), scales=rs_t[i][:], in_=rg_t[i][:].bitcast(BF16))
+        def t_turn(i, b):
+            rt_t[i, b] = psum.tile([P, 4, P], F32, name="bank", tag="bank", bufs=8)
+            for t in range(4):
+                u, e = divmod(t, 2)
+                first_col = 512 * (b % 2) + 256 * u + e
+                nc.tensor.transpose(
+                    rt_t[i, b][:, t, :], t_t[i, b // 2][:, first_col : first_col + 255 : 2], ident[:]
+                )
+
+        def t_weigh(i, b):
+            nc.vector.tensor_tensor(
+                out=r_tile(i)[:, 256 * b : 256 * (b + 1)].bitcast(BF16).rearrange("p (m t) -> p m t", t=4),
+                in0=rt_t[i, b][:].rearrange("p t m -> p m t"),
+                in1=v_col[:, 4 * b : 4 * b + 4].unsqueeze(1).to_broadcast([P, P, 4]),
+                op=ALU.mult,
+            )
+
+        def r_quant(i, b0=0, b1=NG):
+            if b0 == 0:
+                rc_t[i] = work.tile([P, NG * P], U32, name="rc", bufs=TILES, align_bytes=64)
+                rs_t[i] = work.tile([P, NG * P], U8, name="rs", bufs=TILES, align_bytes=64)
+            nc.vector.quantize_mx(
+                out=rc_t[i][:, P * b0 : P * b1].bitcast(E5M2X4),
+                scales=rs_t[i][:, P * b0 : P * b1],
+                in_=rg_t[i][:, 256 * b0 : 256 * b1].bitcast(BF16),
+            )
+
+        f_words = keep.tile([P, 2 * NG * 2048], BF16, name="f_words", align_bytes=64)
+        f_codes = keep.tile([P, 2 * NG * 512], U32, name="f_codes", align_bytes=64)
+        f_scales = keep.tile([P, 2 * NG * 512], U8, name="f_scales", align_bytes=64)
 
         def f_copy(piece):
-            pair, rest = divmod(piece, 4)
-            c, q = divmod(rest, 2)
-            if rest == 0:
-                fg_t[pair] = work.tile([P, 2, 512, 4], BF16, name="fg", bufs=2, align_bytes=64)
+            c, q = divmod(piece, 2)
             nc.scalar.copy(
-                out=fg_t[pair][:, c, 256 * q : 256 * (q + 1), :].rearrange("p (c i) t -> p c t i", i=4),
-                in_=f_raw[2 * pair + c][:, :, 256 * q : 256 * (q + 1)].rearrange("p t (c i) -> p c t i", i=4),
+                out=f_words[:, 1024 * piece : 1024 * (piece + 1)].rearrange("p (c i t) -> p c t i", i=4, t=4),
+                in_=f_raw[c][:, :, 256 * q : 256 * (q + 1)].rearrange("p t (c i) -> p c t i", i=4),
             )
 
-        def f_quant(pair):
-            fc_t[pair] = work.tile([P, 1024], U32, name="fc", bufs=NG, align_bytes=64)
-            fs_t[pair] = work.tile([P, 1024], U8, name="fs", bufs=NG, align_bytes=64)
+        def f_quant(c0, c1):
             nc.vector.quantize_mx(
-                out=fc_t[pair][:].bitcast(E4M3X4),
-                scales=fs_t[pair][:],
-                in_=fg_t[pair][:].rearrange("p g c j -> p (g c j)"),
+                out=f_codes[:, 512 * c0 : 512 * c1].bitcast(E4M3X4),
+                scales=f_scales[:, 512 * c0 : 512 * c1],
+                in_=f_words[:, 2048 * c0 : 2048 * c1],
             )
 
         def second(i, kh):
@@ -209,8 +250,8 @@ def tile_ftn_residual_turn_s9_kernel(tc, lam, amp, h_words, h_scales, y, v, f, o
                     out=d_t[i, kh][:],
                     lhsT=rc_t[i][:, P * g : P * (g + 1)].bitcast(E5M2X4),
                     lhsT_scale=rs_t[i][:, P * g : P * (g + 1)],
-                    rhs=fc_t[2 * kh + g // 2][:, 512 * (g % 2) : 512 * (g % 2 + 1)].bitcast(E4M3X4),
-                    rhs_scale=fs_t[2 * kh + g // 2][:, 512 * (g % 2) : 512 * (g % 2 + 1)],
+                    rhs=f_codes[:, 512 * (NG * kh + g) : 512 * (NG * kh + g + 1)].bitcast(E4M3X4),
+                    rhs_scale=f_scales[:, 512 * (NG * kh + g) : 512 * (NG * kh + g + 1)],
                     start=(g == 0),
                     stop=(g == NG - 1),
                 )
@@ -223,14 +264,17 @@ def tile_ftn_residual_turn_s9_kernel(tc, lam, amp, h_words, h_scales, y, v, f, o
 
         v_rows = keep.tile([P, NG * 256], F32, name="v_rows", align_bytes=64)
 
-        def spread_v():
+        def v_turn(half):
             words = v_col[:].bitcast(F32)
-            for half in range(2):
-                bank = psum.tile([P, 4, P], F32, name="bank", tag="bank", bufs=8)
-                for j in range(4):
-                    w = 4 * half + j
-                    nc.tensor.transpose(bank[:, j, :], words[:, w : w + 1].to_broadcast([P, P]), ident[:])
-                nc.scalar.copy(out=v_rows[:, 512 * half : 512 * (half + 1)], in_=bank[:].rearrange("p j m -> p (j m)"))
+            vt_t[half] = psum.tile([P, 4, P], F32, name="bank", tag="bank", bufs=8)
+            for j in range(4):
+                w = 4 * half + j
+                nc.tensor.transpose(vt_t[half][:, j, :], words[:, w : w + 1].to_broadcast([P, P]), ident[:])
+
+        def v_copy(half):
+            nc.vector.tensor_copy(
+                out=v_rows[:, 512 * half : 512 * (half + 1)], in_=vt_t[half][:].rearrange("p j m -> p (j m)")
+            )
 
         todo = [(i, kh) for i in range(TILES) for kh in range(2)]
         waiting = []
@@ -241,9 +285,9 @@ def tile_ftn_residual_turn_s9_kernel(tc, lam, amp, h_words, h_scales, y, v, f, o
         def tile_ok(i):
             return 0 <= i < TILES
 
-        def next_second(j):
-            ready = [x for x in todo if x[0] in known_r and 2 * x[1] + 1 in known_f]
-            if ready and j >= FIRST_SECOND:
+        def next_second():
+            ready = [x for x in todo if x[0] in known_r and NG * x[1] + NG - 1 in known_f]
+            if ready:
                 todo.remove(ready[0])
                 second(*ready[0])
                 waiting.append(ready[0])
@@ -257,74 +301,99 @@ def tile_ftn_residual_turn_s9_kernel(tc, lam, amp, h_words, h_scales, y, v, f, o
                 f_copy(len(f_copied))
                 f_copied.append(0)
 
-        def next_f_quant():
-            if len(f_quantised) < len(f_copied) // 4:
-                f_quant(len(f_quantised))
-                f_quantised.append(0)
+        def next_f_quant(margin):
+            c0 = len(f_quantised)
+            c1 = min((len(f_copied) - (margin if len(f_copied) < 4 * NG else 0)) // 2, c0 + 2)
+            if c1 > c0:
+                f_quant(c0, c1)
+                f_quantised.extend(range(c0, c1))
 
-        x_tanh(0)
-        x_turn(0)
+        last = TILES - 1
+        x_tanh(0, 0, 1)
+        x_turn(0, 0, 1)
+        x_tanh(0, 1, 2)
+        x_turn(0, 1, 2)
+        v_turn(0)
+        v_turn(1)
         x_tanh(1)
         x_amp(0, 0)
         x_amp(0, 1)
-        spread_v()
-        x_quant(0)
-        x_turn(1)
-        x_tanh(2)
-        x_amp(1, 0)
-        x_amp(1, 1)
-        x_quant(1)
-        for j in range(TILES + 2):
-            known_f = set(fc_t)
-            if tile_ok(j):
-                first(j, 0)
-                first(j, 1)
-                sub(j, 0)
-                sub(j, 1)
-            next_f_quant()
-            if tile_ok(j):
-                weigh(nc.gpsimd, j, 0, 2)
-            next_second(j)
-            next_f_copy()
-            next_f_copy()
+        x_quant(0, 0, 1)
+        x_quant(0, 1, 2)
+        v_copy(0)
+        v_copy(1)
+        for j in range(TILES):
+            f_now = F_COUNT[j] if j < len(F_COUNT) else 0
+            first(j, 0)
+            first(j, 1)
+            sub(j, 0)
+            sub(j, 1)
+            next_f_quant(2)
+            weigh(nc.gpsimd, j, 0, 2)
+            next_second()
+            if j == 0:
+                next_f_copy()
+                next_f_copy()
+            if j - 1 in A_TILES:
+                t_turn(j - 1, 2)
+            if j < last:
+                x_turn(j + 1)
+            if j > 0:
+                h1 = 3 if j - 1 in A_TILES else 2
+                r_turn(j - 1, 0, 2)
+                r_turn(j - 1, h1, 4)
+                if j - 1 not in V_COPY:
+                    r_copy(j - 1, 0, 2)
+                r_copy(j - 1, h1, 4)
             if tile_ok(j + 2):
-                x_turn(j + 2)
-            if tile_ok(j - 1):
-                r_turn(j - 1, 0)
-                r_turn(j - 1, 1)
-                r_copy(j - 1, 0)
-                r_copy(j - 1, 1)
-            if tile_ok(j + 3):
-                x_tanh(j + 3)
+                x_tanh(j + 2)
             known_r = set(rc_t)
-            if tile_ok(j):
-                first(j, 2)
+            known_f = set(f_quantised)
+            first(j, 2)
             next_add()
-            if tile_ok(j + 2):
-                x_amp(j + 2, 0)
-                x_amp(j + 2, 1)
-            if tile_ok(j):
-                sub(j, 2)
-            if tile_ok(j + 2):
-                x_quant(j + 2)
-            if tile_ok(j):
-                weigh(nc.gpsimd, j, 2, 3)
-            next_second(j)
-            if tile_ok(j):
-                first(j, 3)
+            if j - 1 in A_TILES:
+                t_weigh(j - 1, 2)
+            if j < last:
+                x_amp(j + 1, 0)
+                x_amp(j + 1, 1)
+            sub(j, 2)
+            if j < last:
+                x_quant(j + 1)
+                if j not in A_TILES:
+                    weigh(nc.gpsimd, j, 2, 3)
+            if j in A_TILES:
+                next_f_quant(0)
+            known_f = set(f_quantised)
+            next_second()
+            first(j, 3)
             next_add()
-            if tile_ok(j):
-                sub(j, 3)
-            if tile_ok(j - 1):
+            if j - 1 in V_COPY:
+                r_copy(j - 1, 0, 2, True)
+            if j >= THIRD_FROM:
+                next_second()
+            sub(j, 3)
+            if j > 0:
                 r_quant(j - 1)
-            if tile_ok(j):
+            if j < last:
                 weigh(nc.gpsimd, j, 3, 4)
-            for c in range(F_PER_PERIOD - 2 + (j < 1)):
+            if j >= THIRD_FROM:
+                next_add()
+            for c in range(f_now):
                 next_f_copy()
         known_r = set(rc_t)
+        next_second()
+        weigh(nc.vector, last, 2, 4)
+        r_turn(last, 0, 2)
+        r_copy(last, 0, 2)
+        r_turn(last, 2, 4)
+        r_copy(last, 2, 4)
+        next_second()
+        next_add()
+        next_second()
+        r_quant(last)
+        known_r = set(rc_t)
         while todo:
-            next_second(TILES)
-            if len(waiting) == 2:
-                next_add()
+            next_add()
+            next_second()
         while waiting:
             next_add()

@@ -21,10 +21,11 @@ TILES = M // P
 KG = K // 512
 NG = N // 512
 F_COUNT = (2, 3, 3, 4, 2)
-A_TILES = (0, 1, 2, 3)
+A_TILES = (0, 1, 2)
 S_AMP_FROM = 8
-THIRD_FROM = 5
-ORDER = 1
+THIRD = (5, 6)
+ORDER = "l1 s h0 y00 f0 h1 y01 l2 f1 y1 f2 l3 f3 y2 f4 l4 f5 y3 f6 l5 f7 y4 l6 y5 l7 y6 y7"
+EARLY1 = 1
 V_COPY = ()
 
 
@@ -81,58 +82,77 @@ def tile_ftn_residual_turn_s9_kernel(tc, lam, amp, h_words, h_scales, y, v, f, o
             out=v_col[:].rearrange("p (g t) -> p g t", t=4), in_=v.rearrange("(g p t) -> p g t", g=NG, t=4)
         )
         nc.scalar.activation(out=warm_out[:], in_=warm[:], func=TANH)
-        for q in range(4):
-            nc.sync.dma_start(
-                out=hs[32 * q : 32 * q + 4].bitcast(I32),
-                in_=h_scales[:, 4 * q : 4 * q + 4, :].rearrange("g r n -> r g n").bitcast(I32),
-            )
-        load_h(0)
-        load_y(0, 0, 1)
-        load_lam(1)
-        if ORDER == 1:
-            load_f(0)
-        load_h(1)
-        load_y(0, 1, 2)
-        if ORDER == 0:
-            load_f(0)
-        load_lam(2)
-        load_f(1)
-        for i in range(1, TILES):
-            load_y(i)
-            for c in (2 * i, 2 * i + 1):
-                if c < 2 * NG:
-                    load_f(c)
-            if i + 2 < TILES:
-                load_lam(i + 2)
+
+        def load_scales():
+            for q in range(4):
+                nc.sync.dma_start(
+                    out=hs[32 * q : 32 * q + 4].bitcast(I32),
+                    in_=h_scales[:, 4 * q : 4 * q + 4, :].rearrange("g r n -> r g n").bitcast(I32),
+                )
+
+        for c in ORDER.split():
+            if c == "s":
+                load_scales()
+            elif c[0] == "l":
+                load_lam(int(c[1]))
+            elif c[0] == "h":
+                load_h(int(c[1]))
+            elif c[0] == "f":
+                load_f(int(c[1]))
+            elif len(c) == 3:
+                load_y(int(c[1]), int(c[2]), int(c[2]) + 1)
+            else:
+                load_y(int(c[1]))
 
         xf_t, xt_t, xb_t, xc_t, xs_t = {}, {}, {}, {}, {}
         z_t, t_t, r_t, rt_t, rg_t, rc_t, rs_t, d_t = {}, {}, {}, {}, {}, {}, {}, {}
         vt_t = {}
 
+        def x_turn(i, g0=0, g1=KG):
+            bank = psum.tile([P, 2 * KG, P], F32, name="bank", tag="bank", bufs=7)
+            words = lam_t[i][:].bitcast(F32)
+            for g in range(g0, g1):
+                xt_t[i, g] = bank
+                for u in range(2):
+                    nc.tensor.transpose(
+                        bank[:, 2 * g + u, :], words[:, 256 * g + u : 256 * (g + 1) : 2], ident[:]
+                    )
+
         def x_tanh(i, g0=0, g1=KG):
             if g0 == 0:
-                xf_t[i] = work.tile([P, KG, 4, P], F32, name="xf", bufs=2, align_bytes=64)
-            nc.scalar.activation(
-                out=xf_t[i][:, g0:g1].rearrange("p g t q -> p g q t"),
-                in_=lam_t[i][:, 512 * g0 : 512 * g1].rearrange("p (g q t) -> p g q t", q=P, t=4),
-                func=TANH,
-            )
-
-        def x_turn(i, g0=0, g1=KG):
+                xf_t[i] = work.tile([P, KG, P, 4], F32, name="xf", bufs=2, align_bytes=64)
             for g in range(g0, g1):
-                xt_t[i, g] = psum.tile([P, 4, P], F32, name="bank", tag="bank", bufs=8)
-                for t in range(4):
-                    nc.tensor.transpose(xt_t[i, g][:, t, :], xf_t[i][:, g, t, :], ident[:])
+                nc.scalar.activation(
+                    out=xf_t[i][:, g].rearrange("p m (u e) -> p m u e", u=2),
+                    in_=xt_t[i, g][:, 2 * g : 2 * g + 2, :].bitcast(BF16).rearrange("p u (m e) -> p m u e", e=2),
+                    func=TANH,
+                )
 
-        def x_amp(i, g):
-            if g == 0:
+        def x_amp(i, g0=0, g1=KG):
+            if g0 == 0:
                 xb_t[i] = work.tile([P, KG, P, 4], BF16, name="xb", bufs=2, align_bytes=64)
-            nc.vector.tensor_tensor(
-                out=xb_t[i][:, g],
-                in0=xt_t[i, g][:].rearrange("p t m -> p m t"),
-                in1=amp_col[:, g, :].unsqueeze(1).to_broadcast([P, P, 4]),
-                op=ALU.mult,
-            )
+            if i == 0:
+                factor = amp_col[:, g0:g1, :].unsqueeze(2).to_broadcast([P, g1 - g0, P, 4])
+            else:
+                factor = amp_bank[:].bitcast(BF16).rearrange("p m (g t) -> p g m t", g=KG)[:, g0:g1]
+            nc.vector.tensor_tensor(out=xb_t[i][:, g0:g1], in0=xf_t[i][:, g0:g1], in1=factor, op=ALU.mult)
+
+        amp_bank = psum.tile([P, P, 4], F32, name="amp_bank", tag="amp_bank", bufs=1)
+        amp_rows = keep.tile([P, 4 * P], F32, name="amp_rows", align_bytes=64)
+
+        def amp_spread():
+            words = amp_col[:].rearrange("p g t -> p (g t)").bitcast(F32)
+            bank = psum.tile([P, 4, P], F32, name="bank", tag="bank", bufs=7)
+            for w in range(4):
+                nc.tensor.transpose(bank[:, w, :], words[:, w : w + 1].to_broadcast([P, P]), ident[:])
+            vt_t["amp"] = bank
+
+        def amp_copy():
+            nc.vector.tensor_copy(out=amp_rows[:], in_=vt_t["amp"][:].rearrange("p w m -> p (w m)"))
+
+        def amp_back():
+            for w in range(4):
+                nc.tensor.transpose(amp_bank[:, :, w], amp_rows[:, P * w : P * (w + 1)], ident[:])
 
         def x_quant(i, g0=0, g1=KG):
             if g0 == 0:
@@ -145,7 +165,7 @@ def tile_ftn_residual_turn_s9_kernel(tc, lam, amp, h_words, h_scales, y, v, f, o
             )
 
         def first(i, b):
-            z_t[i, b] = psum.tile([P, 512], F32, name="z", tag="bank", bufs=8)
+            z_t[i, b] = psum.tile([P, 512], F32, name="z", tag="bank", bufs=7)
             half, c = divmod(b, 2)
             for g in range(KG):
                 nc.tensor.matmul_mx(
@@ -181,7 +201,7 @@ def tile_ftn_residual_turn_s9_kernel(tc, lam, amp, h_words, h_scales, y, v, f, o
             )
 
         def r_turn(i, b0, b1):
-            rt_t[i, b0] = psum.tile([P, 4, P], F32, name="bank", tag="bank", bufs=8)
+            rt_t[i, b0] = psum.tile([P, 4, P], F32, name="bank", tag="bank", bufs=7)
             words = r_t[i, b0 // 2][:].bitcast(F32)
             for j in range(2 * (b0 % 2), 2 * (b0 % 2 + b1 - b0)):
                 nc.tensor.transpose(rt_t[i, b0][:, j, :], words[:, P * j : P * (j + 1)], ident[:])
@@ -199,7 +219,7 @@ def tile_ftn_residual_turn_s9_kernel(tc, lam, amp, h_words, h_scales, y, v, f, o
             )
 
         def t_turn(i, b):
-            rt_t[i, b] = psum.tile([P, 4, P], F32, name="bank", tag="bank", bufs=8)
+            rt_t[i, b] = psum.tile([P, 4, P], F32, name="bank", tag="bank", bufs=7)
             for t in range(4):
                 u, e = divmod(t, 2)
                 first_col = 512 * (b % 2) + 256 * u + e
@@ -244,7 +264,7 @@ def tile_ftn_residual_turn_s9_kernel(tc, lam, amp, h_words, h_scales, y, v, f, o
             )
 
         def second(i, kh):
-            d_t[i, kh] = psum.tile([P, 512], F32, name="d", tag="bank", bufs=8)
+            d_t[i, kh] = psum.tile([P, 512], F32, name="d", tag="bank", bufs=7)
             for g in range(NG):
                 nc.tensor.matmul_mx(
                     out=d_t[i, kh][:],
@@ -266,7 +286,7 @@ def tile_ftn_residual_turn_s9_kernel(tc, lam, amp, h_words, h_scales, y, v, f, o
 
         def v_turn(half):
             words = v_col[:].bitcast(F32)
-            vt_t[half] = psum.tile([P, 4, P], F32, name="bank", tag="bank", bufs=8)
+            vt_t[half] = psum.tile([P, 4, P], F32, name="bank", tag="bank", bufs=7)
             for j in range(4):
                 w = 4 * half + j
                 nc.tensor.transpose(vt_t[half][:, j, :], words[:, w : w + 1].to_broadcast([P, P]), ident[:])
@@ -309,53 +329,62 @@ def tile_ftn_residual_turn_s9_kernel(tc, lam, amp, h_words, h_scales, y, v, f, o
                 f_quantised.extend(range(c0, c1))
 
         last = TILES - 1
-        x_tanh(0, 0, 1)
         x_turn(0, 0, 1)
-        x_tanh(0, 1, 2)
+        x_tanh(0, 0, 1)
         x_turn(0, 1, 2)
+        x_tanh(0, 1, 2)
+        amp_spread()
         v_turn(0)
         v_turn(1)
-        x_tanh(1)
-        x_amp(0, 0)
-        x_amp(0, 1)
+        if EARLY1:
+            x_turn(1)
+            x_tanh(1)
+        x_amp(0, 0, 1)
+        x_amp(0, 1, 2)
         x_quant(0, 0, 1)
         x_quant(0, 1, 2)
+        amp_copy()
         v_copy(0)
-        v_copy(1)
         for j in range(TILES):
             f_now = F_COUNT[j] if j < len(F_COUNT) else 0
+            known_r = set(rc_t)
             first(j, 0)
             first(j, 1)
+            if j == 0:
+                if not EARLY1:
+                    x_turn(1)
+                amp_back()
+                if not EARLY1:
+                    x_tanh(1)
             sub(j, 0)
+            if j == 0:
+                v_copy(1)
             sub(j, 1)
             next_f_quant(2)
             weigh(nc.gpsimd, j, 0, 2)
-            next_second()
             if j == 0:
                 next_f_copy()
                 next_f_copy()
             if j - 1 in A_TILES:
                 t_turn(j - 1, 2)
-            if j < last:
-                x_turn(j + 1)
+            next_second()
+            first(j, 2)
+            if tile_ok(j + 2):
+                x_turn(j + 2)
             if j > 0:
                 h1 = 3 if j - 1 in A_TILES else 2
                 r_turn(j - 1, 0, 2)
                 r_turn(j - 1, h1, 4)
-                if j - 1 not in V_COPY:
-                    r_copy(j - 1, 0, 2)
+                r_copy(j - 1, 0, 2)
                 r_copy(j - 1, h1, 4)
             if tile_ok(j + 2):
                 x_tanh(j + 2)
-            known_r = set(rc_t)
             known_f = set(f_quantised)
-            first(j, 2)
+            if j < last:
+                x_amp(j + 1)
             next_add()
             if j - 1 in A_TILES:
                 t_weigh(j - 1, 2)
-            if j < last:
-                x_amp(j + 1, 0)
-                x_amp(j + 1, 1)
             sub(j, 2)
             if j < last:
                 x_quant(j + 1)
@@ -364,29 +393,30 @@ def tile_ftn_residual_turn_s9_kernel(tc, lam, amp, h_words, h_scales, y, v, f, o
             if j in A_TILES:
                 next_f_quant(0)
             known_f = set(f_quantised)
-            next_second()
+            if j < last:
+                next_second()
             first(j, 3)
             next_add()
-            if j - 1 in V_COPY:
-                r_copy(j - 1, 0, 2, True)
-            if j >= THIRD_FROM:
+            if j in THIRD:
                 next_second()
             sub(j, 3)
             if j > 0:
                 r_quant(j - 1)
             if j < last:
                 weigh(nc.gpsimd, j, 3, 4)
-            if j >= THIRD_FROM:
+            if j in THIRD:
                 next_add()
             for c in range(f_now):
                 next_f_copy()
-        known_r = set(rc_t)
         next_second()
         weigh(nc.vector, last, 2, 4)
+        next_second()
+        known_r = set(rc_t)
         r_turn(last, 0, 2)
         r_copy(last, 0, 2)
         r_turn(last, 2, 4)
         r_copy(last, 2, 4)
+        next_add()
         next_second()
         next_add()
         next_second()

@@ -23,9 +23,12 @@ NG = N // 512
 F_COUNT = (2, 3, 3, 4, 2)
 A_TILES = (0, 1, 2)
 S_AMP_FROM = 8
-THIRD = (5, 6)
-ORDER = "l1 s h0 y00 f0 h1 y01 l2 f1 y1 f2 l3 f3 y2 f4 l4 f5 y3 f6 l5 f7 y4 l6 y5 l7 y6 y7"
+THIRD = (4, 5, 6)
+ORDER = "l1 s h0 y00 f0 h1 y01 l2 y10 f1 y11 l3 f2 f3 y2 f4 l4 f5 y3 f6 l5 f7 y4 l6 y5 l7 y6 y7"
 EARLY1 = 1
+MARGIN_A = 2
+MARGIN_B = 0
+SPLIT_UNTIL = 4
 V_COPY = ()
 
 
@@ -131,7 +134,7 @@ def tile_ftn_residual_turn_s9_kernel(tc, lam, amp, h_words, h_scales, y, v, f, o
         def x_amp(i, g0=0, g1=KG):
             if g0 == 0:
                 xb_t[i] = work.tile([P, KG, P, 4], BF16, name="xb", bufs=2, align_bytes=64)
-            if i == 0:
+            if i < 2:
                 factor = amp_col[:, g0:g1, :].unsqueeze(2).to_broadcast([P, g1 - g0, P, 4])
             else:
                 factor = amp_bank[:].bitcast(BF16).rearrange("p m (g t) -> p g m t", g=KG)[:, g0:g1]
@@ -333,88 +336,108 @@ def tile_ftn_residual_turn_s9_kernel(tc, lam, amp, h_words, h_scales, y, v, f, o
         x_tanh(0, 0, 1)
         x_turn(0, 1, 2)
         x_tanh(0, 1, 2)
-        amp_spread()
+        x_turn(1)
+        x_tanh(1)
         v_turn(0)
         v_turn(1)
-        if EARLY1:
-            x_turn(1)
-            x_tanh(1)
         x_amp(0, 0, 1)
         x_amp(0, 1, 2)
         x_quant(0, 0, 1)
         x_quant(0, 1, 2)
-        amp_copy()
         v_copy(0)
+        x_amp(1)
+        first(0, 0)
+        first(0, 1)
+        amp_spread()
         for j in range(TILES):
             f_now = F_COUNT[j] if j < len(F_COUNT) else 0
-            known_r = set(rc_t)
-            first(j, 0)
-            first(j, 1)
-            if j == 0:
-                if not EARLY1:
-                    x_turn(1)
-                amp_back()
-                if not EARLY1:
-                    x_tanh(1)
+            after_a = j == 0 or j - 1 in A_TILES
+            old = len(waiting)
+            if not after_a:
+                next_add()
+                if j < last:
+                    x_amp(j + 1, 0, 1)
+                elif old > 1:
+                    next_add()
             sub(j, 0)
             if j == 0:
-                v_copy(1)
+                x_quant(1)
             sub(j, 1)
-            next_f_quant(2)
+            next_f_quant(MARGIN_A)
             weigh(nc.gpsimd, j, 0, 2)
             if j == 0:
                 next_f_copy()
                 next_f_copy()
             if j - 1 in A_TILES:
                 t_turn(j - 1, 2)
-            next_second()
-            first(j, 2)
+            if after_a or j == last:
+                first(j, 2)
+            if j in (0, last):
+                first(j, 3)
+            if j == 0:
+                v_copy(1)
+                amp_copy()
+                amp_back()
+            if j > 0:
+                r_turn(j - 1, 0, 2)
             if tile_ok(j + 2):
                 x_turn(j + 2)
+            early_z = not after_a and j <= SPLIT_UNTIL
+            if early_z:
+                while waiting:
+                    next_add()
+                first(j, 2)
+                first(j, 3)
             if j > 0:
                 h1 = 3 if j - 1 in A_TILES else 2
-                r_turn(j - 1, 0, 2)
                 r_turn(j - 1, h1, 4)
                 r_copy(j - 1, 0, 2)
                 r_copy(j - 1, h1, 4)
             if tile_ok(j + 2):
                 x_tanh(j + 2)
-            known_f = set(f_quantised)
+            while waiting:
+                next_add()
             if j < last:
-                x_amp(j + 1)
-            next_add()
+                if not after_a and not early_z:
+                    first(j, 2)
+                if j > 0:
+                    if not early_z:
+                        first(j, 3)
+                    x_amp(j + 1, 0 if after_a else 1, 2)
             if j - 1 in A_TILES:
                 t_weigh(j - 1, 2)
-            sub(j, 2)
-            if j < last:
-                x_quant(j + 1)
-                if j not in A_TILES:
-                    weigh(nc.gpsimd, j, 2, 3)
-            if j in A_TILES:
-                next_f_quant(0)
             known_f = set(f_quantised)
-            if j < last:
-                next_second()
-            first(j, 3)
-            next_add()
-            if j in THIRD:
-                next_second()
+            known_r = set(rc_t)
+            next_second()
+            sub(j, 2)
+            next_second()
+            if j in A_TILES and j > 0:
+                x_quant(j + 1)
+                next_f_quant(MARGIN_B)
             sub(j, 3)
+            if j < last:
+                if j > 0 and j not in A_TILES:
+                    x_quant(j + 1)
+                first(j + 1, 0)
+                first(j + 1, 1)
+                if j not in A_TILES or j == 0:
+                    next_f_quant(MARGIN_B)
+            else:
+                weigh(nc.vector, last, 2, 4)
             if j > 0:
                 r_quant(j - 1)
-            if j < last:
-                weigh(nc.gpsimd, j, 3, 4)
             if j in THIRD:
-                next_add()
+                known_f = set(f_quantised)
+                known_r = set(rc_t)
+                next_second()
+            if j < last:
+                weigh(nc.gpsimd, j, 3 if j in A_TILES else 2, 4)
             for c in range(f_now):
                 next_f_copy()
-        next_second()
-        weigh(nc.vector, last, 2, 4)
-        next_second()
         known_r = set(rc_t)
         r_turn(last, 0, 2)
-        r_copy(last, 0, 2)
         r_turn(last, 2, 4)
+        r_copy(last, 0, 2)
         r_copy(last, 2, 4)
         next_add()
         next_second()

@@ -40,9 +40,6 @@ def tile_ftn_residual_turn_s9_kernel(tc, lam, amp, h_words, h_scales, y, v, f, o
         psum = ctx.enter_context(tc.psum_pool(name="psum", bufs=2))
         ctx.enter_context(tc.manual_schedule())
 
-        warm = keep.tile([P, 1], F32, name="warm")
-        nc.vector.memset(warm[:], 0.0)
-        warm_out = keep.tile([P, 1], F32, name="warm_out")
         hs = keep.tile([P, KG, N], U8, name="hs", align_bytes=64)
         nc.vector.memset(hs[:].rearrange("p g n -> p (g n)").bitcast(I32), 0)
         ident = keep.tile([P, P], F32, name="ident", align_bytes=64)
@@ -84,7 +81,6 @@ def tile_ftn_residual_turn_s9_kernel(tc, lam, amp, h_words, h_scales, y, v, f, o
         nc.scalar.dma_start(
             out=v_col[:].rearrange("p (g t) -> p g t", t=4), in_=v.rearrange("(g p t) -> p g t", g=NG, t=4)
         )
-        nc.scalar.activation(out=warm_out[:], in_=warm[:], func=TANH)
 
         def load_scales():
             for q in range(4):

@@ -21,14 +21,20 @@ TILES = M // P
 KG = K // 512
 NG = N // 512
 F_COUNT = (2, 3, 3, 4, 2)
-A_TILES = (0, 1, 2)
+A_TILES = ()
 S_AMP_FROM = 8
-THIRD = (4, 5, 6)
-ORDER = "l1 s h0 y00 f0 h1 y01 l2 y10 f1 y11 l3 f2 f3 y2 f4 l4 f5 y3 f6 l5 f7 y4 l6 y5 l7 y6 y7"
+THIRD = (5, 6)
+ORDER = "l1 s h0 y00 f0 h1 y01 l2 y10 f1 y11 l3 f2 f3 y2 l4 f4 f5 y3 l5 f6 f7 y4 l6 y5 l7 y6 y7"
 EARLY1 = 1
 MARGIN_A = 2
 MARGIN_B = 0
 SPLIT_UNTIL = 4
+CUT = 640
+CUT_UNTIL = 6
+AMP_FIRST = ()
+CUTS = {}
+N_A = 3
+TANH_AT = 2
 V_COPY = ()
 
 
@@ -178,52 +184,47 @@ def tile_ftn_residual_turn_s9_kernel(tc, lam, amp, h_words, h_scales, y, v, f, o
                 )
 
         def sub(i, b):
-            half, c = divmod(b, 2)
-            if c == 0:
-                t_t[i, half] = work.tile([P, 1024], F32, name="t", bufs=4, align_bytes=64)
+            if b == 0:
+                t_t[i] = work.tile([P, N], F32, name="t", bufs=2, align_bytes=64)
+                r_t[i] = work.tile([P, N], BF16, name="r", bufs=2, align_bytes=64)
+            cols = slice(512 * b, 512 * (b + 1))
             nc.vector.tensor_sub(
-                out=t_t[i, half][:, 512 * c : 512 * (c + 1)].rearrange("p (u q e) -> p q u e", u=2, e=2),
-                in0=y_t[i][:, 512 * b : 512 * (b + 1)].rearrange("p (q u e) -> p q u e", u=2, e=2),
+                out=t_t[i][:, cols].rearrange("p (u q e) -> p q u e", u=2, e=2),
+                in0=y_t[i][:, cols].rearrange("p (q u e) -> p q u e", u=2, e=2),
                 in1=z_t[i, b][:].rearrange("p (q u e) -> p q u e", u=2, e=2),
             )
 
-        def weigh(engine, i, b0, b1):
-            half, c = divmod(b0, 2)
-            if (i, half) not in r_t:
-                r_t[i, half] = work.tile([P, 1024], BF16, name="r", bufs=4, align_bytes=64)
-            cols = slice(512 * c, 512 * (c + b1 - b0))
+        def weigh(engine, i, c0, c1):
             engine.tensor_tensor(
-                out=r_t[i, half][:, cols],
-                in0=t_t[i, half][:, cols],
-                in1=v_rows[:, 256 * b0 : 256 * b1].bitcast(BF16),
-                op=ALU.mult,
+                out=r_t[i][:, c0:c1], in0=t_t[i][:, c0:c1], in1=v_rows[:].bitcast(BF16)[:, c0:c1], op=ALU.mult
             )
 
         def r_turn(i, b0, b1):
             rt_t[i, b0] = psum.tile([P, 4, P], F32, name="bank", tag="bank", bufs=7)
-            words = r_t[i, b0 // 2][:].bitcast(F32)
-            for j in range(2 * (b0 % 2), 2 * (b0 % 2 + b1 - b0)):
-                nc.tensor.transpose(rt_t[i, b0][:, j, :], words[:, P * j : P * (j + 1)], ident[:])
+            words = r_t[i][:].bitcast(F32)
+            for j in range(2 * (b1 - b0)):
+                c = 256 * b0 + P * j
+                nc.tensor.transpose(rt_t[i, b0][:, j, :], words[:, c : c + P], ident[:])
 
         def r_tile(i):
             if i not in rg_t:
-                rg_t[i] = work.tile([P, 1024], F32, name="rg", bufs=2, align_bytes=64)
+                rg_t[i] = work.tile([P, 1024], F32, name="rg", bufs=3, align_bytes=64)
             return rg_t[i]
 
         def r_copy(i, b0, b1, on_vector=False):
             copy = nc.vector.tensor_copy if on_vector else nc.scalar.copy
             copy(
                 out=r_tile(i)[:, 256 * b0 : 256 * b1].rearrange("p (g m u) -> p g m u", m=P, u=2),
-                in_=rt_t[i, b0][:, 2 * (b0 % 2) : 2 * (b0 % 2 + b1 - b0)].rearrange("p (g u) m -> p g m u", u=2),
+                in_=rt_t[i, b0][:, 0 : 2 * (b1 - b0)].rearrange("p (g u) m -> p g m u", u=2),
             )
 
         def t_turn(i, b):
             rt_t[i, b] = psum.tile([P, 4, P], F32, name="bank", tag="bank", bufs=7)
             for t in range(4):
                 u, e = divmod(t, 2)
-                first_col = 512 * (b % 2) + 256 * u + e
+                first_col = 512 * b + 256 * u + e
                 nc.tensor.transpose(
-                    rt_t[i, b][:, t, :], t_t[i, b // 2][:, first_col : first_col + 255 : 2], ident[:]
+                    rt_t[i, b][:, t, :], t_t[i][:, first_col : first_col + 255 : 2], ident[:]
                 )
 
         def t_weigh(i, b):
@@ -275,11 +276,13 @@ def tile_ftn_residual_turn_s9_kernel(tc, lam, amp, h_words, h_scales, y, v, f, o
                     stop=(g == NG - 1),
                 )
 
-        def add(i, kh):
-            o = work.tile([P, 512], F32, name="o", bufs=4, align_bytes=64)
-            cols = slice(512 * kh, 512 * (kh + 1))
-            nc.vector.tensor_add(out=o[:], in0=d_t[i, kh][:], in1=lam_t[i][:, cols])
-            nc.sync.dma_start(out=out[P * i : P * (i + 1), cols], in_=o[:])
+        def add(i, kh, parts=1):
+            width = 512 // parts
+            for c in range(parts):
+                o = work.tile([P, width], F32, name="o", bufs=4, align_bytes=64)
+                cols = slice(512 * kh + width * c, 512 * kh + width * (c + 1))
+                nc.vector.tensor_add(out=o[:], in0=d_t[i, kh][:, width * c : width * (c + 1)], in1=lam_t[i][:, cols])
+                nc.sync.dma_start(out=out[P * i : P * (i + 1), cols], in_=o[:])
 
         v_rows = keep.tile([P, NG * 256], F32, name="v_rows", align_bytes=64)
 
@@ -346,90 +349,75 @@ def tile_ftn_residual_turn_s9_kernel(tc, lam, amp, h_words, h_scales, y, v, f, o
         first(0, 1)
         amp_spread()
         for j in range(TILES):
-            f_now = F_COUNT[j] if j < len(F_COUNT) else 0
-            after_a = j == 0 or j - 1 in A_TILES
-            old = len(waiting)
-            if not after_a:
+            a_prev = 0 < j <= N_A
+            cut = 1024 if j == 0 or j >= CUT_UNTIL else CUT
+            older = len(waiting) - (1 if j > N_A + 1 else 0)
+            for c in range(older):
                 next_add()
-                if j < last:
-                    x_amp(j + 1, 0, 1)
-                elif old > 1:
-                    next_add()
             sub(j, 0)
+            if 0 < j < last:
+                x_amp(j + 1)
             if j == 0:
                 x_quant(1)
             sub(j, 1)
+            if 0 < j < last:
+                x_quant(j + 1)
             next_f_quant(MARGIN_A)
-            weigh(nc.gpsimd, j, 0, 2)
+            if 1 < j <= N_A:
+                r_quant(j - 2)
+            weigh(nc.gpsimd, j, 0, cut)
             if j == 0:
                 next_f_copy()
                 next_f_copy()
-            if j - 1 in A_TILES:
-                t_turn(j - 1, 2)
-            if after_a or j == last:
-                first(j, 2)
-            if j in (0, last):
-                first(j, 3)
+            order = (3, 2) if j < N_A else (2, 3)
+            first(j, order[0])
+            first(j, order[1])
             if j == 0:
                 v_copy(1)
                 amp_copy()
                 amp_back()
-            if j > 0:
+                x_turn(2)
+                x_tanh(2)
+            else:
                 r_turn(j - 1, 0, 2)
-            if tile_ok(j + 2):
-                x_turn(j + 2)
-            early_z = not after_a and j <= SPLIT_UNTIL
-            if early_z:
-                while waiting:
-                    next_add()
-                first(j, 2)
-                first(j, 3)
-            if j > 0:
-                h1 = 3 if j - 1 in A_TILES else 2
-                r_turn(j - 1, h1, 4)
+                r_turn(j - 1, 2, 3 if a_prev else 4)
                 r_copy(j - 1, 0, 2)
-                r_copy(j - 1, h1, 4)
-            if tile_ok(j + 2):
-                x_tanh(j + 2)
+                r_copy(j - 1, 2, 3 if a_prev else 4)
             while waiting:
                 next_add()
-            if j < last:
-                if not after_a and not early_z:
-                    first(j, 2)
-                if j > 0:
-                    if not early_z:
-                        first(j, 3)
-                    x_amp(j + 1, 0 if after_a else 1, 2)
-            if j - 1 in A_TILES:
-                t_weigh(j - 1, 2)
+            if a_prev:
+                t_weigh(j - 1, 3)
             known_f = set(f_quantised)
             known_r = set(rc_t)
             next_second()
-            sub(j, 2)
+            sub(j, order[0])
             next_second()
-            if j in A_TILES and j > 0:
-                x_quant(j + 1)
-                next_f_quant(MARGIN_B)
-            sub(j, 3)
+            sub(j, order[1])
             if j < last:
-                if j > 0 and j not in A_TILES:
-                    x_quant(j + 1)
                 first(j + 1, 0)
                 first(j + 1, 1)
-                if j not in A_TILES or j == 0:
-                    next_f_quant(MARGIN_B)
-            else:
-                weigh(nc.vector, last, 2, 4)
-            if j > 0:
+            if j < N_A:
+                t_turn(j, 3)
+            if tile_ok(j + 3):
+                x_turn(j + 3)
+            next_f_quant(MARGIN_B)
+            if j == last:
+                weigh(nc.vector, last, cut, N)
+            if j >= N_A:
                 r_quant(j - 1)
-            if j in THIRD:
+            if j < last:
+                weigh(nc.gpsimd, j, cut, 1536 if j < N_A else N)
+            f_now = F_COUNT[j] if j < len(F_COUNT) else 0
+            for c in range(min(f_now, TANH_AT)):
+                next_f_copy()
+            if tile_ok(j + 3):
+                x_tanh(j + 3)
+            for c in range(f_now - TANH_AT):
+                next_f_copy()
+            if N_A < j < last:
                 known_f = set(f_quantised)
                 known_r = set(rc_t)
                 next_second()
-            if j < last:
-                weigh(nc.gpsimd, j, 3 if j in A_TILES else 2, 4)
-            for c in range(f_now):
-                next_f_copy()
         known_r = set(rc_t)
         r_turn(last, 0, 2)
         r_turn(last, 2, 4)
@@ -444,5 +432,5 @@ def tile_ftn_residual_turn_s9_kernel(tc, lam, amp, h_words, h_scales, y, v, f, o
         while todo:
             next_add()
             next_second()
-        while waiting:
-            next_add()
+        next_add()
+        add(*waiting.pop(), 2)

@@ -31,6 +31,7 @@ MARGIN_B = 0
 SPLIT_UNTIL = 4
 CUT = 640
 CUT_UNTIL = 6
+CUT0 = 640
 AMP_FIRST = ()
 CUTS = {}
 N_A = 3
@@ -52,7 +53,8 @@ def tile_ftn_residual_turn_s9_kernel(tc, lam, amp, h_words, h_scales, y, v, f, o
         make_identity(nc, ident[:])
 
         amp_col = keep.tile([P, KG, 4], BF16, name="amp_col", align_bytes=64)
-        v_col = keep.tile([P, NG * 4], BF16, name="v_col", align_bytes=64)
+        v_in = keep.tile([P, 16], BF16, name="v_in", align_bytes=64)
+        v_col = keep.tile([P, 2], F32, name="v_col", align_bytes=64)
         lam_t, y_t, f_raw, hw = {}, {}, {}, {}
 
         def load_lam(i, parts=1):
@@ -84,15 +86,13 @@ def tile_ftn_residual_turn_s9_kernel(tc, lam, amp, h_words, h_scales, y, v, f, o
 
         load_lam(0, 2)
         nc.scalar.dma_start(out=amp_col[:], in_=amp.rearrange("(g p t) -> p g t", g=KG, t=4))
-        nc.scalar.dma_start(
-            out=v_col[:].rearrange("p (g t) -> p g t", t=4), in_=v.rearrange("(g p t) -> p g t", g=NG, t=4)
-        )
+        nc.scalar.dma_start(out=v_in[:], in_=v.rearrange("(q c) -> q c", c=16))
 
         def load_scales():
-            for q in range(4):
+            for r in range(4):
                 nc.sync.dma_start(
-                    out=hs[32 * q : 32 * q + 4].bitcast(I32),
-                    in_=h_scales[:, 4 * q : 4 * q + 4, :].rearrange("g r n -> r g n").bitcast(I32),
+                    out=hs[r:P:32].bitcast(I32),
+                    in_=h_scales[:, r:16:4, :].rearrange("g q n -> q g n").bitcast(I32),
                 )
 
         for c in ORDER.split():
@@ -231,7 +231,7 @@ def tile_ftn_residual_turn_s9_kernel(tc, lam, amp, h_words, h_scales, y, v, f, o
             nc.vector.tensor_tensor(
                 out=r_tile(i)[:, 256 * b : 256 * (b + 1)].bitcast(BF16).rearrange("p (m t) -> p m t", t=4),
                 in0=rt_t[i, b][:].rearrange("p t m -> p m t"),
-                in1=v_col[:, 4 * b : 4 * b + 4].unsqueeze(1).to_broadcast([P, P, 4]),
+                in1=v_col[:].bitcast(BF16).unsqueeze(1).to_broadcast([P, P, 4]),
                 op=ALU.mult,
             )
 
@@ -286,17 +286,25 @@ def tile_ftn_residual_turn_s9_kernel(tc, lam, amp, h_words, h_scales, y, v, f, o
 
         v_rows = keep.tile([P, NG * 256], F32, name="v_rows", align_bytes=64)
 
-        def v_turn(half):
-            words = v_col[:].bitcast(F32)
-            vt_t[half] = psum.tile([P, 4, P], F32, name="bank", tag="bank", bufs=7)
-            for j in range(4):
-                w = 4 * half + j
-                nc.tensor.transpose(vt_t[half][:, j, :], words[:, w : w + 1].to_broadcast([P, P]), ident[:])
+        def v_turn(u):
+            words = v_in[:].bitcast(F32)
+            vt_t[u] = psum.tile([P, 4, P], F32, name="bank", tag="bank", bufs=7)
+            for i in range(4):
+                w = 2 * i + u
+                nc.tensor.transpose(vt_t[u][:, i, :], words[:, w : w + 1].to_broadcast([P, P]), ident[:])
 
-        def v_copy(half):
+        def v_copy(u):
             nc.vector.tensor_copy(
-                out=v_rows[:, 512 * half : 512 * (half + 1)], in_=vt_t[half][:].rearrange("p j m -> p (j m)")
+                out=v_rows[:].rearrange("p (g u q i) -> p g u q i", g=NG, u=2, i=4)[:, :, u],
+                in_=vt_t[u][:].rearrange("p i (g q) -> p g q i", g=NG),
             )
+
+        def v_back():
+            bank = psum.tile([P, 4, P], F32, name="bank", tag="bank", bufs=7)
+            for u in range(2):
+                c = 256 * (NG - 1) + P * u
+                nc.tensor.transpose(bank[:, u, :], v_rows[:, c : c + P], ident[:])
+            nc.scalar.copy(out=v_col[:], in_=bank[:, 0:2, 0])
 
         todo = [(i, kh) for i in range(TILES) for kh in range(2)]
         waiting = []
@@ -345,12 +353,13 @@ def tile_ftn_residual_turn_s9_kernel(tc, lam, amp, h_words, h_scales, y, v, f, o
         x_quant(0, 1, 2)
         v_copy(0)
         x_amp(1)
+        v_copy(1)
         first(0, 0)
         first(0, 1)
         amp_spread()
         for j in range(TILES):
             a_prev = 0 < j <= N_A
-            cut = 1024 if j == 0 or j >= CUT_UNTIL else CUT
+            cut = CUT0 if j == 0 else 1024 if j >= CUT_UNTIL else CUT
             older = len(waiting) - (1 if j > N_A + 1 else 0)
             for c in range(older):
                 next_add()
@@ -373,9 +382,7 @@ def tile_ftn_residual_turn_s9_kernel(tc, lam, amp, h_words, h_scales, y, v, f, o
             first(j, order[0])
             first(j, order[1])
             if j == 0:
-                v_copy(1)
                 amp_copy()
-                amp_back()
                 x_turn(2)
                 x_tanh(2)
             else:
@@ -396,6 +403,9 @@ def tile_ftn_residual_turn_s9_kernel(tc, lam, amp, h_words, h_scales, y, v, f, o
             if j < last:
                 first(j + 1, 0)
                 first(j + 1, 1)
+            if j == 0:
+                amp_back()
+                v_back()
             if j < N_A:
                 t_turn(j, 3)
             if tile_ok(j + 3):

@@ -20,11 +20,11 @@ FLOPS = 2 * M * K * N * 2
 TILES = M // P
 KG = K // 512
 NG = N // 512
-F_COUNT = (2, 3, 3, 4, 2)
+F_COUNT = (3, 3, 2, 4, 2)
 A_TILES = ()
 S_AMP_FROM = 8
 THIRD = (5, 6)
-ORDER = "l1 s h0 y00 f0 h1 y01 l2 y10 f1 y11 l3 f2 f3 y2 l4 f4 f5 y3 l5 f6 f7 y4 l6 y5 l7 y6 y7"
+ORDER = "l1 s h0 y00 f0 h1 y01 l2 y10 f1 y11 l3 f2 y2 l4 f3 f4 y3 l5 f5 f6 y4 f7 l6 y5 l7 y6 y7"
 EARLY1 = 1
 MARGIN_A = 2
 MARGIN_B = 0
@@ -32,6 +32,9 @@ SPLIT_UNTIL = 4
 CUT = 640
 CUT_UNTIL = 6
 CUT0 = 640
+V_LATE = 0
+CUT3 = 704
+MOVE = 1
 AMP_FIRST = ()
 CUTS = {}
 N_A = 3
@@ -86,7 +89,8 @@ def tile_ftn_residual_turn_s9_kernel(tc, lam, amp, h_words, h_scales, y, v, f, o
 
         load_lam(0, 2)
         nc.scalar.dma_start(out=amp_col[:], in_=amp.rearrange("(g p t) -> p g t", g=KG, t=4))
-        nc.scalar.dma_start(out=v_in[:], in_=v.rearrange("(q c) -> q c", c=16))
+        if not V_LATE:
+            nc.scalar.dma_start(out=v_in[:], in_=v.rearrange("(q c) -> q c", c=16))
 
         def load_scales():
             for r in range(4):
@@ -102,6 +106,8 @@ def tile_ftn_residual_turn_s9_kernel(tc, lam, amp, h_words, h_scales, y, v, f, o
                 load_lam(int(c[1]))
             elif c[0] == "h":
                 load_h(int(c[1]))
+                if V_LATE and c == "h0":
+                    nc.scalar.dma_start(out=v_in[:], in_=v.rearrange("(q c) -> q c", c=16))
             elif c[0] == "f":
                 load_f(int(c[1]))
             elif len(c) == 3:
@@ -304,7 +310,10 @@ def tile_ftn_residual_turn_s9_kernel(tc, lam, amp, h_words, h_scales, y, v, f, o
             for u in range(2):
                 c = 256 * (NG - 1) + P * u
                 nc.tensor.transpose(bank[:, u, :], v_rows[:, c : c + P], ident[:])
-            nc.scalar.copy(out=v_col[:], in_=bank[:, 0:2, 0])
+            vt_t["col"] = bank
+
+        def v_col_copy():
+            nc.vector.tensor_copy(out=v_col[:], in_=vt_t["col"][:, 0:2, 0])
 
         todo = [(i, kh) for i in range(TILES) for kh in range(2)]
         waiting = []
@@ -331,12 +340,11 @@ def tile_ftn_residual_turn_s9_kernel(tc, lam, amp, h_words, h_scales, y, v, f, o
                 f_copy(len(f_copied))
                 f_copied.append(0)
 
-        def next_f_quant(margin):
-            c0 = len(f_quantised)
-            c1 = min((len(f_copied) - (margin if len(f_copied) < 4 * NG else 0)) // 2, c0 + 2)
-            if c1 > c0:
-                f_quant(c0, c1)
-                f_quantised.extend(range(c0, c1))
+        def next_f_quant():
+            c = len(f_quantised)
+            if c < 2 * NG:
+                f_quant(c, c + 1)
+                f_quantised.append(c)
 
         last = TILES - 1
         x_turn(0, 0, 1)
@@ -346,32 +354,41 @@ def tile_ftn_residual_turn_s9_kernel(tc, lam, amp, h_words, h_scales, y, v, f, o
         x_turn(1)
         x_tanh(1)
         v_turn(0)
-        v_turn(1)
+        if not V_LATE:
+            v_turn(1)
         x_amp(0, 0, 1)
         x_amp(0, 1, 2)
         x_quant(0, 0, 1)
         x_quant(0, 1, 2)
         v_copy(0)
         x_amp(1)
-        v_copy(1)
+        if not V_LATE:
+            v_copy(1)
         first(0, 0)
         first(0, 1)
+        if V_LATE:
+            v_turn(1)
         amp_spread()
         for j in range(TILES):
             a_prev = 0 < j <= N_A
-            cut = CUT0 if j == 0 else 1024 if j >= CUT_UNTIL else CUT
+            cut = CUT0 if j == 0 else CUT3 if j == N_A else 1024 if j >= CUT_UNTIL else CUT
             older = len(waiting) - (1 if j > N_A + 1 else 0)
             for c in range(older):
                 next_add()
             sub(j, 0)
             if 0 < j < last:
                 x_amp(j + 1)
+            if j == 1:
+                v_col_copy()
             if j == 0:
                 x_quant(1)
             sub(j, 1)
             if 0 < j < last:
                 x_quant(j + 1)
-            next_f_quant(MARGIN_A)
+            if j == 0 and V_LATE:
+                v_copy(1)
+            if j >= N_A:
+                next_f_quant()
             if 1 < j <= N_A:
                 r_quant(j - 2)
             weigh(nc.gpsimd, j, 0, cut)
@@ -384,10 +401,16 @@ def tile_ftn_residual_turn_s9_kernel(tc, lam, amp, h_words, h_scales, y, v, f, o
             if j == 0:
                 amp_copy()
                 x_turn(2)
+                amp_back()
                 x_tanh(2)
             else:
+                if j == N_A + 1 and MOVE:
+                    next_second()
                 r_turn(j - 1, 0, 2)
                 r_turn(j - 1, 2, 3 if a_prev else 4)
+                if j == 1:
+                    x_turn(3)
+                    x_tanh(3)
                 r_copy(j - 1, 0, 2)
                 r_copy(j - 1, 2, 3 if a_prev else 4)
             while waiting:
@@ -398,19 +421,20 @@ def tile_ftn_residual_turn_s9_kernel(tc, lam, amp, h_words, h_scales, y, v, f, o
             known_r = set(rc_t)
             next_second()
             sub(j, order[0])
-            next_second()
+            if j != N_A or not MOVE:
+                next_second()
             sub(j, order[1])
             if j < last:
                 first(j + 1, 0)
                 first(j + 1, 1)
             if j == 0:
-                amp_back()
                 v_back()
             if j < N_A:
                 t_turn(j, 3)
-            if tile_ok(j + 3):
+            if j > 0 and tile_ok(j + 3):
                 x_turn(j + 3)
-            next_f_quant(MARGIN_B)
+            if j <= N_A + 1:
+                next_f_quant()
             if j == last:
                 weigh(nc.vector, last, cut, N)
             if j >= N_A:
@@ -420,7 +444,7 @@ def tile_ftn_residual_turn_s9_kernel(tc, lam, amp, h_words, h_scales, y, v, f, o
             f_now = F_COUNT[j] if j < len(F_COUNT) else 0
             for c in range(min(f_now, TANH_AT)):
                 next_f_copy()
-            if tile_ok(j + 3):
+            if j > 0 and tile_ok(j + 3):
                 x_tanh(j + 3)
             for c in range(f_now - TANH_AT):
                 next_f_copy()

@@ -29,12 +29,15 @@ EARLY1 = 1
 MARGIN_A = 2
 MARGIN_B = 0
 SPLIT_UNTIL = 4
-CUT = 640
+CUT = 704
 CUT_UNTIL = 6
 CUT0 = 640
 V_LATE = 0
 CUT3 = 704
 MOVE = 1
+LT7 = 1
+QF_FIRST = 0
+PAIR = 0
 AMP_FIRST = ()
 CUTS = {}
 N_A = 3
@@ -159,7 +162,7 @@ def tile_ftn_residual_turn_s9_kernel(tc, lam, amp, h_words, h_scales, y, v, f, o
             vt_t["amp"] = bank
 
         def amp_copy():
-            nc.vector.tensor_copy(out=amp_rows[:], in_=vt_t["amp"][:].rearrange("p w m -> p (w m)"))
+            nc.scalar.copy(out=amp_rows[:], in_=vt_t["amp"][:].rearrange("p w m -> p (w m)"))
 
         def amp_back():
             for w in range(4):
@@ -340,19 +343,21 @@ def tile_ftn_residual_turn_s9_kernel(tc, lam, amp, h_words, h_scales, y, v, f, o
                 f_copy(len(f_copied))
                 f_copied.append(0)
 
-        def next_f_quant():
+        def next_f_quant(count=1):
             c = len(f_quantised)
             if c < 2 * NG:
-                f_quant(c, c + 1)
-                f_quantised.append(c)
+                f_quant(c, c + count)
+                f_quantised.extend(range(c, c + count))
 
         last = TILES - 1
         x_turn(0, 0, 1)
         x_tanh(0, 0, 1)
         x_turn(0, 1, 2)
         x_tanh(0, 1, 2)
+        amp_spread()
         x_turn(1)
         x_tanh(1)
+        amp_copy()
         v_turn(0)
         if not V_LATE:
             v_turn(1)
@@ -366,9 +371,7 @@ def tile_ftn_residual_turn_s9_kernel(tc, lam, amp, h_words, h_scales, y, v, f, o
             v_copy(1)
         first(0, 0)
         first(0, 1)
-        if V_LATE:
-            v_turn(1)
-        amp_spread()
+        amp_back()
         for j in range(TILES):
             a_prev = 0 < j <= N_A
             cut = CUT0 if j == 0 else CUT3 if j == N_A else 1024 if j >= CUT_UNTIL else CUT
@@ -383,12 +386,14 @@ def tile_ftn_residual_turn_s9_kernel(tc, lam, amp, h_words, h_scales, y, v, f, o
             if j == 0:
                 x_quant(1)
             sub(j, 1)
+            if j == N_A + 2 and QF_FIRST:
+                next_f_quant(1 + PAIR)
             if 0 < j < last:
                 x_quant(j + 1)
             if j == 0 and V_LATE:
                 v_copy(1)
             if j >= N_A:
-                next_f_quant()
+                next_f_quant(1 + PAIR if j == N_A + 2 else 1)
             if 1 < j <= N_A:
                 r_quant(j - 2)
             weigh(nc.gpsimd, j, 0, cut)
@@ -399,13 +404,13 @@ def tile_ftn_residual_turn_s9_kernel(tc, lam, amp, h_words, h_scales, y, v, f, o
             first(j, order[0])
             first(j, order[1])
             if j == 0:
-                amp_copy()
                 x_turn(2)
-                amp_back()
                 x_tanh(2)
             else:
                 if j == N_A + 1 and MOVE:
                     next_second()
+                    if LT7:
+                        x_turn(j + 3)
                 r_turn(j - 1, 0, 2)
                 r_turn(j - 1, 2, 3 if a_prev else 4)
                 if j == 1:
@@ -413,6 +418,8 @@ def tile_ftn_residual_turn_s9_kernel(tc, lam, amp, h_words, h_scales, y, v, f, o
                     x_tanh(3)
                 r_copy(j - 1, 0, 2)
                 r_copy(j - 1, 2, 3 if a_prev else 4)
+                if j == N_A + 1 and LT7:
+                    x_tanh(j + 3)
             while waiting:
                 next_add()
             if a_prev:
@@ -431,9 +438,9 @@ def tile_ftn_residual_turn_s9_kernel(tc, lam, amp, h_words, h_scales, y, v, f, o
                 v_back()
             if j < N_A:
                 t_turn(j, 3)
-            if j > 0 and tile_ok(j + 3):
+            if j > 0 and tile_ok(j + 3 + LT7):
                 x_turn(j + 3)
-            if j <= N_A + 1:
+            if j <= N_A + 1 - PAIR:
                 next_f_quant()
             if j == last:
                 weigh(nc.vector, last, cut, N)
@@ -444,7 +451,7 @@ def tile_ftn_residual_turn_s9_kernel(tc, lam, amp, h_words, h_scales, y, v, f, o
             f_now = F_COUNT[j] if j < len(F_COUNT) else 0
             for c in range(min(f_now, TANH_AT)):
                 next_f_copy()
-            if j > 0 and tile_ok(j + 3):
+            if j > 0 and tile_ok(j + 3 + LT7):
                 x_tanh(j + 3)
             for c in range(f_now - TANH_AT):
                 next_f_copy()

@@ -20,29 +20,13 @@ FLOPS = 2 * M * K * N * 2
 TILES = M // P
 KG = K // 512
 NG = N // 512
-F_COUNT = (3, 3, 2, 4, 2)
-A_TILES = ()
-S_AMP_FROM = 8
-THIRD = (5, 6)
-ORDER = "l1 s h0 y00 f0 h1 y01 l2 y10 f1 y11 l3 f2 y2 l4 f3 f4 y3 l5 f5 f6 y4 f7 l6 y5 l7 y6 y7"
-EARLY1 = 1
-MARGIN_A = 2
-MARGIN_B = 0
-SPLIT_UNTIL = 4
+LAST = TILES - 1
+EARLY = 3
 CUT = 704
+CUT_FIRST = 640
 CUT_UNTIL = 6
-CUT0 = 640
-V_LATE = 0
-CUT3 = 704
-MOVE = 1
-LT7 = 1
-QF_FIRST = 0
-PAIR = 0
-AMP_FIRST = ()
-CUTS = {}
-N_A = 3
-TANH_AT = 2
-V_COPY = ()
+F_PER_PERIOD = 3
+F_BEFORE_TANH = 2
 
 
 def tile_ftn_residual_turn_s9_kernel(tc, lam, amp, h_words, h_scales, y, v, f, out):
@@ -92,31 +76,30 @@ def tile_ftn_residual_turn_s9_kernel(tc, lam, amp, h_words, h_scales, y, v, f, o
 
         load_lam(0, 2)
         nc.scalar.dma_start(out=amp_col[:], in_=amp.rearrange("(g p t) -> p g t", g=KG, t=4))
-        if not V_LATE:
-            nc.scalar.dma_start(out=v_in[:], in_=v.rearrange("(q c) -> q c", c=16))
-
-        def load_scales():
-            for r in range(4):
-                nc.sync.dma_start(
-                    out=hs[r:P:32].bitcast(I32),
-                    in_=h_scales[:, r:16:4, :].rearrange("g q n -> q g n").bitcast(I32),
-                )
-
-        for c in ORDER.split():
-            if c == "s":
-                load_scales()
-            elif c[0] == "l":
-                load_lam(int(c[1]))
-            elif c[0] == "h":
-                load_h(int(c[1]))
-                if V_LATE and c == "h0":
-                    nc.scalar.dma_start(out=v_in[:], in_=v.rearrange("(q c) -> q c", c=16))
-            elif c[0] == "f":
-                load_f(int(c[1]))
-            elif len(c) == 3:
-                load_y(int(c[1]), int(c[2]), int(c[2]) + 1)
-            else:
-                load_y(int(c[1]))
+        nc.scalar.dma_start(out=v_in[:], in_=v.rearrange("(q c) -> q c", c=16))
+        load_lam(1)
+        for r in range(4):
+            nc.sync.dma_start(
+                out=hs[r:P:32].bitcast(I32),
+                in_=h_scales[:, r:16:4, :].rearrange("g q n -> q g n").bitcast(I32),
+            )
+        load_h(0)
+        load_y(0, 0, 1)
+        load_f(0)
+        load_h(1)
+        load_y(0, 1, 2)
+        load_lam(2)
+        load_y(1, 0, 1)
+        load_f(1)
+        load_y(1, 1, 2)
+        load_lam(3)
+        load_f(2)
+        for i in range(2, TILES):
+            load_y(i)
+            if i + 2 < TILES:
+                load_lam(i + 2)
+            for c in range(2 * i - 1, min(2 * i + 1, 2 * NG)):
+                load_f(c)
 
         xf_t, xt_t, xb_t, xc_t, xs_t = {}, {}, {}, {}, {}
         z_t, t_t, r_t, rt_t, rg_t, rc_t, rs_t, d_t = {}, {}, {}, {}, {}, {}, {}, {}
@@ -220,14 +203,13 @@ def tile_ftn_residual_turn_s9_kernel(tc, lam, amp, h_words, h_scales, y, v, f, o
                 rg_t[i] = work.tile([P, 1024], F32, name="rg", bufs=3, align_bytes=64)
             return rg_t[i]
 
-        def r_copy(i, b0, b1, on_vector=False):
-            copy = nc.vector.tensor_copy if on_vector else nc.scalar.copy
-            copy(
+        def r_copy(i, b0, b1):
+            nc.scalar.copy(
                 out=r_tile(i)[:, 256 * b0 : 256 * b1].rearrange("p (g m u) -> p g m u", m=P, u=2),
                 in_=rt_t[i, b0][:, 0 : 2 * (b1 - b0)].rearrange("p (g u) m -> p g m u", u=2),
             )
 
-        def t_turn(i, b):
+        def t_turn(i, b=NG - 1):
             rt_t[i, b] = psum.tile([P, 4, P], F32, name="bank", tag="bank", bufs=7)
             for t in range(4):
                 u, e = divmod(t, 2)
@@ -236,7 +218,7 @@ def tile_ftn_residual_turn_s9_kernel(tc, lam, amp, h_words, h_scales, y, v, f, o
                     rt_t[i, b][:, t, :], t_t[i][:, first_col : first_col + 255 : 2], ident[:]
                 )
 
-        def t_weigh(i, b):
+        def t_weigh(i, b=NG - 1):
             nc.vector.tensor_tensor(
                 out=r_tile(i)[:, 256 * b : 256 * (b + 1)].bitcast(BF16).rearrange("p (m t) -> p m t", t=4),
                 in0=rt_t[i, b][:].rearrange("p t m -> p m t"),
@@ -244,15 +226,10 @@ def tile_ftn_residual_turn_s9_kernel(tc, lam, amp, h_words, h_scales, y, v, f, o
                 op=ALU.mult,
             )
 
-        def r_quant(i, b0=0, b1=NG):
-            if b0 == 0:
-                rc_t[i] = work.tile([P, NG * P], U32, name="rc", bufs=TILES, align_bytes=64)
-                rs_t[i] = work.tile([P, NG * P], U8, name="rs", bufs=TILES, align_bytes=64)
-            nc.vector.quantize_mx(
-                out=rc_t[i][:, P * b0 : P * b1].bitcast(E5M2X4),
-                scales=rs_t[i][:, P * b0 : P * b1],
-                in_=rg_t[i][:, 256 * b0 : 256 * b1].bitcast(BF16),
-            )
+        def r_quant(i):
+            rc_t[i] = work.tile([P, NG * P], U32, name="rc", bufs=TILES, align_bytes=64)
+            rs_t[i] = work.tile([P, NG * P], U8, name="rs", bufs=TILES, align_bytes=64)
+            nc.vector.quantize_mx(out=rc_t[i][:].bitcast(E5M2X4), scales=rs_t[i][:], in_=rg_t[i][:].bitcast(BF16))
 
         f_words = keep.tile([P, 2 * NG * 2048], BF16, name="f_words", align_bytes=64)
         f_codes = keep.tile([P, 2 * NG * 512], U32, name="f_codes", align_bytes=64)
@@ -265,11 +242,11 @@ def tile_ftn_residual_turn_s9_kernel(tc, lam, amp, h_words, h_scales, y, v, f, o
                 in_=f_raw[c][:, :, 256 * q : 256 * (q + 1)].rearrange("p t (c i) -> p c t i", i=4),
             )
 
-        def f_quant(c0, c1):
+        def f_quant(c):
             nc.vector.quantize_mx(
-                out=f_codes[:, 512 * c0 : 512 * c1].bitcast(E4M3X4),
-                scales=f_scales[:, 512 * c0 : 512 * c1],
-                in_=f_words[:, 2048 * c0 : 2048 * c1],
+                out=f_codes[:, 512 * c : 512 * (c + 1)].bitcast(E4M3X4),
+                scales=f_scales[:, 512 * c : 512 * (c + 1)],
+                in_=f_words[:, 2048 * c : 2048 * (c + 1)],
             )
 
         def second(i, kh):
@@ -319,37 +296,32 @@ def tile_ftn_residual_turn_s9_kernel(tc, lam, amp, h_words, h_scales, y, v, f, o
             nc.vector.tensor_copy(out=v_col[:], in_=vt_t["col"][:, 0:2, 0])
 
         todo = [(i, kh) for i in range(TILES) for kh in range(2)]
-        waiting = []
-        known_r, known_f = set(), set()
-        f_copied = []
-        f_quantised = []
+        ready, waiting = [], []
+        f_halves = list(range(4 * NG))
+        f_pieces = list(range(2 * NG))
 
-        def tile_ok(i):
-            return 0 <= i < TILES
+        def look():
+            ready[:] = [(i, kh) for i, kh in todo if i in rc_t and NG * kh + NG - 1 not in f_pieces]
 
         def next_second():
-            ready = [x for x in todo if x[0] in known_r and NG * x[1] + NG - 1 in known_f]
             if ready:
                 todo.remove(ready[0])
                 second(*ready[0])
-                waiting.append(ready[0])
+                waiting.append(ready.pop(0))
 
-        def next_add():
-            if waiting:
+        def next_adds(count):
+            for c in range(count):
                 add(*waiting.pop(0))
 
-        def next_f_copy():
-            if len(f_copied) < 4 * NG:
-                f_copy(len(f_copied))
-                f_copied.append(0)
+        def next_f_copies(count):
+            for piece in f_halves[:count]:
+                f_copy(piece)
+                f_halves.remove(piece)
 
-        def next_f_quant(count=1):
-            c = len(f_quantised)
-            if c < 2 * NG:
-                f_quant(c, c + count)
-                f_quantised.extend(range(c, c + count))
+        def next_f_quant():
+            if f_pieces:
+                f_quant(f_pieces.pop(0))
 
-        last = TILES - 1
         x_turn(0, 0, 1)
         x_tanh(0, 0, 1)
         x_turn(0, 1, 2)
@@ -359,119 +331,109 @@ def tile_ftn_residual_turn_s9_kernel(tc, lam, amp, h_words, h_scales, y, v, f, o
         x_tanh(1)
         amp_copy()
         v_turn(0)
-        if not V_LATE:
-            v_turn(1)
+        v_turn(1)
         x_amp(0, 0, 1)
         x_amp(0, 1, 2)
         x_quant(0, 0, 1)
         x_quant(0, 1, 2)
         v_copy(0)
         x_amp(1)
-        if not V_LATE:
-            v_copy(1)
+        v_copy(1)
         first(0, 0)
         first(0, 1)
         amp_back()
+
         for j in range(TILES):
-            a_prev = 0 < j <= N_A
-            cut = CUT0 if j == 0 else CUT3 if j == N_A else 1024 if j >= CUT_UNTIL else CUT
-            older = len(waiting) - (1 if j > N_A + 1 else 0)
-            for c in range(older):
-                next_add()
+            early, after_early = j < EARLY, 0 < j <= EARLY
+            cut = CUT_FIRST if j == 0 else CUT if j < CUT_UNTIL else N // 2
+
+            next_adds(len(waiting) - (1 if j > EARLY + 1 else 0))
             sub(j, 0)
-            if 0 < j < last:
+            if 0 < j < LAST:
                 x_amp(j + 1)
             if j == 1:
                 v_col_copy()
             if j == 0:
                 x_quant(1)
             sub(j, 1)
-            if j == N_A + 2 and QF_FIRST:
-                next_f_quant(1 + PAIR)
-            if 0 < j < last:
+            if 0 < j < LAST:
                 x_quant(j + 1)
-            if j == 0 and V_LATE:
-                v_copy(1)
-            if j >= N_A:
-                next_f_quant(1 + PAIR if j == N_A + 2 else 1)
-            if 1 < j <= N_A:
+            if not early:
+                next_f_quant()
+            if after_early and j > 1:
                 r_quant(j - 2)
             weigh(nc.gpsimd, j, 0, cut)
             if j == 0:
-                next_f_copy()
-                next_f_copy()
-            order = (3, 2) if j < N_A else (2, 3)
-            first(j, order[0])
-            first(j, order[1])
+                next_f_copies(2)
+
+            b0, b1 = (3, 2) if early else (2, 3)
+            first(j, b0)
+            first(j, b1)
             if j == 0:
                 x_turn(2)
                 x_tanh(2)
             else:
-                if j == N_A + 1 and MOVE:
+                if j == EARLY + 1:
                     next_second()
-                    if LT7:
-                        x_turn(j + 3)
+                    x_turn(LAST)
+                end = NG - 1 if after_early else NG
                 r_turn(j - 1, 0, 2)
-                r_turn(j - 1, 2, 3 if a_prev else 4)
+                r_turn(j - 1, 2, end)
                 if j == 1:
                     x_turn(3)
                     x_tanh(3)
                 r_copy(j - 1, 0, 2)
-                r_copy(j - 1, 2, 3 if a_prev else 4)
-                if j == N_A + 1 and LT7:
-                    x_tanh(j + 3)
-            while waiting:
-                next_add()
-            if a_prev:
-                t_weigh(j - 1, 3)
-            known_f = set(f_quantised)
-            known_r = set(rc_t)
+                r_copy(j - 1, 2, end)
+                if j == EARLY + 1:
+                    x_tanh(LAST)
+            next_adds(len(waiting))
+            if after_early:
+                t_weigh(j - 1)
+            look()
             next_second()
-            sub(j, order[0])
-            if j != N_A or not MOVE:
+            sub(j, b0)
+            if j != EARLY:
                 next_second()
-            sub(j, order[1])
-            if j < last:
+            sub(j, b1)
+            if j < LAST:
                 first(j + 1, 0)
                 first(j + 1, 1)
             if j == 0:
                 v_back()
-            if j < N_A:
-                t_turn(j, 3)
-            if j > 0 and tile_ok(j + 3 + LT7):
+            if early:
+                t_turn(j)
+            if 0 < j <= EARLY:
                 x_turn(j + 3)
-            if j <= N_A + 1 - PAIR:
+            if j <= EARLY + 1:
                 next_f_quant()
-            if j == last:
-                weigh(nc.vector, last, cut, N)
-            if j >= N_A:
+            if j == LAST:
+                weigh(nc.vector, j, cut, N)
+            if not early:
                 r_quant(j - 1)
-            if j < last:
-                weigh(nc.gpsimd, j, cut, 1536 if j < N_A else N)
-            f_now = F_COUNT[j] if j < len(F_COUNT) else 0
-            for c in range(min(f_now, TANH_AT)):
-                next_f_copy()
-            if j > 0 and tile_ok(j + 3 + LT7):
+            if j < LAST:
+                weigh(nc.gpsimd, j, cut, N - 512 if early else N)
+
+            count = F_PER_PERIOD - (j == EARLY - 1) + (j == EARLY)
+            next_f_copies(F_BEFORE_TANH)
+            if 0 < j <= EARLY:
                 x_tanh(j + 3)
-            for c in range(f_now - TANH_AT):
-                next_f_copy()
-            if N_A < j < last:
-                known_f = set(f_quantised)
-                known_r = set(rc_t)
+            next_f_copies(count - F_BEFORE_TANH)
+            if EARLY < j < LAST:
+                look()
                 next_second()
-        known_r = set(rc_t)
-        r_turn(last, 0, 2)
-        r_turn(last, 2, 4)
-        r_copy(last, 0, 2)
-        r_copy(last, 2, 4)
-        next_add()
-        next_second()
-        next_add()
-        next_second()
-        r_quant(last)
-        known_r = set(rc_t)
-        while todo:
-            next_add()
+
+        look()
+        r_turn(LAST, 0, 2)
+        r_turn(LAST, 2, NG)
+        r_copy(LAST, 0, 2)
+        r_copy(LAST, 2, NG)
+        for c in range(2):
+            next_adds(1)
             next_second()
-        next_add()
+        r_quant(LAST)
+        look()
+        while todo:
+            next_adds(1)
+            next_second()
+        next_adds(1)
         add(*waiting.pop(), 2)

@@ -21,12 +21,10 @@ TILES = M // P
 KG = K // 512
 NG = N // 512
 LAST = TILES - 1
-EARLY = 3
-CUT = 704
-CUT_FIRST = 640
-CUT_UNTIL = 6
-F_PER_PERIOD = 3
-F_BEFORE_TANH = 2
+EARLY = 2
+XF_BUFS = 2
+T_BUFS = 4
+BANKS = 7
 
 
 def tile_ftn_residual_turn_s9_kernel(tc, lam, amp, h_words, h_scales, y, v, f, out):
@@ -44,7 +42,6 @@ def tile_ftn_residual_turn_s9_kernel(tc, lam, amp, h_words, h_scales, y, v, f, o
 
         amp_col = keep.tile([P, KG, 4], BF16, name="amp_col", align_bytes=64)
         v_in = keep.tile([P, 16], BF16, name="v_in", align_bytes=64)
-        v_col = keep.tile([P, 2], F32, name="v_col", align_bytes=64)
         lam_t, y_t, f_raw, hw = {}, {}, {}, {}
 
         def load_lam(i, parts=1):
@@ -74,56 +71,40 @@ def tile_ftn_residual_turn_s9_kernel(tc, lam, amp, h_words, h_scales, y, v, f, o
                 in_=h_words[:, :, N * half : N * (half + 1)].rearrange("g p c -> p g c").bitcast(I32),
             )
 
-        load_lam(0, 2)
-        nc.scalar.dma_start(out=amp_col[:], in_=amp.rearrange("(g p t) -> p g t", g=KG, t=4))
-        nc.scalar.dma_start(out=v_in[:], in_=v.rearrange("(q c) -> q c", c=16))
-        load_lam(1)
-        for r in range(4):
-            nc.sync.dma_start(
-                out=hs[r:P:32].bitcast(I32),
-                in_=h_scales[:, r:16:4, :].rearrange("g q n -> q g n").bitcast(I32),
-            )
-        load_h(0)
-        load_y(0, 0, 1)
-        load_f(0)
-        load_h(1)
-        load_y(0, 1, 2)
-        load_lam(2)
-        load_y(1, 0, 1)
-        load_f(1)
-        load_y(1, 1, 2)
-        load_lam(3)
-        load_f(2)
-        for i in range(2, TILES):
-            load_y(i)
-            if i + 2 < TILES:
-                load_lam(i + 2)
-            for c in range(2 * i - 1, min(2 * i + 1, 2 * NG)):
-                load_f(c)
+        def load_scales(c0, c1):
+            for r in range(4):
+                nc.sync.dma_start(
+                    out=hs[r:P:32, :, c0:c1].bitcast(I32),
+                    in_=h_scales[:, r:16:4, c0:c1].rearrange("g q n -> q g n").bitcast(I32),
+                )
 
         xf_t, xt_t, xb_t, xc_t, xs_t = {}, {}, {}, {}, {}
-        z_t, t_t, r_t, rt_t, rg_t, rc_t, rs_t, d_t = {}, {}, {}, {}, {}, {}, {}, {}
-        vt_t = {}
+        z_t, t_t, r_at, rt_t, rg_t, rc_t, rs_t, d_t = {}, {}, {}, {}, {}, {}, {}, {}
+        small = {}
+
+        def new_bank():
+            return psum.tile([P, 4, P], F32, name="bank", tag="bank", bufs=7)
 
         def x_turn(i, g0=0, g1=KG):
-            bank = psum.tile([P, 2 * KG, P], F32, name="bank", tag="bank", bufs=7)
+            bank = new_bank()
             words = lam_t[i][:].bitcast(F32)
             for g in range(g0, g1):
                 xt_t[i, g] = bank
                 for u in range(2):
-                    nc.tensor.transpose(
-                        bank[:, 2 * g + u, :], words[:, 256 * g + u : 256 * (g + 1) : 2], ident[:]
-                    )
+                    nc.tensor.transpose(bank[:, 2 * g + u, :], words[:, 256 * g + u : 256 * (g + 1) : 2], ident[:])
 
         def x_tanh(i, g0=0, g1=KG):
             if g0 == 0:
-                xf_t[i] = work.tile([P, KG, P, 4], F32, name="xf", bufs=2, align_bytes=64)
+                xf_t[i] = work.tile([P, KG, P, 4], F32, name="xf", bufs=XF_BUFS, align_bytes=64)
             for g in range(g0, g1):
                 nc.scalar.activation(
                     out=xf_t[i][:, g].rearrange("p m (u e) -> p m u e", u=2),
                     in_=xt_t[i, g][:, 2 * g : 2 * g + 2, :].bitcast(BF16).rearrange("p u (m e) -> p m u e", e=2),
                     func=TANH,
                 )
+
+        amp_bank = psum.tile([P, P, 4], F32, name="amp_bank", tag="factor", bufs=1)
+        amp_rows = keep.tile([P, 4 * P], F32, name="amp_rows", align_bytes=64)
 
         def x_amp(i, g0=0, g1=KG):
             if g0 == 0:
@@ -134,18 +115,14 @@ def tile_ftn_residual_turn_s9_kernel(tc, lam, amp, h_words, h_scales, y, v, f, o
                 factor = amp_bank[:].bitcast(BF16).rearrange("p m (g t) -> p g m t", g=KG)[:, g0:g1]
             nc.vector.tensor_tensor(out=xb_t[i][:, g0:g1], in0=xf_t[i][:, g0:g1], in1=factor, op=ALU.mult)
 
-        amp_bank = psum.tile([P, P, 4], F32, name="amp_bank", tag="amp_bank", bufs=1)
-        amp_rows = keep.tile([P, 4 * P], F32, name="amp_rows", align_bytes=64)
-
         def amp_spread():
             words = amp_col[:].rearrange("p g t -> p (g t)").bitcast(F32)
-            bank = psum.tile([P, 4, P], F32, name="bank", tag="bank", bufs=7)
+            small["amp"] = new_bank()
             for w in range(4):
-                nc.tensor.transpose(bank[:, w, :], words[:, w : w + 1].to_broadcast([P, P]), ident[:])
-            vt_t["amp"] = bank
+                nc.tensor.transpose(small["amp"][:, w, :], words[:, w : w + 1].to_broadcast([P, P]), ident[:])
 
         def amp_copy():
-            nc.scalar.copy(out=amp_rows[:], in_=vt_t["amp"][:].rearrange("p w m -> p (w m)"))
+            nc.scalar.copy(out=amp_rows[:], in_=small["amp"][:].rearrange("p w m -> p (w m)"))
 
         def amp_back():
             for w in range(4):
@@ -153,8 +130,8 @@ def tile_ftn_residual_turn_s9_kernel(tc, lam, amp, h_words, h_scales, y, v, f, o
 
         def x_quant(i, g0=0, g1=KG):
             if g0 == 0:
-                xc_t[i] = work.tile([P, KG * P], U32, name="xc", bufs=3, align_bytes=64)
-                xs_t[i] = work.tile([P, KG * P], U8, name="xs", bufs=3, align_bytes=64)
+                xc_t[i] = work.tile([P, KG * P], U32, name="xc", bufs=4, align_bytes=64)
+                xs_t[i] = work.tile([P, KG * P], U8, name="xs", bufs=4, align_bytes=64)
             nc.vector.quantize_mx(
                 out=xc_t[i][:, P * g0 : P * g1].bitcast(E4M3X4),
                 scales=xs_t[i][:, P * g0 : P * g1],
@@ -162,11 +139,11 @@ def tile_ftn_residual_turn_s9_kernel(tc, lam, amp, h_words, h_scales, y, v, f, o
             )
 
         def first(i, b):
-            z_t[i, b] = psum.tile([P, 512], F32, name="z", tag="bank", bufs=7)
+            z_t[i, b] = new_bank()
             half, c = divmod(b, 2)
             for g in range(KG):
                 nc.tensor.matmul_mx(
-                    out=z_t[i, b][:],
+                    out=z_t[i, b][:].rearrange("p a m -> p (a m)"),
                     lhsT=xc_t[i][:, P * g : P * (g + 1)].bitcast(E4M3X4),
                     lhsT_scale=xs_t[i][:, P * g : P * (g + 1)],
                     rhs=hw[half][:, g, 1024 * c : 1024 * (c + 1)].bitcast(E2M1X4),
@@ -176,69 +153,132 @@ def tile_ftn_residual_turn_s9_kernel(tc, lam, amp, h_words, h_scales, y, v, f, o
                 )
 
         def sub(i, b):
-            if b == 0:
-                t_t[i] = work.tile([P, N], F32, name="t", bufs=2, align_bytes=64)
-                r_t[i] = work.tile([P, N], BF16, name="r", bufs=2, align_bytes=64)
+            if i not in t_t:
+                t_t[i] = work.tile([P, N], F32, name="t", bufs=T_BUFS, align_bytes=64)
             cols = slice(512 * b, 512 * (b + 1))
             nc.vector.tensor_sub(
-                out=t_t[i][:, cols].rearrange("p (u q e) -> p q u e", u=2, e=2),
-                in0=y_t[i][:, cols].rearrange("p (q u e) -> p q u e", u=2, e=2),
-                in1=z_t[i, b][:].rearrange("p (q u e) -> p q u e", u=2, e=2),
+                out=t_t[i][:, cols].rearrange("p (u q e) -> p u q e", u=2, e=2),
+                in0=y_t[i][:, cols].rearrange("p (q u e) -> p u q e", u=2, e=2),
+                in1=z_t[i, b][:].rearrange("p a (q u e) -> p u (a q) e", u=2, e=2),
             )
 
-        def weigh(engine, i, c0, c1):
-            engine.tensor_tensor(
-                out=r_t[i][:, c0:c1], in0=t_t[i][:, c0:c1], in1=v_rows[:].bitcast(BF16)[:, c0:c1], op=ALU.mult
+        v_rows = keep.tile([P, NG * 256], F32, name="v_rows", align_bytes=64)
+
+        def v_turn(u):
+            bank = small[u] = new_bank()
+            words = v_in[:].bitcast(F32)
+            for i in range(4):
+                w = 2 * i + u
+                nc.tensor.transpose(bank[:, i, :], words[:, w : w + 1].to_broadcast([P, P]), ident[:])
+
+        def v_copy(u):
+            nc.scalar.copy(
+                out=v_rows[:].rearrange("p (g u q i) -> p g u q i", g=NG, u=2, i=4)[:, :, u],
+                in_=small[u][:].rearrange("p i (g q) -> p g q i", g=NG),
             )
 
-        def r_turn(i, b0, b1):
-            rt_t[i, b0] = psum.tile([P, 4, P], F32, name="bank", tag="bank", bufs=7)
-            words = r_t[i][:].bitcast(F32)
-            for j in range(2 * (b1 - b0)):
-                c = 256 * b0 + P * j
-                nc.tensor.transpose(rt_t[i, b0][:, j, :], words[:, c : c + P], ident[:])
+        def weigh(i, c0, c1, space, engine=nc.gpsimd):
+            dst = space[:, space.shape[1] - (c1 - c0) :]
+            for c in range(c0, c1, 256):
+                r_at[i, c // 256] = dst[:, c - c0 : c - c0 + 256]
+            engine.tensor_tensor(out=dst, in0=t_t[i][:, c0:c1], in1=v_rows[:].bitcast(BF16)[:, c0:c1], op=ALU.mult)
+
+        def weigh_even(i, g0, g1, space):
+            dst = space[:, space.shape[1] - 256 * (g1 - g0) :]
+            for g in range(g0, g1):
+                r_at[i, 2 * g] = dst[:, 256 * (g - g0) : 256 * (g - g0 + 1)]
+            nc.gpsimd.tensor_tensor(
+                out=dst.rearrange("p (g c) -> p g c", c=256),
+                in0=t_t[i][:].rearrange("p (g u c) -> p g u c", u=2, c=256)[:, g0:g1, 0],
+                in1=v_rows[:].bitcast(BF16).rearrange("p (g u c) -> p g u c", u=2, c=256)[:, g0:g1, 0],
+                op=ALU.mult,
+            )
+
+        def odd_turn():
+            small["odd"] = psum.tile([P, P, 4], F32, name="odd_bank", tag="factor", bufs=1)
+            words = v_in[:].bitcast(F32)
+            for i in range(4):
+                w = 2 * i + 1
+                nc.tensor.transpose(small["odd"][:, :, i], words[:, w : w + 1].to_broadcast([P, P]), ident[:])
+
+        def weigh_odd(i, g0, g1):
+            dst = work.tile([P, 512], BF16, name="r_odd", bufs=4, align_bytes=64)
+            for g in range(g0, g1):
+                r_at[i, 2 * g + 1] = dst[:, 256 * (g - g0) : 256 * (g - g0 + 1)]
+            factor = small["odd"][:].rearrange("p q i -> p (q i)").bitcast(BF16)
+            nc.vector.tensor_tensor(
+                out=dst[:, : 256 * (g1 - g0)].rearrange("p (g c) -> p g c", c=256),
+                in0=t_t[i][:].rearrange("p (g u c) -> p g u c", u=2, c=256)[:, g0:g1, 1],
+                in1=factor.rearrange("p (g c) -> p g c", c=256)[:, g0:g1],
+                op=ALU.mult,
+            )
+
+        def r_turn(i, half):
+            rt_t[i, half] = new_bank()
+            for j in range(r_blocks(i, half)):
+                nc.tensor.transpose(rt_t[i, half][:, j, :], r_at[i, 4 * half + j].bitcast(F32), ident[:])
+
+        def r_blocks(i, half):
+            return 2 if i < EARLY and half == 1 else 4
 
         def r_tile(i):
             if i not in rg_t:
                 rg_t[i] = work.tile([P, 1024], F32, name="rg", bufs=3, align_bytes=64)
             return rg_t[i]
 
-        def r_copy(i, b0, b1):
+        def r_copy(i, half):
+            count = r_blocks(i, half)
             nc.scalar.copy(
-                out=r_tile(i)[:, 256 * b0 : 256 * b1].rearrange("p (g m u) -> p g m u", m=P, u=2),
-                in_=rt_t[i, b0][:, 0 : 2 * (b1 - b0)].rearrange("p (g u) m -> p g m u", u=2),
+                out=r_tile(i)[:, 512 * half : 512 * half + P * count].rearrange("p (g m u) -> p g m u", m=P, u=2),
+                in_=rt_t[i, half][:, :count].rearrange("p (g u) m -> p g m u", u=2),
             )
 
-        def t_turn(i, b=NG - 1):
-            rt_t[i, b] = psum.tile([P, 4, P], F32, name="bank", tag="bank", bufs=7)
+        v_col = keep.tile([P, 2], F32, name="v_col", align_bytes=64)
+
+        def v_back():
+            small["col"] = new_bank()
+            for u in range(2):
+                c = 256 * (NG - 1) + P * u
+                nc.tensor.transpose(small["col"][:, u, :], v_rows[:, c : c + P], ident[:])
+
+        def v_col_copy():
+            nc.scalar.copy(out=v_col[:], in_=small["col"][:, 0:2, 0])
+
+        def t_turn(i):
+            rt_t[i, "t"] = new_bank()
             for t in range(4):
                 u, e = divmod(t, 2)
-                first_col = 512 * b + 256 * u + e
-                nc.tensor.transpose(
-                    rt_t[i, b][:, t, :], t_t[i][:, first_col : first_col + 255 : 2], ident[:]
-                )
+                c = 512 * (NG - 1) + 256 * u + e
+                nc.tensor.transpose(rt_t[i, "t"][:, t, :], t_t[i][:, c : c + 255 : 2], ident[:])
 
-        def t_weigh(i, b=NG - 1):
+        def t_weigh(i):
             nc.vector.tensor_tensor(
-                out=r_tile(i)[:, 256 * b : 256 * (b + 1)].bitcast(BF16).rearrange("p (m t) -> p m t", t=4),
-                in0=rt_t[i, b][:].rearrange("p t m -> p m t"),
+                out=r_tile(i)[:, 256 * (NG - 1) :].bitcast(BF16).rearrange("p (m t) -> p m t", t=4),
+                in0=rt_t[i, "t"][:].rearrange("p t m -> p m t"),
                 in1=v_col[:].bitcast(BF16).unsqueeze(1).to_broadcast([P, P, 4]),
                 op=ALU.mult,
             )
 
-        def r_quant(i):
-            rc_t[i] = work.tile([P, NG * P], U32, name="rc", bufs=TILES, align_bytes=64)
-            rs_t[i] = work.tile([P, NG * P], U8, name="rs", bufs=TILES, align_bytes=64)
-            nc.vector.quantize_mx(out=rc_t[i][:].bitcast(E5M2X4), scales=rs_t[i][:], in_=rg_t[i][:].bitcast(BF16))
+        def r_quant(i, h0=0, h1=2):
+            if h0 == 0:
+                rc_t[i] = work.tile([P, NG * P], U32, name="rc", bufs=5, align_bytes=64)
+                rs_t[i] = work.tile([P, NG * P], U8, name="rs", bufs=5, align_bytes=64)
+            nc.vector.quantize_mx(
+                out=rc_t[i][:, 256 * h0 : 256 * h1].bitcast(E5M2X4),
+                scales=rs_t[i][:, 256 * h0 : 256 * h1],
+                in_=rg_t[i][:, 512 * h0 : 512 * h1].bitcast(BF16),
+            )
 
-        f_words = keep.tile([P, 2 * NG * 2048], BF16, name="f_words", align_bytes=64)
+        f_words = {}
         f_codes = keep.tile([P, 2 * NG * 512], U32, name="f_codes", align_bytes=64)
         f_scales = keep.tile([P, 2 * NG * 512], U8, name="f_scales", align_bytes=64)
 
         def f_copy(piece):
             c, q = divmod(piece, 2)
+            if q == 0:
+                f_words[c] = work.tile([P, 2048], BF16, name="f_words", bufs=4, align_bytes=64)
             nc.scalar.copy(
-                out=f_words[:, 1024 * piece : 1024 * (piece + 1)].rearrange("p (c i t) -> p c t i", i=4, t=4),
+                out=f_words[c][:, 1024 * q : 1024 * (q + 1)].rearrange("p (c i t) -> p c t i", i=4, t=4),
                 in_=f_raw[c][:, :, 256 * q : 256 * (q + 1)].rearrange("p t (c i) -> p c t i", i=4),
             )
 
@@ -246,14 +286,14 @@ def tile_ftn_residual_turn_s9_kernel(tc, lam, amp, h_words, h_scales, y, v, f, o
             nc.vector.quantize_mx(
                 out=f_codes[:, 512 * c : 512 * (c + 1)].bitcast(E4M3X4),
                 scales=f_scales[:, 512 * c : 512 * (c + 1)],
-                in_=f_words[:, 2048 * c : 2048 * (c + 1)],
+                in_=f_words[c][:],
             )
 
         def second(i, kh):
-            d_t[i, kh] = psum.tile([P, 512], F32, name="d", tag="bank", bufs=7)
+            d_t[i, kh] = new_bank()
             for g in range(NG):
                 nc.tensor.matmul_mx(
-                    out=d_t[i, kh][:],
+                    out=d_t[i, kh][:].rearrange("p a m -> p (a m)"),
                     lhsT=rc_t[i][:, P * g : P * (g + 1)].bitcast(E5M2X4),
                     lhsT_scale=rs_t[i][:, P * g : P * (g + 1)],
                     rhs=f_codes[:, 512 * (NG * kh + g) : 512 * (NG * kh + g + 1)].bitcast(E4M3X4),
@@ -262,178 +302,165 @@ def tile_ftn_residual_turn_s9_kernel(tc, lam, amp, h_words, h_scales, y, v, f, o
                     stop=(g == NG - 1),
                 )
 
-        def add(i, kh, parts=1):
+        def add(i, kh):
+            parts = 2 if (i, kh) == (LAST, 1) else 1
             width = 512 // parts
+            d = d_t[i, kh][:].rearrange("p a m -> p (a m)")
             for c in range(parts):
-                o = work.tile([P, width], F32, name="o", bufs=4, align_bytes=64)
+                o = work.tile([P, width], F32, name="o", bufs=6, align_bytes=64)
                 cols = slice(512 * kh + width * c, 512 * kh + width * (c + 1))
-                nc.vector.tensor_add(out=o[:], in0=d_t[i, kh][:, width * c : width * (c + 1)], in1=lam_t[i][:, cols])
+                nc.vector.tensor_add(out=o[:], in0=d[:, width * c : width * (c + 1)], in1=lam_t[i][:, cols])
                 nc.sync.dma_start(out=out[P * i : P * (i + 1), cols], in_=o[:])
 
-        v_rows = keep.tile([P, NG * 256], F32, name="v_rows", align_bytes=64)
+        load_lam(0, 2)
+        nc.scalar.dma_start(out=amp_col[:], in_=amp.rearrange("(g p t) -> p g t", g=KG, t=4))
+        nc.scalar.dma_start(out=v_in[:], in_=v.rearrange("(q c) -> q c", c=16))
+        load_lam(1)
+        load_scales(0, N)
+        load_lam(2)
+        load_h(0)
+        load_f(0)
+        load_h(1)
+        load_y(0, 0, 1)
+        load_y(0, 1, 2)
+        load_lam(3)
+        load_y(1, 0, 1)
+        load_f(1)
+        load_y(1, 1, 2)
+        for i in range(2, TILES):
+            if i + 2 < TILES:
+                load_lam(i + 2)
+            load_f(i)
+            load_y(i)
 
-        def v_turn(u):
-            words = v_in[:].bitcast(F32)
-            vt_t[u] = psum.tile([P, 4, P], F32, name="bank", tag="bank", bufs=7)
-            for i in range(4):
-                w = 2 * i + u
-                nc.tensor.transpose(vt_t[u][:, i, :], words[:, w : w + 1].to_broadcast([P, P]), ident[:])
-
-        def v_copy(u):
-            nc.vector.tensor_copy(
-                out=v_rows[:].rearrange("p (g u q i) -> p g u q i", g=NG, u=2, i=4)[:, :, u],
-                in_=vt_t[u][:].rearrange("p i (g q) -> p g q i", g=NG),
-            )
-
-        def v_back():
-            bank = psum.tile([P, 4, P], F32, name="bank", tag="bank", bufs=7)
-            for u in range(2):
-                c = 256 * (NG - 1) + P * u
-                nc.tensor.transpose(bank[:, u, :], v_rows[:, c : c + P], ident[:])
-            vt_t["col"] = bank
-
-        def v_col_copy():
-            nc.vector.tensor_copy(out=v_col[:], in_=vt_t["col"][:, 0:2, 0])
-
-        todo = [(i, kh) for i in range(TILES) for kh in range(2)]
-        ready, waiting = [], []
-        f_halves = list(range(4 * NG))
-        f_pieces = list(range(2 * NG))
-
-        def look():
-            ready[:] = [(i, kh) for i, kh in todo if i in rc_t and NG * kh + NG - 1 not in f_pieces]
-
-        def next_second():
-            if ready:
-                todo.remove(ready[0])
-                second(*ready[0])
-                waiting.append(ready.pop(0))
-
-        def next_adds(count):
-            for c in range(count):
-                add(*waiting.pop(0))
-
-        def next_f_copies(count):
-            for piece in f_halves[:count]:
-                f_copy(piece)
-                f_halves.remove(piece)
-
-        def next_f_quant():
-            if f_pieces:
-                f_quant(f_pieces.pop(0))
-
-        x_turn(0, 0, 1)
-        x_tanh(0, 0, 1)
-        x_turn(0, 1, 2)
-        x_tanh(0, 1, 2)
-        amp_spread()
-        x_turn(1)
-        x_tanh(1)
-        amp_copy()
-        v_turn(0)
-        v_turn(1)
-        x_amp(0, 0, 1)
-        x_amp(0, 1, 2)
-        x_quant(0, 0, 1)
-        x_quant(0, 1, 2)
-        v_copy(0)
-        x_amp(1)
-        v_copy(1)
-        first(0, 0)
-        first(0, 1)
-        amp_back()
-
-        for j in range(TILES):
-            early, after_early = j < EARLY, 0 < j <= EARLY
-            cut = CUT_FIRST if j == 0 else CUT if j < CUT_UNTIL else N // 2
-
-            next_adds(len(waiting) - (1 if j > EARLY + 1 else 0))
-            sub(j, 0)
-            if 0 < j < LAST:
-                x_amp(j + 1)
-            if j == 1:
-                v_col_copy()
-            if j == 0:
-                x_quant(1)
-            sub(j, 1)
-            if 0 < j < LAST:
-                x_quant(j + 1)
-            if not early:
-                next_f_quant()
-            if after_early and j > 1:
-                r_quant(j - 2)
-            weigh(nc.gpsimd, j, 0, cut)
-            if j == 0:
-                next_f_copies(2)
-
-            b0, b1 = (3, 2) if early else (2, 3)
-            first(j, b0)
-            first(j, b1)
-            if j == 0:
-                x_turn(2)
-                x_tanh(2)
+        def weigh_tile(i):
+            if i == 4:
+                space = f_words[2 * NG - 1][:]
+            elif i == LAST - 1:
+                space = y_t[LAST][:, : N // 2]
+            elif i == LAST:
+                space = rg_t[LAST - 2][:].bitcast(BF16)
             else:
-                if j == EARLY + 1:
-                    next_second()
-                    x_turn(LAST)
-                end = NG - 1 if after_early else NG
-                r_turn(j - 1, 0, 2)
-                r_turn(j - 1, 2, end)
-                if j == 1:
-                    x_turn(3)
-                    x_tanh(3)
-                r_copy(j - 1, 0, 2)
-                r_copy(j - 1, 2, end)
-                if j == EARLY + 1:
-                    x_tanh(LAST)
-            next_adds(len(waiting))
-            if after_early:
-                t_weigh(j - 1)
-            look()
-            next_second()
-            sub(j, b0)
-            if j != EARLY:
-                next_second()
-            sub(j, b1)
-            if j < LAST:
-                first(j + 1, 0)
-                first(j + 1, 1)
+                r = work.tile([P, N], BF16, name="r", bufs=2, align_bytes=64)
+                space = r[:]
+            if i >= LAST - 1:
+                weigh_even(i, 0, NG, space)
+            else:
+                weigh(i, 0, N - 512 if i < EARLY else N, space)
+
+        def blocks_of(i):
+            return [(sub, i, b) for b in ((0, 1, 3, 2) if i < EARLY else range(NG))]
+
+        def product(step):
+            return (first if step[0] == sub else second, *step[1:])
+
+        vector = [(x_amp, 0, 0, 1), (x_amp, 0, 1, 2), (x_quant, 0, 0, 1), (x_quant, 0, 1, 2), (x_amp, 1), (x_quant, 1), (x_amp, 2)]
+        s = blocks_of(0)
+        vector.extend([s[0], (x_quant, 2), s[1], (f_quant, 0), s[2], s[3], (weigh_tile, 0)])
+        tensor = [(x_turn, 0, 0, 1), (x_turn, 0, 1, 2), (amp_spread,), (x_turn, 1), (v_turn, 0), (v_turn, 1), (x_turn, 2), (amp_back,)]
+        scalar = [(x_tanh, 0, 0, 1), (x_tanh, 0, 1, 2), (amp_copy,), (x_tanh, 1), (v_copy, 0), (v_copy, 1), (x_tanh, 2), (f_copy, 0), (f_copy, 1)]
+        runs, piece = [s], 1
+        for j in range(1, LAST - 1):
+            own = blocks_of(j)[max(0, j - 3) :]
+            subs = own[:-1] + blocks_of(j + 1)[: max(0, j - 2)] + own[-1:]
+            extra = (t_weigh, j - 1) if j - 1 < EARLY else (add, j - 3, 0)
+            runs.append(subs[:2] + [(x_amp, j + 2), subs[2], extra] + subs[3:])
+            end = min(piece + 1 if j % 2 else NG * j // 2, 2 * NG)
+            vector.extend(runs[j] + [(x_quant, j + 2)] + [(r_quant, j - 2)][: j // 2])
+            vector.extend([(f_quant, c) for c in range(piece, end)] + [(weigh_tile, j)])
+            piece = end
+        a, b = LAST - 1, LAST
+        runs.append([(add, 0, 1), (add, 1, 1), (add, 2, 1), (sub, a, 3), (weigh_odd, a, 0, 2), (sub, b, 0), (weigh_odd, a, 2, 4), (sub, b, 1)])
+        runs.append([(add, 3, 0), (sub, b, 2), (add, 3, 1), (sub, b, 3)])
+        vector.extend(runs[a] + [(r_quant, a - 2), (weigh_tile, a)] + runs[b] + [(r_quant, b - 2), (weigh_tile, b)])
+        vector.extend([(weigh_odd, b, 0, 2), (add, 4, 0), (weigh_odd, b, 2, 4), (add, 4, 1)])
+        vector.extend([(r_quant, a), (add, 5, 0), (add, 5, 1), (r_quant, b), (add, a, 0), (add, a, 1), (add, b, 0), (add, b, 1)])
+
+        def products(run):
+            return [product(x) for x in run if x[0] in (sub, add)]
+
+        done = 0
+        for j in range(LAST - 1):
+            tensor.extend(products(runs[j])[done:])
+            if j + 3 < TILES:
+                tensor.append((x_turn, j + 3))
             if j == 0:
-                v_back()
-            if early:
-                t_turn(j)
-            if 0 < j <= EARLY:
-                x_turn(j + 3)
-            if j <= EARLY + 1:
-                next_f_quant()
-            if j == LAST:
-                weigh(nc.vector, j, cut, N)
-            if not early:
-                r_quant(j - 1)
-            if j < LAST:
-                weigh(nc.gpsimd, j, cut, N - 512 if early else N)
+                tensor.append((v_back,))
+            ahead = [x for x in products(runs[j + 1])[: 2 if j < LAST - 2 else 3] if x[1] <= j + 1]
+            done = len(ahead)
+            tensor.extend(ahead)
+            if j == LAST - 2:
+                tensor.append((odd_turn,))
+            if j > 0:
+                tensor.extend([(r_turn, j - 1, 0), (r_turn, j - 1, 1)])
+            if j < EARLY:
+                tensor.append((t_turn, j))
+        rest = products(runs[a])[done:] + products(runs[b])
+        tensor.extend(rest[:-1] + [(r_turn, a - 1, 0), (r_turn, a - 1, 1)] + rest[-1:])
+        for i in range(4, TILES):
+            tensor.extend([(second, i, 0), (second, i, 1)])
+            if i + 2 < TILES:
+                tensor.extend([(r_turn, i + 2, 0), (r_turn, i + 2, 1)])
 
-            count = F_PER_PERIOD - (j == EARLY - 1) + (j == EARLY)
-            next_f_copies(F_BEFORE_TANH)
-            if 0 < j <= EARLY:
-                x_tanh(j + 3)
-            next_f_copies(count - F_BEFORE_TANH)
-            if EARLY < j < LAST:
-                look()
-                next_second()
+        def pieces(c0, c1):
+            return [(f_copy, q) for q in range(2 * c0, 2 * c1)]
 
-        look()
-        r_turn(LAST, 0, 2)
-        r_turn(LAST, 2, NG)
-        r_copy(LAST, 0, 2)
-        r_copy(LAST, 2, NG)
-        for c in range(2):
-            next_adds(1)
-            next_second()
-        r_quant(LAST)
-        look()
-        while todo:
-            next_adds(1)
-            next_second()
-        next_adds(1)
-        add(*waiting.pop(), 2)
+        def copies(i):
+            return [(r_copy, i, 0), (r_copy, i, 1)]
+
+        scalar.extend([(x_tanh, 3), (v_col_copy,)] + pieces(1, 2) + [(x_tanh, 4)] + pieces(2, 3) + copies(0) + pieces(3, 4))
+        for j in range(2, LAST - 2):
+            scalar.extend([(x_tanh, j + 3)] + copies(j - 1) + pieces(2 * j, min(2 * j + 2, 2 * NG)))
+        for i in range(4, TILES):
+            scalar.extend(copies(i))
+
+        def weighed(i):
+            return [(weigh_tile, i)] + [(weigh_odd, i, g, g + 2) for g in (0, 2) if i >= LAST - 1]
+
+        def needs(step):
+            call, i = step[0], step[1] if len(step) > 1 else 0
+            table = {
+                x_tanh: [(x_turn, *step[1:])] + [(x_amp, k) if k else (x_amp, 0, 1, 2) for k in (i - XF_BUFS,) if k >= 0],
+                x_amp: [(x_tanh, *step[1:])] + [(amp_back,)][: i // 2],
+                amp_copy: [(amp_spread,)],
+                amp_back: [(amp_copy,)],
+                v_copy: [(v_turn, i)],
+                v_back: [(v_copy, 0), (v_copy, 1)],
+                v_col_copy: [(v_back,)],
+                odd_turn: [(x_amp, LAST)],
+                weigh_odd: [(odd_turn,)],
+                weigh_tile: [(v_copy, 1)] + [(r_turn, k, 1) for k in (i - 2,) if k >= 0],
+                first: [(x_quant, i) if i else (x_quant, 0, 1, 2)],
+                sub: [(first, *step[1:])],
+                t_turn: [(sub, i, NG - 1)],
+                t_weigh: [(t_turn, i), (v_col_copy,)],
+                r_turn: weighed(i),
+                r_copy: [(r_turn, *step[1:])] + [(r_quant, k) for k in (i - 3,) if k >= 0],
+                r_quant: copies(i),
+                f_copy: [(f_quant, k) for k in (i // 2 - 4,) if k >= 0],
+                f_quant: pieces(i, i + 1),
+                second: [(r_quant, i), (f_quant, NG - 1 if step[-1] == 0 else 2 * NG - 1)],
+                add: [(second, *step[1:])],
+            }
+            return table.get(call, [])
+
+        reader = {x_turn: x_tanh, amp_spread: amp_copy, v_turn: v_copy, v_back: v_col_copy, first: sub, second: add,
+                  r_turn: r_copy, t_turn: t_weigh}
+        written, banks = set(), []
+        queues = [tensor, scalar, vector]
+        while any(queues):
+            moved = False
+            for queue in queues:
+                while queue:
+                    step = queue[0]
+                    wanted = needs(step)
+                    if step[0] in reader and len(banks) >= BANKS:
+                        wanted = wanted + [banks[-BANKS]]
+                    if not all(x in written for x in wanted):
+                        break
+                    if step[0] in reader:
+                        banks.append((reader[step[0]], *step[1:]))
+                    step[0](*step[1:])
+                    written.add(queue.pop(0))
+                    moved = True
+            assert moved

@@ -21,10 +21,10 @@ TILES = M // P
 KG = K // 512
 NG = N // 512
 LAST = TILES - 1
-EARLY = 2
-XF_BUFS = 2
-T_BUFS = 4
+PAIRS = TILES // 2
 BANKS = 7
+XF_BUFS = 2
+F_BUFS = 4
 
 
 def tile_ftn_residual_turn_s9_kernel(tc, lam, amp, h_words, h_scales, y, v, f, out):
@@ -32,16 +32,18 @@ def tile_ftn_residual_turn_s9_kernel(tc, lam, amp, h_words, h_scales, y, v, f, o
     with ExitStack() as ctx:
         keep = ctx.enter_context(tc.tile_pool(name="keep", bufs=1))
         work = ctx.enter_context(tc.tile_pool(name="work", bufs=2))
-        psum = ctx.enter_context(tc.psum_pool(name="psum", bufs=2))
+        psum = ctx.enter_context(tc.psum_pool(name="psum", bufs=1))
         ctx.enter_context(tc.manual_schedule())
 
+        amp_rows = keep.tile([P, 256], F32, name="amp_rows", align_bytes=64)
+        nc.vector.memset(amp_rows[:], 0.0)
         hs = keep.tile([P, KG, N], U8, name="hs", align_bytes=64)
         nc.vector.memset(hs[:].rearrange("p g n -> p (g n)").bitcast(I32), 0)
         ident = keep.tile([P, P], F32, name="ident", align_bytes=64)
         make_identity(nc, ident[:])
 
-        amp_col = keep.tile([P, KG, 4], BF16, name="amp_col", align_bytes=64)
         v_in = keep.tile([P, 16], BF16, name="v_in", align_bytes=64)
+        v_col = {}
         lam_t, y_t, f_raw, hw = {}, {}, {}, {}
 
         def load_lam(i, parts=1):
@@ -71,62 +73,76 @@ def tile_ftn_residual_turn_s9_kernel(tc, lam, amp, h_words, h_scales, y, v, f, o
                 in_=h_words[:, :, N * half : N * (half + 1)].rearrange("g p c -> p g c").bitcast(I32),
             )
 
-        def load_scales(c0, c1):
+        def load_scales():
             for r in range(4):
                 nc.sync.dma_start(
-                    out=hs[r:P:32, :, c0:c1].bitcast(I32),
-                    in_=h_scales[:, r:16:4, c0:c1].rearrange("g q n -> q g n").bitcast(I32),
+                    out=hs[r:P:32].bitcast(I32),
+                    in_=h_scales[:, r:16:4].rearrange("g q n -> q g n").bitcast(I32),
                 )
 
-        xf_t, xt_t, xb_t, xc_t, xs_t = {}, {}, {}, {}, {}
-        z_t, t_t, r_at, rt_t, rg_t, rc_t, rs_t, d_t = {}, {}, {}, {}, {}, {}, {}, {}
-        small = {}
+        def load_v_col(g, queue):
+            v_col[g] = work.tile([P, 4], BF16, name="v_col", bufs=2, align_bytes=64)
+            queue.dma_start(out=v_col[g][:], in_=v[512 * g : 512 * (g + 1)].rearrange("(q c) -> q c", c=4))
 
-        def new_bank():
-            return psum.tile([P, 4, P], F32, name="bank", tag="bank", bufs=7)
+        xf_t, xb_t, xc_t, xs_t = {}, {}, {}, {}
+        t_t, r_at, rc_t, rs_t = {}, {}, {}, {}
+        bank_of, free = {}, list(range(BANKS))
+
+        def take(key):
+            k = free.pop(0)
+            bank_of[key] = (k, psum.tile([P, 4, P], F32, name="bank", tag="bank%d" % k, bufs=1))
+            return bank_of[key][1]
+
+        def give(key):
+            k, bank = bank_of[key]
+            free.append(k)
+            return bank
+
+        factors = psum.tile([P, 512], F32, name="factors", tag="factors", bufs=1)
+        amp_col = keep.tile([P, 4], F32, name="amp_col", align_bytes=64)
+
+        def amp_turn():
+            for u in range(2):
+                nc.tensor.transpose(factors[:, u:256:2], amp_rows[:, u:256:2], ident[:])
+
+        def v_col_turn(g):
+            words = v_col[g][:].bitcast(F32)
+            for u in range(2):
+                c = 256 * (g - 2) + P * u
+                nc.tensor.transpose(factors[:, c : c + P], words[:, u : u + 1].to_broadcast([P, P]), ident[:])
+
+        def amp_copy():
+            nc.vector.tensor_copy(out=amp_col[:], in_=factors[:, 0:4])
 
         def x_turn(i, g0=0, g1=KG):
-            bank = new_bank()
+            bank = take(("x", i, g0))
             words = lam_t[i][:].bitcast(F32)
             for g in range(g0, g1):
-                xt_t[i, g] = bank
                 for u in range(2):
                     nc.tensor.transpose(bank[:, 2 * g + u, :], words[:, 256 * g + u : 256 * (g + 1) : 2], ident[:])
 
         def x_tanh(i, g0=0, g1=KG):
             if g0 == 0:
                 xf_t[i] = work.tile([P, KG, P, 4], F32, name="xf", bufs=XF_BUFS, align_bytes=64)
+            bank = give(("x", i, g0))
             for g in range(g0, g1):
                 nc.scalar.activation(
                     out=xf_t[i][:, g].rearrange("p m (u e) -> p m u e", u=2),
-                    in_=xt_t[i, g][:, 2 * g : 2 * g + 2, :].bitcast(BF16).rearrange("p u (m e) -> p m u e", e=2),
+                    in_=bank[:, 2 * g : 2 * g + 2, :].bitcast(BF16).rearrange("p u (m e) -> p m u e", e=2),
                     func=TANH,
                 )
 
-        amp_bank = psum.tile([P, P, 4], F32, name="amp_bank", tag="factor", bufs=1)
-        amp_rows = keep.tile([P, 4 * P], F32, name="amp_rows", align_bytes=64)
-
         def x_amp(i, g0=0, g1=KG):
             if g0 == 0:
-                xb_t[i] = work.tile([P, KG, P, 4], BF16, name="xb", bufs=2, align_bytes=64)
-            if i < 2:
-                factor = amp_col[:, g0:g1, :].unsqueeze(2).to_broadcast([P, g1 - g0, P, 4])
-            else:
-                factor = amp_bank[:].bitcast(BF16).rearrange("p m (g t) -> p g m t", g=KG)[:, g0:g1]
-            nc.vector.tensor_tensor(out=xb_t[i][:, g0:g1], in0=xf_t[i][:, g0:g1], in1=factor, op=ALU.mult)
-
-        def amp_spread():
-            words = amp_col[:].rearrange("p g t -> p (g t)").bitcast(F32)
-            small["amp"] = new_bank()
-            for w in range(4):
-                nc.tensor.transpose(small["amp"][:, w, :], words[:, w : w + 1].to_broadcast([P, P]), ident[:])
-
-        def amp_copy():
-            nc.scalar.copy(out=amp_rows[:], in_=small["amp"][:].rearrange("p w m -> p (w m)"))
-
-        def amp_back():
-            for w in range(4):
-                nc.tensor.transpose(amp_bank[:, :, w], amp_rows[:, P * w : P * (w + 1)], ident[:])
+                xb_t[i] = work.tile([P, KG * P * 4], BF16, name="xb", bufs=2, align_bytes=64)
+            engine, words = (nc.gpsimd, amp_col[:]) if i == 3 else (nc.vector, factors[:, 0:4])
+            factor = words.bitcast(BF16).rearrange("p (g t) -> p g t", g=KG)[:, g0:g1]
+            engine.tensor_tensor(
+                out=xb_t[i][:].rearrange("p (g m t) -> p g m t", g=KG, t=4)[:, g0:g1],
+                in0=xf_t[i][:, g0:g1],
+                in1=factor.unsqueeze(2).to_broadcast([P, g1 - g0, P, 4]),
+                op=ALU.mult,
+            )
 
         def x_quant(i, g0=0, g1=KG):
             if g0 == 0:
@@ -135,15 +151,15 @@ def tile_ftn_residual_turn_s9_kernel(tc, lam, amp, h_words, h_scales, y, v, f, o
             nc.vector.quantize_mx(
                 out=xc_t[i][:, P * g0 : P * g1].bitcast(E4M3X4),
                 scales=xs_t[i][:, P * g0 : P * g1],
-                in_=xb_t[i][:, g0:g1].rearrange("p g m t -> p (g m t)"),
+                in_=xb_t[i][:, 512 * g0 : 512 * g1],
             )
 
         def first(i, b):
-            z_t[i, b] = new_bank()
+            z = take(("z", i, b))
             half, c = divmod(b, 2)
             for g in range(KG):
                 nc.tensor.matmul_mx(
-                    out=z_t[i, b][:].rearrange("p a m -> p (a m)"),
+                    out=z[:].rearrange("p a m -> p (a m)"),
                     lhsT=xc_t[i][:, P * g : P * (g + 1)].bitcast(E4M3X4),
                     lhsT_scale=xs_t[i][:, P * g : P * (g + 1)],
                     rhs=hw[half][:, g, 1024 * c : 1024 * (c + 1)].bitcast(E2M1X4),
@@ -152,20 +168,24 @@ def tile_ftn_residual_turn_s9_kernel(tc, lam, amp, h_words, h_scales, y, v, f, o
                     stop=(g == KG - 1),
                 )
 
+        def t_col(i, b):
+            pair, j = divmod(i, 2)
+            return 512 * (NG * j + b if pair == PAIRS - 1 else 2 * b + j)
+
         def sub(i, b):
-            if i not in t_t:
-                t_t[i] = work.tile([P, N], F32, name="t", bufs=T_BUFS, align_bytes=64)
-            cols = slice(512 * b, 512 * (b + 1))
+            if i // 2 not in t_t:
+                t_t[i // 2] = work.tile([P, 2 * N], F32, name="t", bufs=2, align_bytes=64)
+            c = t_col(i, b)
             nc.vector.tensor_sub(
-                out=t_t[i][:, cols].rearrange("p (u q e) -> p u q e", u=2, e=2),
-                in0=y_t[i][:, cols].rearrange("p (q u e) -> p u q e", u=2, e=2),
-                in1=z_t[i, b][:].rearrange("p a (q u e) -> p u (a q) e", u=2, e=2),
+                out=t_t[i // 2][:, c : c + 512].rearrange("p (u q e) -> p u q e", u=2, e=2),
+                in0=y_t[i][:, 512 * b : 512 * (b + 1)].rearrange("p (q u e) -> p u q e", u=2, e=2),
+                in1=give(("z", i, b))[:].rearrange("p a (q u e) -> p u (a q) e", u=2, e=2),
             )
 
         v_rows = keep.tile([P, NG * 256], F32, name="v_rows", align_bytes=64)
 
         def v_turn(u):
-            bank = small[u] = new_bank()
+            bank = take(("v", u))
             words = v_in[:].bitcast(F32)
             for i in range(4):
                 w = 2 * i + u
@@ -174,109 +194,75 @@ def tile_ftn_residual_turn_s9_kernel(tc, lam, amp, h_words, h_scales, y, v, f, o
         def v_copy(u):
             nc.scalar.copy(
                 out=v_rows[:].rearrange("p (g u q i) -> p g u q i", g=NG, u=2, i=4)[:, :, u],
-                in_=small[u][:].rearrange("p i (g q) -> p g q i", g=NG),
+                in_=give(("v", u))[:].rearrange("p i (g q) -> p g q i", g=NG),
             )
 
-        def weigh(i, c0, c1, space, engine=nc.gpsimd):
-            dst = space[:, space.shape[1] - (c1 - c0) :]
-            for c in range(c0, c1, 256):
-                r_at[i, c // 256] = dst[:, c - c0 : c - c0 + 256]
-            engine.tensor_tensor(out=dst, in0=t_t[i][:, c0:c1], in1=v_rows[:].bitcast(BF16)[:, c0:c1], op=ALU.mult)
+        stage = [keep.tile([P, 2 * N], BF16, name="stage_a", align_bytes=64), keep.tile([P, 2 * N], BF16, name="stage_b", align_bytes=64)]
+        f_words = {}
 
-        def weigh_even(i, g0, g1, space):
-            dst = space[:, space.shape[1] - 256 * (g1 - g0) :]
-            for g in range(g0, g1):
-                r_at[i, 2 * g] = dst[:, 256 * (g - g0) : 256 * (g - g0 + 1)]
-            nc.gpsimd.tensor_tensor(
-                out=dst.rearrange("p (g c) -> p g c", c=256),
-                in0=t_t[i][:].rearrange("p (g u c) -> p g u c", u=2, c=256)[:, g0:g1, 0],
-                in1=v_rows[:].bitcast(BF16).rearrange("p (g u c) -> p g u c", u=2, c=256)[:, g0:g1, 0],
-                op=ALU.mult,
-            )
+        def r_space(i, j, b0):
+            if i == 0:
+                return f_words[0][:] if b0 == 0 else stage[0][:, :N]
+            if i == LAST - 1:
+                return xb_t[LAST if b0 == 0 else LAST - 1][:]
+            if i == LAST:
+                return stage[1][:, 512 * b0 : 512 * b0 + 1024]
+            return stage[i // 2 % 2][:, 1024 * b0 :]
 
-        def odd_turn():
-            small["odd"] = psum.tile([P, P, 4], F32, name="odd_bank", tag="factor", bufs=1)
-            words = v_in[:].bitcast(F32)
-            for i in range(4):
-                w = 2 * i + 1
-                nc.tensor.transpose(small["odd"][:, :, i], words[:, w : w + 1].to_broadcast([P, P]), ident[:])
-
-        def weigh_odd(i, g0, g1):
-            dst = work.tile([P, 512], BF16, name="r_odd", bufs=4, align_bytes=64)
-            for g in range(g0, g1):
-                r_at[i, 2 * g + 1] = dst[:, 256 * (g - g0) : 256 * (g - g0 + 1)]
-            factor = small["odd"][:].rearrange("p q i -> p (q i)").bitcast(BF16)
-            nc.vector.tensor_tensor(
-                out=dst[:, : 256 * (g1 - g0)].rearrange("p (g c) -> p g c", c=256),
-                in0=t_t[i][:].rearrange("p (g u c) -> p g u c", u=2, c=256)[:, g0:g1, 1],
-                in1=factor.rearrange("p (g c) -> p g c", c=256)[:, g0:g1],
-                op=ALU.mult,
-            )
+        def weigh(i, j, b0, b1):
+            tiles, groups = j - i, b1 - b0
+            width = 512 * tiles * groups
+            dst = r_space(i, j, b0)[:, :width]
+            for b in range(b0, b1):
+                for a in range(tiles):
+                    c = 512 * (tiles * (b - b0) + a)
+                    r_at[i + a, b] = dst[:, c : c + 512]
+            by_vector = b1 == NG and i > 0
+            if by_vector:
+                engine, rows = nc.vector, factors[:].bitcast(BF16)[:, 512 * (b0 - 2) :]
+            else:
+                engine, rows = nc.gpsimd, v_rows[:].bitcast(BF16)[:, 512 * b0 : 512 * b1]
+            c = t_col(i, b0)
+            src = t_t[i // 2][:, c : c + width]
+            if tiles > 1:
+                rows = rows.rearrange("p (g c) -> p g c", c=512).unsqueeze(2).to_broadcast([P, groups, tiles, 512])
+                src = src.rearrange("p (g a c) -> p g a c", a=tiles, c=512)
+                dst = dst.rearrange("p (g a c) -> p g a c", a=tiles, c=512)
+            engine.tensor_tensor(out=dst, in0=src, in1=rows, op=ALU.mult)
 
         def r_turn(i, half):
-            rt_t[i, half] = new_bank()
-            for j in range(r_blocks(i, half)):
-                nc.tensor.transpose(rt_t[i, half][:, j, :], r_at[i, 4 * half + j].bitcast(F32), ident[:])
+            bank = take(("r", i, half))
+            for a in range(4):
+                g, u = divmod(a, 2)
+                nc.tensor.transpose(bank[:, a, :], r_at[i, 2 * half + g][:, 256 * u : 256 * (u + 1)].bitcast(F32), ident[:])
 
-        def r_blocks(i, half):
-            return 2 if i < EARLY and half == 1 else 4
-
-        def r_tile(i):
-            if i not in rg_t:
-                rg_t[i] = work.tile([P, 1024], F32, name="rg", bufs=3, align_bytes=64)
-            return rg_t[i]
+        def r_words(i, half):
+            pair, j = divmod(i, 2)
+            slot = 3 - (2 * half + j if pair < PAIRS - 1 else 2 * j + half)
+            return stage[(pair + 1) % 2][:, 1024 * slot : 1024 * (slot + 1)]
 
         def r_copy(i, half):
-            count = r_blocks(i, half)
             nc.scalar.copy(
-                out=r_tile(i)[:, 512 * half : 512 * half + P * count].rearrange("p (g m u) -> p g m u", m=P, u=2),
-                in_=rt_t[i, half][:, :count].rearrange("p (g u) m -> p g m u", u=2),
+                out=r_words(i, half).bitcast(F32).rearrange("p (g m u) -> p g m u", m=P, u=2),
+                in_=give(("r", i, half))[:].rearrange("p (g u) m -> p g m u", u=2),
             )
 
-        v_col = keep.tile([P, 2], F32, name="v_col", align_bytes=64)
-
-        def v_back():
-            small["col"] = new_bank()
-            for u in range(2):
-                c = 256 * (NG - 1) + P * u
-                nc.tensor.transpose(small["col"][:, u, :], v_rows[:, c : c + P], ident[:])
-
-        def v_col_copy():
-            nc.scalar.copy(out=v_col[:], in_=small["col"][:, 0:2, 0])
-
-        def t_turn(i):
-            rt_t[i, "t"] = new_bank()
-            for t in range(4):
-                u, e = divmod(t, 2)
-                c = 512 * (NG - 1) + 256 * u + e
-                nc.tensor.transpose(rt_t[i, "t"][:, t, :], t_t[i][:, c : c + 255 : 2], ident[:])
-
-        def t_weigh(i):
-            nc.vector.tensor_tensor(
-                out=r_tile(i)[:, 256 * (NG - 1) :].bitcast(BF16).rearrange("p (m t) -> p m t", t=4),
-                in0=rt_t[i, "t"][:].rearrange("p t m -> p m t"),
-                in1=v_col[:].bitcast(BF16).unsqueeze(1).to_broadcast([P, P, 4]),
-                op=ALU.mult,
-            )
-
-        def r_quant(i, h0=0, h1=2):
-            if h0 == 0:
-                rc_t[i] = work.tile([P, NG * P], U32, name="rc", bufs=5, align_bytes=64)
-                rs_t[i] = work.tile([P, NG * P], U8, name="rs", bufs=5, align_bytes=64)
+        def r_quant(i, half):
+            if half == 0:
+                rc_t[i] = work.tile([P, NG * P], U32, name="rc", bufs=4, align_bytes=64)
+                rs_t[i] = work.tile([P, NG * P], U8, name="rs", bufs=4, align_bytes=64)
             nc.vector.quantize_mx(
-                out=rc_t[i][:, 256 * h0 : 256 * h1].bitcast(E5M2X4),
-                scales=rs_t[i][:, 256 * h0 : 256 * h1],
-                in_=rg_t[i][:, 512 * h0 : 512 * h1].bitcast(BF16),
+                out=rc_t[i][:, 256 * half : 256 * (half + 1)].bitcast(E5M2X4),
+                scales=rs_t[i][:, 256 * half : 256 * (half + 1)],
+                in_=r_words(i, half),
             )
 
-        f_words = {}
         f_codes = keep.tile([P, 2 * NG * 512], U32, name="f_codes", align_bytes=64)
         f_scales = keep.tile([P, 2 * NG * 512], U8, name="f_scales", align_bytes=64)
 
-        def f_copy(piece):
-            c, q = divmod(piece, 2)
+        def f_copy(c, q):
             if q == 0:
-                f_words[c] = work.tile([P, 2048], BF16, name="f_words", bufs=4, align_bytes=64)
+                f_words[c] = work.tile([P, 2048], BF16, name="f_words", bufs=F_BUFS, align_bytes=64)
             nc.scalar.copy(
                 out=f_words[c][:, 1024 * q : 1024 * (q + 1)].rearrange("p (c i t) -> p c t i", i=4, t=4),
                 in_=f_raw[c][:, :, 256 * q : 256 * (q + 1)].rearrange("p t (c i) -> p c t i", i=4),
@@ -289,11 +275,11 @@ def tile_ftn_residual_turn_s9_kernel(tc, lam, amp, h_words, h_scales, y, v, f, o
                 in_=f_words[c][:],
             )
 
-        def second(i, kh):
-            d_t[i, kh] = new_bank()
-            for g in range(NG):
+        def second(i, kh, h0=0, h1=2):
+            d = take(("d", i, kh)) if h0 == 0 else bank_of["d", i, kh][1]
+            for g in range(2 * h0, 2 * h1):
                 nc.tensor.matmul_mx(
-                    out=d_t[i, kh][:].rearrange("p a m -> p (a m)"),
+                    out=d[:].rearrange("p a m -> p (a m)"),
                     lhsT=rc_t[i][:, P * g : P * (g + 1)].bitcast(E5M2X4),
                     lhsT_scale=rs_t[i][:, P * g : P * (g + 1)],
                     rhs=f_codes[:, 512 * (NG * kh + g) : 512 * (NG * kh + g + 1)].bitcast(E4M3X4),
@@ -305,162 +291,131 @@ def tile_ftn_residual_turn_s9_kernel(tc, lam, amp, h_words, h_scales, y, v, f, o
         def add(i, kh):
             parts = 2 if (i, kh) == (LAST, 1) else 1
             width = 512 // parts
-            d = d_t[i, kh][:].rearrange("p a m -> p (a m)")
+            d = give(("d", i, kh))[:].rearrange("p a m -> p (a m)")
             for c in range(parts):
                 o = work.tile([P, width], F32, name="o", bufs=6, align_bytes=64)
                 cols = slice(512 * kh + width * c, 512 * kh + width * (c + 1))
                 nc.vector.tensor_add(out=o[:], in0=d[:, width * c : width * (c + 1)], in1=lam_t[i][:, cols])
                 nc.sync.dma_start(out=out[P * i : P * (i + 1), cols], in_=o[:])
 
-        load_lam(0, 2)
-        nc.scalar.dma_start(out=amp_col[:], in_=amp.rearrange("(g p t) -> p g t", g=KG, t=4))
         nc.scalar.dma_start(out=v_in[:], in_=v.rearrange("(q c) -> q c", c=16))
-        load_lam(1)
-        load_scales(0, N)
-        load_lam(2)
+        load_v_col(3, nc.scalar)
+        load_lam(0, 2)
+        nc.sync.dma_start(out=amp_rows[0:KG, :].bitcast(BF16), in_=amp.rearrange("(g c) -> g c", g=KG))
+        for i in range(1, 4):
+            load_lam(i)
+        load_scales()
         load_h(0)
         load_f(0)
-        load_h(1)
         load_y(0, 0, 1)
-        load_y(0, 1, 2)
-        load_lam(3)
         load_y(1, 0, 1)
+        load_lam(4)
+        load_lam(5)
+        load_h(1)
         load_f(1)
+        load_y(0, 1, 2)
         load_y(1, 1, 2)
-        for i in range(2, TILES):
-            if i + 2 < TILES:
-                load_lam(i + 2)
-            load_f(i)
-            load_y(i)
+        load_f(2)
+        load_y(2, 0, 1)
+        load_y(3, 0, 1)
+        load_f(3)
+        load_y(2, 1, 2)
+        load_y(3, 1, 2)
+        load_lam(6)
+        load_f(4)
+        load_y(4, 0, 1)
+        load_f(5)
+        load_y(5, 0, 1)
+        load_y(4, 1, 2)
+        load_f(6)
+        load_y(5, 1, 2)
+        load_f(7)
+        load_lam(7)
+        load_y(6)
+        load_y(7)
+        load_v_col(2, nc.sync)
 
-        def weigh_tile(i):
-            if i == 4:
-                space = f_words[2 * NG - 1][:]
-            elif i == LAST - 1:
-                space = y_t[LAST][:, : N // 2]
-            elif i == LAST:
-                space = rg_t[LAST - 2][:].bitcast(BF16)
-            else:
-                r = work.tile([P, N], BF16, name="r", bufs=2, align_bytes=64)
-                space = r[:]
-            if i >= LAST - 1:
-                weigh_even(i, 0, NG, space)
-            else:
-                weigh(i, 0, N - 512 if i < EARLY else N, space)
+        def halves(call, i):
+            return [(call, i, 0), (call, i, 1)]
 
-        def blocks_of(i):
-            return [(sub, i, b) for b in ((0, 1, 3, 2) if i < EARLY else range(NG))]
+        def left(call, i):
+            return [(call, i, 0), (call, i, 1), (call, i + 1, 0), (call, i + 1, 1)]
 
-        def product(step):
-            return (first if step[0] == sub else second, *step[1:])
+        def right(call, i):
+            return [(call, i, 2), (call, i + 1, 2), (call, i, 3), (call, i + 1, 3)]
 
-        vector = [(x_amp, 0, 0, 1), (x_amp, 0, 1, 2), (x_quant, 0, 0, 1), (x_quant, 0, 1, 2), (x_amp, 1), (x_quant, 1), (x_amp, 2)]
-        s = blocks_of(0)
-        vector.extend([s[0], (x_quant, 2), s[1], (f_quant, 0), s[2], s[3], (weigh_tile, 0)])
-        tensor = [(x_turn, 0, 0, 1), (x_turn, 0, 1, 2), (amp_spread,), (x_turn, 1), (v_turn, 0), (v_turn, 1), (x_turn, 2), (amp_back,)]
-        scalar = [(x_tanh, 0, 0, 1), (x_tanh, 0, 1, 2), (amp_copy,), (x_tanh, 1), (v_copy, 0), (v_copy, 1), (x_tanh, 2), (f_copy, 0), (f_copy, 1)]
-        runs, piece = [s], 1
-        for j in range(1, LAST - 1):
-            own = blocks_of(j)[max(0, j - 3) :]
-            subs = own[:-1] + blocks_of(j + 1)[: max(0, j - 2)] + own[-1:]
-            extra = (t_weigh, j - 1) if j - 1 < EARLY else (add, j - 3, 0)
-            runs.append(subs[:2] + [(x_amp, j + 2), subs[2], extra] + subs[3:])
-            end = min(piece + 1 if j % 2 else NG * j // 2, 2 * NG)
-            vector.extend(runs[j] + [(x_quant, j + 2)] + [(r_quant, j - 2)][: j // 2])
-            vector.extend([(f_quant, c) for c in range(piece, end)] + [(weigh_tile, j)])
-            piece = end
-        a, b = LAST - 1, LAST
-        runs.append([(add, 0, 1), (add, 1, 1), (add, 2, 1), (sub, a, 3), (weigh_odd, a, 0, 2), (sub, b, 0), (weigh_odd, a, 2, 4), (sub, b, 1)])
-        runs.append([(add, 3, 0), (sub, b, 2), (add, 3, 1), (sub, b, 3)])
-        vector.extend(runs[a] + [(r_quant, a - 2), (weigh_tile, a)] + runs[b] + [(r_quant, b - 2), (weigh_tile, b)])
-        vector.extend([(weigh_odd, b, 0, 2), (add, 4, 0), (weigh_odd, b, 2, 4), (add, 4, 1)])
-        vector.extend([(r_quant, a), (add, 5, 0), (add, 5, 1), (r_quant, b), (add, a, 0), (add, a, 1), (add, b, 0), (add, b, 1)])
+        def across(call, i):
+            return [(call, i, 0), (call, i + 1, 0), (call, i, 1), (call, i + 1, 1)]
 
-        def products(run):
-            return [product(x) for x in run if x[0] in (sub, add)]
+        vector = [(x_amp, 0, 0, 1), (x_amp, 0, 1, 2), (x_quant, 0, 0, 1), (x_quant, 0, 1, 2), (amp_copy,), (x_amp, 1), (x_amp, 2), (x_quant, 1), (x_quant, 2), (x_amp, 3)]
+        vector.extend(left(sub, 0) + [(x_quant, 3), (f_quant, 0), (weigh, 0, 2, 0, 2)])
+        vector.extend([(x_amp, 4)] + right(sub, 0) + [(weigh, 0, 2, 2, 4), (x_amp, 5)] + left(sub, 2) + right(sub, 2))
+        vector.extend([(x_quant, 4), (x_quant, 5), (f_quant, 1), (f_quant, 2), (f_quant, 3)] + across(r_quant, 0) + [(weigh, 2, 4, 0, 2), (weigh, 2, 4, 2, 3)])
+        vector.extend([(sub, 4, 0), (weigh, 2, 4, 3, 4), (sub, 4, 1), (add, 0, 0), (sub, 5, 0), (x_amp, 6), (sub, 5, 1)] + right(sub, 4))
+        vector.extend([(x_quant, 6), (f_quant, 4), (f_quant, 5), (f_quant, 6)] + across(r_quant, 2)[:2] + [(f_quant, 7)] + across(r_quant, 2)[2:])
+        vector.extend([(weigh, 4, 6, 0, 2), (weigh, 4, 6, 2, 3)])
+        vector.extend([(add, 1, 0), (sub, 6, 0), (add, 0, 1), (x_amp, 7), (add, 1, 1), (weigh, 4, 6, 3, 4), (sub, 6, 1), (sub, 6, 2), (add, 2, 0), (sub, 6, 3), (add, 2, 1)])
+        vector.extend([(x_quant, 7), (weigh, 6, 7, 0, 2), (add, 3, 0), (weigh, 6, 7, 2, 4), (add, 3, 1), (sub, 7, 0), (sub, 7, 1)])
+        vector.extend(across(r_quant, 4) + [(weigh, 7, 8, 0, 2), (sub, 7, 2), (sub, 7, 3), (add, 4, 0), (weigh, 7, 8, 2, 4)])
+        vector.extend(halves(r_quant, 6) + [(add, 4, 1), (add, 5, 0)] + halves(r_quant, 7) + [(add, 5, 1)] + left(add, 6))
 
-        done = 0
-        for j in range(LAST - 1):
-            tensor.extend(products(runs[j])[done:])
-            if j + 3 < TILES:
-                tensor.append((x_turn, j + 3))
-            if j == 0:
-                tensor.append((v_back,))
-            ahead = [x for x in products(runs[j + 1])[: 2 if j < LAST - 2 else 3] if x[1] <= j + 1]
-            done = len(ahead)
-            tensor.extend(ahead)
-            if j == LAST - 2:
-                tensor.append((odd_turn,))
-            if j > 0:
-                tensor.extend([(r_turn, j - 1, 0), (r_turn, j - 1, 1)])
-            if j < EARLY:
-                tensor.append((t_turn, j))
-        rest = products(runs[a])[done:] + products(runs[b])
-        tensor.extend(rest[:-1] + [(r_turn, a - 1, 0), (r_turn, a - 1, 1)] + rest[-1:])
-        for i in range(4, TILES):
-            tensor.extend([(second, i, 0), (second, i, 1)])
-            if i + 2 < TILES:
-                tensor.extend([(r_turn, i + 2, 0), (r_turn, i + 2, 1)])
+        tensor = [(x_turn, 0, 0, 1), (x_turn, 0, 1, 2), (amp_turn,), (v_col_turn, 3), (x_turn, 1), (x_turn, 2), (v_turn, 0), (x_turn, 3), (v_turn, 1)]
+        tensor.extend(left(first, 0) + [(x_turn, 4), (x_turn, 5)] + right(first, 0) + left(first, 2) + across(r_turn, 0)[:2] + right(first, 2))
+        tensor.extend([(x_turn, 6)] + across(r_turn, 0)[2:] + halves(first, 4) + [(second, 0, 0)] + halves(first, 5) + right(first, 4)[:2])
+        tensor.extend([(x_turn, 7)] + right(first, 4)[2:] + across(r_turn, 2)[:2] + [(second, 1, 0)] + across(r_turn, 2)[2:] + [(first, 6, 0)])
+        tensor.extend([(second, 0, 1, 0, 1), (second, 1, 1, 0, 1), (second, 0, 1, 1, 2), (second, 1, 1, 1, 2)])
+        tensor.extend([(first, 6, 1), (first, 6, 2), (second, 2, 0), (first, 6, 3), (second, 2, 1), (second, 3, 0), (v_col_turn, 2)] + across(r_turn, 4)[:2])
+        tensor.extend([(second, 3, 1)] + across(r_turn, 4)[2:] + [(first, 7, b) for b in range(NG)] + halves(r_turn, 6))
+        tensor.extend(left(second, 4)[:3] + halves(r_turn, 7) + [(second, 5, 1)] + left(second, 6))
 
-        def pieces(c0, c1):
-            return [(f_copy, q) for q in range(2 * c0, 2 * c1)]
+        scalar = [(x_tanh, 0, 0, 1), (x_tanh, 0, 1, 2), (x_tanh, 1), (x_tanh, 2), (v_copy, 0), (x_tanh, 3)] + halves(f_copy, 0)
+        scalar.extend([(v_copy, 1), (x_tanh, 4), (x_tanh, 5)] + left(f_copy, 1) + across(r_copy, 0)[:2] + halves(f_copy, 3))
+        scalar.extend([(x_tanh, 6)] + across(r_copy, 0)[2:] + left(f_copy, 4) + halves(f_copy, 6) + across(r_copy, 2)[:2] + halves(f_copy, 7) + across(r_copy, 2)[2:])
+        scalar.extend([(x_tanh, 7)] + across(r_copy, 4) + left(r_copy, 6))
 
-        def copies(i):
-            return [(r_copy, i, 0), (r_copy, i, 1)]
-
-        scalar.extend([(x_tanh, 3), (v_col_copy,)] + pieces(1, 2) + [(x_tanh, 4)] + pieces(2, 3) + copies(0) + pieces(3, 4))
-        for j in range(2, LAST - 2):
-            scalar.extend([(x_tanh, j + 3)] + copies(j - 1) + pieces(2 * j, min(2 * j + 2, 2 * NG)))
-        for i in range(4, TILES):
-            scalar.extend(copies(i))
-
-        def weighed(i):
-            return [(weigh_tile, i)] + [(weigh_odd, i, g, g + 2) for g in (0, 2) if i >= LAST - 1]
+        windows = [x for x in vector if x[0] == weigh]
 
         def needs(step):
             call, i = step[0], step[1] if len(step) > 1 else 0
-            table = {
-                x_tanh: [(x_turn, *step[1:])] + [(x_amp, k) if k else (x_amp, 0, 1, 2) for k in (i - XF_BUFS,) if k >= 0],
-                x_amp: [(x_tanh, *step[1:])] + [(amp_back,)][: i // 2],
-                amp_copy: [(amp_spread,)],
-                amp_back: [(amp_copy,)],
-                v_copy: [(v_turn, i)],
-                v_back: [(v_copy, 0), (v_copy, 1)],
-                v_col_copy: [(v_back,)],
-                odd_turn: [(x_amp, LAST)],
-                weigh_odd: [(odd_turn,)],
-                weigh_tile: [(v_copy, 1)] + [(r_turn, k, 1) for k in (i - 2,) if k >= 0],
-                first: [(x_quant, i) if i else (x_quant, 0, 1, 2)],
-                sub: [(first, *step[1:])],
-                t_turn: [(sub, i, NG - 1)],
-                t_weigh: [(t_turn, i), (v_col_copy,)],
-                r_turn: weighed(i),
-                r_copy: [(r_turn, *step[1:])] + [(r_quant, k) for k in (i - 3,) if k >= 0],
-                r_quant: copies(i),
-                f_copy: [(f_quant, k) for k in (i // 2 - 4,) if k >= 0],
-                f_quant: pieces(i, i + 1),
-                second: [(r_quant, i), (f_quant, NG - 1 if step[-1] == 0 else 2 * NG - 1)],
-                add: [(second, *step[1:])],
-            }
-            return table.get(call, [])
+            if call == x_tanh:
+                return [(x_turn, *step[1:])] + [(x_amp, k) if k else (x_amp, 0, 1, 2) for k in (i - XF_BUFS,) if k >= 0]
+            if call == x_amp:
+                return [(x_tanh, *step[1:]), (v_col_turn, 3)]
+            if call == first:
+                return [(x_quant, i) if i else (x_quant, 0, 1, 2)]
+            if call == weigh:
+                return [(v_copy, 1)] + [(v_col_turn, 2)][: i // (LAST - 1)]
+            if call == v_col_turn:
+                return [(x_amp, LAST), (weigh, 4, 6, 3, 4)] if i == 2 else []
+            if call == r_turn:
+                return [w for w in windows if w[1] <= i < w[2] and w[3] < 2 * step[2] + 2 and w[4] > 2 * step[2]]
+            if call == f_copy:
+                return [(f_quant, i - F_BUFS)] + across(r_turn, 0)[:2] if i >= F_BUFS else []
+            if call == f_quant:
+                return halves(f_copy, i)
+            if call == second:
+                h = step[4] - 1 if len(step) > 3 else 1
+                return [(r_quant, i, h), (f_quant, NG * step[2] + 2 * h + 1)]
+            if call == add:
+                return [x for x in tensor_all if x[:3] == (second, *step[1:])]
+            producer = {sub: first, v_copy: v_turn, r_copy: r_turn, r_quant: r_copy}
+            return [(producer[call], *step[1:])] if call in producer else []
 
-        reader = {x_turn: x_tanh, amp_spread: amp_copy, v_turn: v_copy, v_back: v_col_copy, first: sub, second: add,
-                  r_turn: r_copy, t_turn: t_weigh}
-        written, banks = set(), []
-        queues = [tensor, scalar, vector]
-        while any(queues):
-            moved = False
-            for queue in queues:
-                while queue:
-                    step = queue[0]
-                    wanted = needs(step)
-                    if step[0] in reader and len(banks) >= BANKS:
-                        wanted = wanted + [banks[-BANKS]]
-                    if not all(x in written for x in wanted):
-                        break
-                    if step[0] in reader:
-                        banks.append((reader[step[0]], *step[1:]))
-                    step[0](*step[1:])
-                    written.add(queue.pop(0))
-                    moved = True
-            assert moved
+        tensor_all = list(tensor)
+        queue_of = {}
+        for queue in (tensor, scalar, vector):
+            for step in queue:
+                queue_of[step] = queue
+        written = set()
+
+        def write(step):
+            queue = queue_of[step]
+            while step not in written:
+                head = queue[0]
+                for other in needs(head):
+                    write(other)
+                head[0](*head[1:])
+                written.add(queue.pop(0))
+
+        for step in list(vector):
+            write(step)

@@ -275,28 +275,31 @@ def tile_ftn_residual_turn_s9_kernel(tc, lam, amp, h_words, h_scales, y, v, f, o
                 in_=f_words[c][:],
             )
 
-        def second(i, kh, h0=0, h1=2):
-            d = take(("d", i, kh)) if h0 == 0 else bank_of["d", i, kh][1]
+        def second(i, c0, c1=None, h0=0, h1=2):
+            c0, c1 = (2 * c0, 2 * c0 + 2) if c1 is None else (c0, c1)
+            d = take(("d", i, c0)) if h0 == 0 else bank_of["d", i, c0][1]
+            kh, q = divmod(c0, 2)
+            width = 256 * (c1 - c0)
             for g in range(2 * h0, 2 * h1):
+                c = 512 * (NG * kh + g) + 256 * q
                 nc.tensor.matmul_mx(
-                    out=d[:].rearrange("p a m -> p (a m)"),
+                    out=d[:].rearrange("p a m -> p (a m)")[:, :width],
                     lhsT=rc_t[i][:, P * g : P * (g + 1)].bitcast(E5M2X4),
                     lhsT_scale=rs_t[i][:, P * g : P * (g + 1)],
-                    rhs=f_codes[:, 512 * (NG * kh + g) : 512 * (NG * kh + g + 1)].bitcast(E4M3X4),
-                    rhs_scale=f_scales[:, 512 * (NG * kh + g) : 512 * (NG * kh + g + 1)],
+                    rhs=f_codes[:, c : c + width].bitcast(E4M3X4),
+                    rhs_scale=f_scales[:, c : c + width],
                     start=(g == 0),
                     stop=(g == NG - 1),
                 )
 
-        def add(i, kh):
-            parts = 2 if (i, kh) == (LAST, 1) else 1
-            width = 512 // parts
-            d = give(("d", i, kh))[:].rearrange("p a m -> p (a m)")
-            for c in range(parts):
-                o = work.tile([P, width], F32, name="o", bufs=6, align_bytes=64)
-                cols = slice(512 * kh + width * c, 512 * kh + width * (c + 1))
-                nc.vector.tensor_add(out=o[:], in0=d[:, width * c : width * (c + 1)], in1=lam_t[i][:, cols])
-                nc.sync.dma_start(out=out[P * i : P * (i + 1), cols], in_=o[:])
+        def add(i, c0, c1=None):
+            c0, c1 = (2 * c0, 2 * c0 + 2) if c1 is None else (c0, c1)
+            width = 256 * (c1 - c0)
+            d = give(("d", i, c0))[:].rearrange("p a m -> p (a m)")
+            o = work.tile([P, width], F32, name="o", bufs=6, align_bytes=64)
+            cols = slice(256 * c0, 256 * c1)
+            nc.vector.tensor_add(out=o[:], in0=d[:, :width], in1=lam_t[i][:, cols])
+            nc.sync.dma_start(out=out[P * i : P * (i + 1), cols], in_=o[:])
 
         nc.scalar.dma_start(out=v_in[:], in_=v.rearrange("(q c) -> q c", c=16))
         load_v_col(3, nc.scalar)
@@ -305,32 +308,24 @@ def tile_ftn_residual_turn_s9_kernel(tc, lam, amp, h_words, h_scales, y, v, f, o
         for i in range(1, 4):
             load_lam(i)
         load_scales()
-        load_h(0)
-        load_f(0)
-        load_y(0, 0, 1)
-        load_y(1, 0, 1)
-        load_lam(4)
-        load_lam(5)
-        load_h(1)
-        load_f(1)
-        load_y(0, 1, 2)
-        load_y(1, 1, 2)
-        load_f(2)
-        load_y(2, 0, 1)
-        load_y(3, 0, 1)
-        load_f(3)
-        load_y(2, 1, 2)
-        load_y(3, 1, 2)
-        load_lam(6)
-        load_f(4)
-        load_y(4, 0, 1)
-        load_f(5)
-        load_y(5, 0, 1)
-        load_y(4, 1, 2)
-        load_f(6)
-        load_y(5, 1, 2)
-        load_f(7)
-        load_lam(7)
+        for half in range(2):
+            load_h(half)
+            load_f(half)
+            load_y(0, half, half + 1)
+            load_y(1, half, half + 1)
+            if half == 0:
+                load_lam(4)
+                load_lam(5)
+        for half in range(2):
+            load_f(2 + half)
+            load_y(2, half, half + 1)
+            load_y(3, half, half + 1)
+        for half in range(2):
+            load_lam(6 + half)
+            load_f(4 + 2 * half)
+            load_y(4, half, half + 1)
+            load_y(5, half, half + 1)
+            load_f(5 + 2 * half)
         load_y(6)
         load_y(7)
         load_v_col(2, nc.sync)
@@ -352,25 +347,27 @@ def tile_ftn_residual_turn_s9_kernel(tc, lam, amp, h_words, h_scales, y, v, f, o
         vector.extend([(x_amp, 4)] + right(sub, 0) + [(weigh, 0, 2, 2, 4), (x_amp, 5)] + left(sub, 2) + right(sub, 2))
         vector.extend([(x_quant, 4), (x_quant, 5), (f_quant, 1), (f_quant, 2), (f_quant, 3)] + across(r_quant, 0) + [(weigh, 2, 4, 0, 2), (weigh, 2, 4, 2, 3)])
         vector.extend([(sub, 4, 0), (weigh, 2, 4, 3, 4), (sub, 4, 1), (add, 0, 0), (sub, 5, 0), (x_amp, 6), (sub, 5, 1)] + right(sub, 4))
-        vector.extend([(x_quant, 6), (f_quant, 4), (f_quant, 5), (f_quant, 6)] + across(r_quant, 2)[:2] + [(f_quant, 7)] + across(r_quant, 2)[2:])
+        vector.extend([(x_quant, 6)] + [(f_quant, c) for c in range(NG, 2 * NG)] + across(r_quant, 2))
         vector.extend([(weigh, 4, 6, 0, 2), (weigh, 4, 6, 2, 3)])
-        vector.extend([(add, 1, 0), (sub, 6, 0), (add, 0, 1), (x_amp, 7), (add, 1, 1), (weigh, 4, 6, 3, 4), (sub, 6, 1), (sub, 6, 2), (add, 2, 0), (sub, 6, 3), (add, 2, 1)])
-        vector.extend([(x_quant, 7), (weigh, 6, 7, 0, 2), (add, 3, 0), (weigh, 6, 7, 2, 4), (add, 3, 1), (sub, 7, 0), (sub, 7, 1)])
-        vector.extend(across(r_quant, 4) + [(weigh, 7, 8, 0, 2), (sub, 7, 2), (sub, 7, 3), (add, 4, 0), (weigh, 7, 8, 2, 4)])
-        vector.extend(halves(r_quant, 6) + [(add, 4, 1), (add, 5, 0)] + halves(r_quant, 7) + [(add, 5, 1)] + left(add, 6))
+        vector.extend([(add, 1, 0), (sub, 6, 0), (add, 0, 2, 4), (x_amp, 7), (add, 1, 2, 4), (weigh, 4, 6, 3, 4), (sub, 6, 1), (sub, 6, 2), (add, 2, 0), (sub, 6, 3), (add, 2, 1)])
+        vector.extend([(x_quant, 7), (weigh, 6, 7, 0, 2), (add, 3, 0), (weigh, 6, 7, 2, 4), (sub, 7, 0), (sub, 7, 1)])
+        vector.extend(across(r_quant, 4) + [(weigh, 7, 8, 0, 2), (sub, 7, 2), (sub, 7, 3), (add, 3, 1), (weigh, 7, 8, 2, 4)])
+        vector.extend(halves(r_quant, 6) + [(add, 4, 0), (add, 4, 1), (r_quant, 7, 0), (add, 5, 0), (r_quant, 7, 1), (add, 5, 1)] + left(add, 6)[:3])
+        vector.extend([(add, LAST, 2, 3), (add, LAST, 3, 4)])
 
         tensor = [(x_turn, 0, 0, 1), (x_turn, 0, 1, 2), (amp_turn,), (v_col_turn, 3), (x_turn, 1), (x_turn, 2), (v_turn, 0), (x_turn, 3), (v_turn, 1)]
         tensor.extend(left(first, 0) + [(x_turn, 4), (x_turn, 5)] + right(first, 0) + left(first, 2) + across(r_turn, 0)[:2] + right(first, 2))
-        tensor.extend([(x_turn, 6)] + across(r_turn, 0)[2:] + halves(first, 4) + [(second, 0, 0)] + halves(first, 5) + right(first, 4)[:2])
-        tensor.extend([(x_turn, 7)] + right(first, 4)[2:] + across(r_turn, 2)[:2] + [(second, 1, 0)] + across(r_turn, 2)[2:] + [(first, 6, 0)])
-        tensor.extend([(second, 0, 1, 0, 1), (second, 1, 1, 0, 1), (second, 0, 1, 1, 2), (second, 1, 1, 1, 2)])
+        tensor.extend(across(r_turn, 0)[2:] + [(x_turn, 6)] + halves(first, 4) + [(second, 0, 0)] + halves(first, 5) + right(first, 4)[:2])
+        tensor.extend([(x_turn, 7)] + right(first, 4)[2:])
+        tensor.extend(across(r_turn, 2)[:2] + [(second, 1, 0)] + across(r_turn, 2)[2:] + [(first, 6, 0)])
+        tensor.extend([(second, i, 2, 4, h, h + 1) for h in range(2) for i in range(2)])
         tensor.extend([(first, 6, 1), (first, 6, 2), (second, 2, 0), (first, 6, 3), (second, 2, 1), (second, 3, 0), (v_col_turn, 2)] + across(r_turn, 4)[:2])
         tensor.extend([(second, 3, 1)] + across(r_turn, 4)[2:] + [(first, 7, b) for b in range(NG)] + halves(r_turn, 6))
-        tensor.extend(left(second, 4)[:3] + halves(r_turn, 7) + [(second, 5, 1)] + left(second, 6))
+        tensor.extend(left(second, 4)[:3] + halves(r_turn, 7) + [(second, 5, 1)] + left(second, 6)[:3] + [(second, LAST, 2, 3), (second, LAST, 3, 4)])
 
-        scalar = [(x_tanh, 0, 0, 1), (x_tanh, 0, 1, 2), (x_tanh, 1), (x_tanh, 2), (v_copy, 0), (x_tanh, 3)] + halves(f_copy, 0)
-        scalar.extend([(v_copy, 1), (x_tanh, 4), (x_tanh, 5)] + left(f_copy, 1) + across(r_copy, 0)[:2] + halves(f_copy, 3))
-        scalar.extend([(x_tanh, 6)] + across(r_copy, 0)[2:] + left(f_copy, 4) + halves(f_copy, 6) + across(r_copy, 2)[:2] + halves(f_copy, 7) + across(r_copy, 2)[2:])
+        scalar = [(x_tanh, 0, 0, 1), (x_tanh, 0, 1, 2), (x_tanh, 1), (x_tanh, 2), (v_copy, 0), (x_tanh, 3), (v_copy, 1)] + halves(f_copy, 0)
+        scalar.extend([(x_tanh, 4), (x_tanh, 5)] + left(f_copy, 1) + across(r_copy, 0)[:2] + halves(f_copy, 3))
+        scalar.extend(across(r_copy, 0)[2:] + [(x_tanh, 6)] + left(f_copy, 4) + left(f_copy, 6)[:3] + across(r_copy, 2)[:2] + [(f_copy, 7, 1)] + across(r_copy, 2)[2:])
         scalar.extend([(x_tanh, 7)] + across(r_copy, 4) + left(r_copy, 6))
 
         windows = [x for x in vector if x[0] == weigh]
@@ -394,10 +391,11 @@ def tile_ftn_residual_turn_s9_kernel(tc, lam, amp, h_words, h_scales, y, v, f, o
             if call == f_quant:
                 return halves(f_copy, i)
             if call == second:
-                h = step[4] - 1 if len(step) > 3 else 1
-                return [(r_quant, i, h), (f_quant, NG * step[2] + 2 * h + 1)]
+                h = step[5] - 1 if len(step) > 4 else 1
+                kh = step[2] // 2 if len(step) > 3 else step[2]
+                return [(r_quant, i, h), (f_quant, NG * kh + 2 * h + 1)]
             if call == add:
-                return [x for x in tensor_all if x[:3] == (second, *step[1:])]
+                return [x for x in tensor_all if x[: len(step)] == (second, *step[1:])]
             producer = {sub: first, v_copy: v_turn, r_copy: r_turn, r_quant: r_copy}
             return [(producer[call], *step[1:])] if call in producer else []
 
@@ -414,8 +412,11 @@ def tile_ftn_residual_turn_s9_kernel(tc, lam, amp, h_words, h_scales, y, v, f, o
                 head = queue[0]
                 for other in needs(head):
                     write(other)
-                head[0](*head[1:])
-                written.add(queue.pop(0))
+                if head not in written:
+                    head[0](*head[1:])
+                    written.add(queue.pop(0))
+                if scalar and all(other in written for other in needs(scalar[0])):
+                    write(scalar[0])
 
         for step in list(vector):
             write(step)

@@ -84,7 +84,11 @@ def tile_ftn_residual_turn_s9_kernel(tc, lam, amp, h_words, h_scales, y, v, f, o
             v_col[g] = work.tile([P, 4], BF16, name="v_col", bufs=2, align_bytes=64)
             queue.dma_start(out=v_col[g][:], in_=v[512 * g : 512 * (g + 1)].rearrange("(q c) -> q c", c=4))
 
-        xf_t, xb_t, xc_t, xs_t = {}, {}, {}, {}
+        xf_t = {}
+        xb_two = keep.tile([P, 2 * K], BF16, name="xb_two", align_bytes=64)
+        xb_one = keep.tile([P, K], BF16, name="xb_one", align_bytes=64)
+        x_codes = keep.tile([P, TILES * KG * P], U32, name="x_codes", align_bytes=64)
+        x_scales = keep.tile([P, TILES * KG * P], U8, name="x_scales", align_bytes=64)
         t_t, r_at, rc_t, rs_t = {}, {}, {}, {}
         bank_of, free = {}, list(range(BANKS))
 
@@ -132,27 +136,22 @@ def tile_ftn_residual_turn_s9_kernel(tc, lam, amp, h_words, h_scales, y, v, f, o
                     func=TANH,
                 )
 
+        def xb_of(i):
+            return xb_one[:] if i in (0, 6, 7) else xb_two[:, K * (i in (2, 5)) :]
+
         def x_amp(i, g0=0, g1=KG):
-            if g0 == 0:
-                xb_t[i] = work.tile([P, KG * P * 4], BF16, name="xb", bufs=2, align_bytes=64)
             engine, words = (nc.gpsimd, amp_col[:]) if i == 3 else (nc.vector, factors[:, 0:4])
             factor = words.bitcast(BF16).rearrange("p (g t) -> p g t", g=KG)[:, g0:g1]
             engine.tensor_tensor(
-                out=xb_t[i][:].rearrange("p (g m t) -> p g m t", g=KG, t=4)[:, g0:g1],
+                out=xb_of(i)[:, :K].rearrange("p (g m t) -> p g m t", g=KG, t=4)[:, g0:g1],
                 in0=xf_t[i][:, g0:g1],
                 in1=factor.unsqueeze(2).to_broadcast([P, g1 - g0, P, 4]),
                 op=ALU.mult,
             )
 
-        def x_quant(i, g0=0, g1=KG):
-            if g0 == 0:
-                xc_t[i] = work.tile([P, KG * P], U32, name="xc", bufs=4, align_bytes=64)
-                xs_t[i] = work.tile([P, KG * P], U8, name="xs", bufs=4, align_bytes=64)
-            nc.vector.quantize_mx(
-                out=xc_t[i][:, P * g0 : P * g1].bitcast(E4M3X4),
-                scales=xs_t[i][:, P * g0 : P * g1],
-                in_=xb_t[i][:, 512 * g0 : 512 * g1],
-            )
+        def x_quant(i, j):
+            cols = slice(KG * P * i, KG * P * j)
+            nc.vector.quantize_mx(out=x_codes[:, cols].bitcast(E4M3X4), scales=x_scales[:, cols], in_=xb_of(i)[:, : K * (j - i)])
 
         def first(i, b):
             z = take(("z", i, b))
@@ -160,8 +159,8 @@ def tile_ftn_residual_turn_s9_kernel(tc, lam, amp, h_words, h_scales, y, v, f, o
             for g in range(KG):
                 nc.tensor.matmul_mx(
                     out=z[:].rearrange("p a m -> p (a m)"),
-                    lhsT=xc_t[i][:, P * g : P * (g + 1)].bitcast(E4M3X4),
-                    lhsT_scale=xs_t[i][:, P * g : P * (g + 1)],
+                    lhsT=x_codes[:, P * (KG * i + g) : P * (KG * i + g + 1)].bitcast(E4M3X4),
+                    lhsT_scale=x_scales[:, P * (KG * i + g) : P * (KG * i + g + 1)],
                     rhs=hw[half][:, g, 1024 * c : 1024 * (c + 1)].bitcast(E2M1X4),
                     rhs_scale=hs[:, g, 512 * b : 512 * (b + 1)],
                     start=(g == 0),
@@ -198,13 +197,16 @@ def tile_ftn_residual_turn_s9_kernel(tc, lam, amp, h_words, h_scales, y, v, f, o
             )
 
         stage = [keep.tile([P, 2 * N], BF16, name="stage_a", align_bytes=64), keep.tile([P, 2 * N], BF16, name="stage_b", align_bytes=64)]
-        f_words = {}
+        f_ring = keep.tile([P, F_BUFS * 2048], BF16, name="f_ring", align_bytes=64)
+
+        def f_words(c, count=1):
+            return f_ring[:, 2048 * (c % F_BUFS) : 2048 * (c % F_BUFS + count)]
 
         def r_space(i, j, b0):
             if i == 0:
-                return f_words[0][:] if b0 == 0 else stage[0][:, :N]
+                return f_words(0) if b0 == 0 else stage[0][:, :N]
             if i == LAST - 1:
-                return xb_t[LAST if b0 == 0 else LAST - 1][:]
+                return f_words(2 * NG - 1)[:, 512 * b0 :]
             if i == LAST:
                 return stage[1][:, 512 * b0 : 512 * b0 + 1024]
             return stage[i // 2 % 2][:, 1024 * b0 :]
@@ -236,10 +238,12 @@ def tile_ftn_residual_turn_s9_kernel(tc, lam, amp, h_words, h_scales, y, v, f, o
                 g, u = divmod(a, 2)
                 nc.tensor.transpose(bank[:, a, :], r_at[i, 2 * half + g][:, 256 * u : 256 * (u + 1)].bitcast(F32), ident[:])
 
+        def r_slot(i, half):
+            return 2 * half + i % 2 if i < LAST - 1 else 2 * (i % 2) + half
+
         def r_words(i, half):
-            pair, j = divmod(i, 2)
-            slot = 3 - (2 * half + j if pair < PAIRS - 1 else 2 * j + half)
-            return stage[(pair + 1) % 2][:, 1024 * slot : 1024 * (slot + 1)]
+            slot = r_slot(i, half)
+            return stage[(i // 2 + 1) % 2][:, 1024 * slot : 1024 * (slot + 1)]
 
         def r_copy(i, half):
             nc.scalar.copy(
@@ -247,32 +251,30 @@ def tile_ftn_residual_turn_s9_kernel(tc, lam, amp, h_words, h_scales, y, v, f, o
                 in_=give(("r", i, half))[:].rearrange("p (g u) m -> p g m u", u=2),
             )
 
-        def r_quant(i, half):
-            if half == 0:
-                rc_t[i] = work.tile([P, NG * P], U32, name="rc", bufs=4, align_bytes=64)
-                rs_t[i] = work.tile([P, NG * P], U8, name="rs", bufs=4, align_bytes=64)
+        def r_quant(pair, part):
+            if part == 0:
+                rc_t[pair] = work.tile([P, 2 * NG * P], U32, name="rc", bufs=2, align_bytes=64)
+                rs_t[pair] = work.tile([P, 2 * NG * P], U8, name="rs", bufs=2, align_bytes=64)
             nc.vector.quantize_mx(
-                out=rc_t[i][:, 256 * half : 256 * (half + 1)].bitcast(E5M2X4),
-                scales=rs_t[i][:, 256 * half : 256 * (half + 1)],
-                in_=r_words(i, half),
+                out=rc_t[pair][:, 512 * part : 512 * (part + 1)].bitcast(E5M2X4),
+                scales=rs_t[pair][:, 512 * part : 512 * (part + 1)],
+                in_=stage[(pair + 1) % 2][:, N * part : N * (part + 1)],
             )
 
         f_codes = keep.tile([P, 2 * NG * 512], U32, name="f_codes", align_bytes=64)
         f_scales = keep.tile([P, 2 * NG * 512], U8, name="f_scales", align_bytes=64)
 
         def f_copy(c, q):
-            if q == 0:
-                f_words[c] = work.tile([P, 2048], BF16, name="f_words", bufs=F_BUFS, align_bytes=64)
             nc.scalar.copy(
-                out=f_words[c][:, 1024 * q : 1024 * (q + 1)].rearrange("p (c i t) -> p c t i", i=4, t=4),
+                out=f_words(c)[:, 1024 * q : 1024 * (q + 1)].rearrange("p (c i t) -> p c t i", i=4, t=4),
                 in_=f_raw[c][:, :, 256 * q : 256 * (q + 1)].rearrange("p t (c i) -> p c t i", i=4),
             )
 
-        def f_quant(c):
+        def f_quant(c0, c1):
             nc.vector.quantize_mx(
-                out=f_codes[:, 512 * c : 512 * (c + 1)].bitcast(E4M3X4),
-                scales=f_scales[:, 512 * c : 512 * (c + 1)],
-                in_=f_words[c][:],
+                out=f_codes[:, 512 * c0 : 512 * c1].bitcast(E4M3X4),
+                scales=f_scales[:, 512 * c0 : 512 * c1],
+                in_=f_words(c0, c1 - c0),
             )
 
         def second(i, c0, c1=None, h0=0, h1=2):
@@ -282,10 +284,11 @@ def tile_ftn_residual_turn_s9_kernel(tc, lam, amp, h_words, h_scales, y, v, f, o
             width = 256 * (c1 - c0)
             for g in range(2 * h0, 2 * h1):
                 c = 512 * (NG * kh + g) + 256 * q
+                a = 256 * r_slot(i, g // 2) + P * (g % 2)
                 nc.tensor.matmul_mx(
                     out=d[:].rearrange("p a m -> p (a m)")[:, :width],
-                    lhsT=rc_t[i][:, P * g : P * (g + 1)].bitcast(E5M2X4),
-                    lhsT_scale=rs_t[i][:, P * g : P * (g + 1)],
+                    lhsT=rc_t[i // 2][:, a : a + P].bitcast(E5M2X4),
+                    lhsT_scale=rs_t[i // 2][:, a : a + P],
                     rhs=f_codes[:, c : c + width].bitcast(E4M3X4),
                     rhs_scale=f_scales[:, c : c + width],
                     start=(g == 0),
@@ -300,6 +303,18 @@ def tile_ftn_residual_turn_s9_kernel(tc, lam, amp, h_words, h_scales, y, v, f, o
             cols = slice(256 * c0, 256 * c1)
             nc.vector.tensor_add(out=o[:], in0=d[:, :width], in1=lam_t[i][:, cols])
             nc.sync.dma_start(out=out[P * i : P * (i + 1), cols], in_=o[:])
+
+        parked = {}
+
+        def park(i, kh):
+            parked[i, kh] = work.tile([P, 512], F32, name="parked", bufs=3, align_bytes=64)
+            nc.scalar.copy(out=parked[i, kh][:], in_=give(("d", i, 2 * kh))[:].rearrange("p a m -> p (a m)"))
+
+        def late_add(i, kh, slot):
+            o = stage[0][:, 1024 * slot : 1024 * (slot + 1)].bitcast(F32)
+            cols = slice(512 * kh, 512 * (kh + 1))
+            nc.gpsimd.tensor_tensor(out=o, in0=parked[i, kh][:], in1=lam_t[i][:, cols], op=ALU.add)
+            nc.sync.dma_start(out=out[P * i : P * (i + 1), cols], in_=o)
 
         nc.scalar.dma_start(out=v_in[:], in_=v.rearrange("(q c) -> q c", c=16))
         load_v_col(3, nc.scalar)
@@ -342,33 +357,34 @@ def tile_ftn_residual_turn_s9_kernel(tc, lam, amp, h_words, h_scales, y, v, f, o
         def across(call, i):
             return [(call, i, 0), (call, i + 1, 0), (call, i, 1), (call, i + 1, 1)]
 
-        vector = [(x_amp, 0, 0, 1), (x_amp, 0, 1, 2), (x_quant, 0, 0, 1), (x_quant, 0, 1, 2), (amp_copy,), (x_amp, 1), (x_amp, 2), (x_quant, 1), (x_quant, 2), (x_amp, 3)]
-        vector.extend(left(sub, 0) + [(x_quant, 3), (f_quant, 0), (weigh, 0, 2, 0, 2)])
-        vector.extend([(x_amp, 4)] + right(sub, 0) + [(weigh, 0, 2, 2, 4), (x_amp, 5)] + left(sub, 2) + right(sub, 2))
-        vector.extend([(x_quant, 4), (x_quant, 5), (f_quant, 1), (f_quant, 2), (f_quant, 3)] + across(r_quant, 0) + [(weigh, 2, 4, 0, 2), (weigh, 2, 4, 2, 3)])
-        vector.extend([(sub, 4, 0), (weigh, 2, 4, 3, 4), (sub, 4, 1), (add, 0, 0), (sub, 5, 0), (x_amp, 6), (sub, 5, 1)] + right(sub, 4))
-        vector.extend([(x_quant, 6)] + [(f_quant, c) for c in range(NG, 2 * NG)] + across(r_quant, 2))
+        vector = [(x_amp, 0, 0, 1), (x_amp, 0, 1, 2), (amp_copy,), (x_quant, 0, 1), (x_amp, 1), (x_amp, 2), (x_quant, 1, 2), (x_quant, 2, 3), (x_amp, 3)]
+        vector.extend(left(sub, 0) + [(f_quant, 0, 1), (x_quant, 3, 4), (weigh, 0, 2, 0, 2)])
+        vector.extend([(x_amp, 4)] + right(sub, 0) + [(weigh, 0, 2, 2, 4), (x_amp, 5)] + left(sub, 2) + right(sub, 2)[:3])
+        vector.extend([(x_quant, 4, 6), (f_quant, 1, 2), (f_quant, 2, 4)] + halves(r_quant, 0) + [(weigh, 2, 4, 0, 2), (weigh, 2, 4, 2, 3)])
+        vector.extend([(sub, 3, 3), (sub, 4, 0), (weigh, 2, 4, 3, 4), (sub, 4, 1), (sub, 5, 0), (x_amp, 6), (sub, 5, 1)] + right(sub, 4)[:3])
+        vector.extend([(x_quant, 6, 7), (f_quant, 4, 6), (f_quant, 6, 8)] + halves(r_quant, 1))
         vector.extend([(weigh, 4, 6, 0, 2), (weigh, 4, 6, 2, 3)])
-        vector.extend([(add, 1, 0), (sub, 6, 0), (add, 0, 2, 4), (x_amp, 7), (add, 1, 2, 4), (weigh, 4, 6, 3, 4), (sub, 6, 1), (sub, 6, 2), (add, 2, 0), (sub, 6, 3), (add, 2, 1)])
-        vector.extend([(x_quant, 7), (weigh, 6, 7, 0, 2), (add, 3, 0), (weigh, 6, 7, 2, 4), (sub, 7, 0), (sub, 7, 1)])
-        vector.extend(across(r_quant, 4) + [(weigh, 7, 8, 0, 2), (sub, 7, 2), (sub, 7, 3), (add, 3, 1), (weigh, 7, 8, 2, 4)])
-        vector.extend(halves(r_quant, 6) + [(add, 4, 0), (add, 4, 1), (r_quant, 7, 0), (add, 5, 0), (r_quant, 7, 1), (add, 5, 1)] + left(add, 6)[:3])
-        vector.extend([(add, LAST, 2, 3), (add, LAST, 3, 4)])
+        vector.extend([(sub, 5, 3), (sub, 6, 0), (x_amp, 7), (add, 1, 2, 4), (weigh, 4, 6, 3, 4), (sub, 6, 2), (sub, 6, 3), (add, 2, 0), (add, 2, 1), (sub, 6, 1)])
+        vector.extend([(x_quant, 7, 8), (weigh, 6, 7, 0, 2), (add, 3, 0), (weigh, 6, 7, 2, 4), (sub, 7, 0), (sub, 7, 1)])
+        vector.extend(halves(r_quant, 2) + [(weigh, 7, 8, 0, 2), (sub, 7, 2), (sub, 7, 3), (add, 3, 1), (weigh, 7, 8, 2, 4)])
+        vector.extend([(r_quant, 3, 0), (add, 4, 0), (add, 4, 1), (late_add, 0, 0, 0), (add, 5, 0), (r_quant, 3, 1), (add, 5, 1), (add, 6, 0), (late_add, 1, 0, 2)])
+        vector.extend([(add, 6, 1), (late_add, 0, 1, 3), (add, LAST, 0), (add, LAST, 2, 3), (add, LAST, 3, 4)])
 
         tensor = [(x_turn, 0, 0, 1), (x_turn, 0, 1, 2), (amp_turn,), (v_col_turn, 3), (x_turn, 1), (x_turn, 2), (v_turn, 0), (x_turn, 3), (v_turn, 1)]
         tensor.extend(left(first, 0) + [(x_turn, 4), (x_turn, 5)] + right(first, 0) + left(first, 2) + across(r_turn, 0)[:2] + right(first, 2))
-        tensor.extend(across(r_turn, 0)[2:] + [(x_turn, 6)] + halves(first, 4) + [(second, 0, 0)] + halves(first, 5) + right(first, 4)[:2])
+        tensor.extend([(x_turn, 6)] + across(r_turn, 0)[2:] + halves(first, 4) + [(second, 0, 0)] + halves(first, 5) + right(first, 4)[:2])
         tensor.extend([(x_turn, 7)] + right(first, 4)[2:])
         tensor.extend(across(r_turn, 2)[:2] + [(second, 1, 0)] + across(r_turn, 2)[2:] + [(first, 6, 0)])
         tensor.extend([(second, i, 2, 4, h, h + 1) for h in range(2) for i in range(2)])
-        tensor.extend([(first, 6, 1), (first, 6, 2), (second, 2, 0), (first, 6, 3), (second, 2, 1), (second, 3, 0), (v_col_turn, 2)] + across(r_turn, 4)[:2])
+        tensor.extend([(first, 6, 2), (first, 6, 3), (second, 2, 0), (second, 2, 1), (first, 6, 1), (second, 3, 0), (v_col_turn, 2)] + across(r_turn, 4)[:2])
         tensor.extend([(second, 3, 1)] + across(r_turn, 4)[2:] + [(first, 7, b) for b in range(NG)] + halves(r_turn, 6))
         tensor.extend(left(second, 4)[:3] + halves(r_turn, 7) + [(second, 5, 1)] + left(second, 6)[:3] + [(second, LAST, 2, 3), (second, LAST, 3, 4)])
 
-        scalar = [(x_tanh, 0, 0, 1), (x_tanh, 0, 1, 2), (x_tanh, 1), (x_tanh, 2), (v_copy, 0), (x_tanh, 3), (v_copy, 1)] + halves(f_copy, 0)
-        scalar.extend([(x_tanh, 4), (x_tanh, 5)] + left(f_copy, 1) + across(r_copy, 0)[:2] + halves(f_copy, 3))
-        scalar.extend(across(r_copy, 0)[2:] + [(x_tanh, 6)] + left(f_copy, 4) + left(f_copy, 6)[:3] + across(r_copy, 2)[:2] + [(f_copy, 7, 1)] + across(r_copy, 2)[2:])
-        scalar.extend([(x_tanh, 7)] + across(r_copy, 4) + left(r_copy, 6))
+        scalar = [(x_tanh, 0, 0, 1), (x_tanh, 0, 1, 2), (x_tanh, 1), (x_tanh, 2), (v_copy, 0), (x_tanh, 3)] + halves(f_copy, 0)
+        scalar.extend([(v_copy, 1), (x_tanh, 4), (x_tanh, 5)] + left(f_copy, 1) + across(r_copy, 0)[:2] + halves(f_copy, 3))
+        scalar.extend([(x_tanh, 6)] + across(r_copy, 0)[2:] + left(f_copy, 4)[:3] + [(park, 0, 0), (f_copy, 5, 1)] + left(f_copy, 6)[:3])
+        scalar.extend(across(r_copy, 2)[:2] + [(f_copy, 7, 1)] + across(r_copy, 2)[2:])
+        scalar.extend([(x_tanh, 7), (park, 1, 0), (park, 0, 1)] + across(r_copy, 4)[:2] + across(r_copy, 4)[2:] + left(r_copy, 6))
 
         windows = [x for x in vector if x[0] == weigh]
 
@@ -379,7 +395,7 @@ def tile_ftn_residual_turn_s9_kernel(tc, lam, amp, h_words, h_scales, y, v, f, o
             if call == x_amp:
                 return [(x_tanh, *step[1:]), (v_col_turn, 3)]
             if call == first:
-                return [(x_quant, i) if i else (x_quant, 0, 1, 2)]
+                return [x for x in quants if x[0] == x_quant and x[1] <= i < x[2]]
             if call == weigh:
                 return [(v_copy, 1)] + [(v_col_turn, 2)][: i // (LAST - 1)]
             if call == v_col_turn:
@@ -387,19 +403,26 @@ def tile_ftn_residual_turn_s9_kernel(tc, lam, amp, h_words, h_scales, y, v, f, o
             if call == r_turn:
                 return [w for w in windows if w[1] <= i < w[2] and w[3] < 2 * step[2] + 2 and w[4] > 2 * step[2]]
             if call == f_copy:
-                return [(f_quant, i - F_BUFS)] + across(r_turn, 0)[:2] if i >= F_BUFS else []
+                return [x for x in quants if x[0] == f_quant and x[1] <= i - F_BUFS < x[2]] + across(r_turn, 0)[: 2 * (i == F_BUFS)]
             if call == f_quant:
-                return halves(f_copy, i)
+                return [(f_copy, step[2] - 1, 1)]
             if call == second:
                 h = step[5] - 1 if len(step) > 4 else 1
                 kh = step[2] // 2 if len(step) > 3 else step[2]
-                return [(r_quant, i, h), (f_quant, NG * kh + 2 * h + 1)]
+                return [(r_quant, i // 2, r_slot(i, h) // 2)] + [x for x in quants if x[0] == f_quant and x[2] == NG * kh + 2 * h + 2]
             if call == add:
                 return [x for x in tensor_all if x[: len(step)] == (second, *step[1:])]
-            producer = {sub: first, v_copy: v_turn, r_copy: r_turn, r_quant: r_copy}
+            if call == park:
+                return [x for x in tensor_all if x[:3] == (second, *step[1:]) or x[:4] == (second, i, 2 * step[2], 2 * step[2] + 2)]
+            if call == late_add:
+                return [(park, i, step[2])]
+            if call == r_quant:
+                return [(r_copy, a, h) for a in (2 * i, 2 * i + 1) for h in range(2) if r_slot(a, h) // 2 == step[2]]
+            producer = {sub: first, v_copy: v_turn, r_copy: r_turn}
             return [(producer[call], *step[1:])] if call in producer else []
 
         tensor_all = list(tensor)
+        quants = [x for x in vector if x[0] in (x_quant, f_quant)]
         queue_of = {}
         for queue in (tensor, scalar, vector):
             for step in queue:

@@ -52,11 +52,11 @@ def tile_ftn_residual_turn_s9_kernel(tc, lam, amp, h_words, h_scales, y, v, f, o
                 cols = slice(K // parts * c, K // parts * (c + 1))
                 nc.sync.dma_start(out=lam_t[i][:, cols], in_=lam[P * i : P * (i + 1), cols])
 
-        def load_y(i, c0=0, c1=2):
-            if c0 == 0:
-                y_t[i] = work.tile([P, N], BF16, name="y_in", bufs=TILES, align_bytes=64)
-            cols = slice(1024 * c0, 1024 * c1)
-            nc.sync.dma_start(out=y_t[i][:, cols], in_=y[P * i : P * (i + 1), cols])
+        def load_y(pair, half, j0=0, j1=2):
+            if j0 == 0:
+                y_t[pair, half] = work.tile([P, 2, K], BF16, name="y_in", bufs=TILES, align_bytes=64)
+            rows = y[P * (2 * pair + j0) : P * (2 * pair + j1), K * half : K * (half + 1)]
+            nc.sync.dma_start(out=y_t[pair, half][:, j0:j1], in_=rows.rearrange("(j p) c -> p j c", p=P))
 
         def load_f(c):
             kh, g = divmod(c, NG)
@@ -177,7 +177,7 @@ def tile_ftn_residual_turn_s9_kernel(tc, lam, amp, h_words, h_scales, y, v, f, o
             c = t_col(i, b)
             nc.vector.tensor_sub(
                 out=t_t[i // 2][:, c : c + 512].rearrange("p (u q e) -> p u q e", u=2, e=2),
-                in0=y_t[i][:, 512 * b : 512 * (b + 1)].rearrange("p (q u e) -> p u q e", u=2, e=2),
+                in0=y_t[i // 2, b // 2][:, i % 2, 512 * (b % 2) : 512 * (b % 2 + 1)].rearrange("p (q u e) -> p u q e", u=2, e=2),
                 in1=give(("z", i, b))[:].rearrange("p a (q u e) -> p u (a q) e", u=2, e=2),
             )
 
@@ -239,7 +239,7 @@ def tile_ftn_residual_turn_s9_kernel(tc, lam, amp, h_words, h_scales, y, v, f, o
                 nc.tensor.transpose(bank[:, a, :], r_at[i, 2 * half + g][:, 256 * u : 256 * (u + 1)].bitcast(F32), ident[:])
 
         def r_slot(i, half):
-            return 2 * half + i % 2 if i < LAST - 1 else 2 * (i % 2) + half
+            return 2 * (1 - half) + i % 2 if i < LAST - 1 else 2 * (i % 2) + half
 
         def r_words(i, half):
             slot = r_slot(i, half)
@@ -252,9 +252,9 @@ def tile_ftn_residual_turn_s9_kernel(tc, lam, amp, h_words, h_scales, y, v, f, o
             )
 
         def r_quant(pair, part):
-            if part == 0:
-                rc_t[pair] = work.tile([P, 2 * NG * P], U32, name="rc", bufs=2, align_bytes=64)
-                rs_t[pair] = work.tile([P, 2 * NG * P], U8, name="rs", bufs=2, align_bytes=64)
+            if pair not in rc_t:
+                rc_t[pair] = work.tile([P, 2 * NG * P], U32, name="rc", bufs=PAIRS, align_bytes=64)
+                rs_t[pair] = work.tile([P, 2 * NG * P], U8, name="rs", bufs=PAIRS, align_bytes=64)
             nc.vector.quantize_mx(
                 out=rc_t[pair][:, 512 * part : 512 * (part + 1)].bitcast(E5M2X4),
                 scales=rs_t[pair][:, 512 * part : 512 * (part + 1)],
@@ -264,10 +264,10 @@ def tile_ftn_residual_turn_s9_kernel(tc, lam, amp, h_words, h_scales, y, v, f, o
         f_codes = keep.tile([P, 2 * NG * 512], U32, name="f_codes", align_bytes=64)
         f_scales = keep.tile([P, 2 * NG * 512], U8, name="f_scales", align_bytes=64)
 
-        def f_copy(c, q):
+        def f_copy(c, q0=0, q1=2):
             nc.scalar.copy(
-                out=f_words(c)[:, 1024 * q : 1024 * (q + 1)].rearrange("p (c i t) -> p c t i", i=4, t=4),
-                in_=f_raw[c][:, :, 256 * q : 256 * (q + 1)].rearrange("p t (c i) -> p c t i", i=4),
+                out=f_words(c)[:, 1024 * q0 : 1024 * q1].rearrange("p (c i t) -> p c t i", i=4, t=4),
+                in_=f_raw[c][:, :, 256 * q0 : 256 * q1].rearrange("p t (c i) -> p c t i", i=4),
             )
 
         def f_quant(c0, c1):
@@ -299,10 +299,10 @@ def tile_ftn_residual_turn_s9_kernel(tc, lam, amp, h_words, h_scales, y, v, f, o
             c0, c1 = (2 * c0, 2 * c0 + 2) if c1 is None else (c0, c1)
             width = 256 * (c1 - c0)
             d = give(("d", i, c0))[:].rearrange("p a m -> p (a m)")
-            o = work.tile([P, width], F32, name="o", bufs=6, align_bytes=64)
             cols = slice(256 * c0, 256 * c1)
-            nc.vector.tensor_add(out=o[:], in0=d[:, :width], in1=lam_t[i][:, cols])
-            nc.sync.dma_start(out=out[P * i : P * (i + 1), cols], in_=o[:])
+            o = y_t[i // 2, c0 // 2][:, i % 2].bitcast(F32)[:, 256 * (c0 % 2) : 256 * (c0 % 2) + width]
+            nc.vector.tensor_add(out=o, in0=d[:, :width], in1=lam_t[i][:, cols])
+            nc.sync.dma_start(out=out[P * i : P * (i + 1), cols], in_=o)
 
         parked = {}
 
@@ -323,26 +323,25 @@ def tile_ftn_residual_turn_s9_kernel(tc, lam, amp, h_words, h_scales, y, v, f, o
         for i in range(1, 4):
             load_lam(i)
         load_scales()
-        for half in range(2):
-            load_h(half)
-            load_f(half)
-            load_y(0, half, half + 1)
-            load_y(1, half, half + 1)
-            if half == 0:
-                load_lam(4)
-                load_lam(5)
+        load_h(0)
+        load_f(0)
+        load_y(0, 0, 0, 1)
+        load_y(0, 0, 1, 2)
+        load_lam(4)
+        load_lam(5)
+        load_h(1)
+        load_y(0, 1)
+        load_f(1)
         for half in range(2):
             load_f(2 + half)
-            load_y(2, half, half + 1)
-            load_y(3, half, half + 1)
+            load_y(1, half)
         for half in range(2):
             load_lam(6 + half)
             load_f(4 + 2 * half)
-            load_y(4, half, half + 1)
-            load_y(5, half, half + 1)
+            load_y(2, half)
             load_f(5 + 2 * half)
-        load_y(6)
-        load_y(7)
+        load_y(3, 0)
+        load_y(3, 1)
         load_v_col(2, nc.sync)
 
         def halves(call, i):
@@ -359,19 +358,20 @@ def tile_ftn_residual_turn_s9_kernel(tc, lam, amp, h_words, h_scales, y, v, f, o
 
         vector = [(x_amp, 0, 0, 1), (x_amp, 0, 1, 2), (amp_copy,), (x_quant, 0, 1), (x_amp, 1), (x_amp, 2), (x_quant, 1, 2), (x_quant, 2, 3), (x_amp, 3)]
         vector.extend(left(sub, 0) + [(f_quant, 0, 1), (x_quant, 3, 4), (weigh, 0, 2, 0, 2)])
-        vector.extend([(x_amp, 4)] + right(sub, 0) + [(weigh, 0, 2, 2, 4), (x_amp, 5)] + left(sub, 2) + right(sub, 2)[:3])
-        vector.extend([(x_quant, 4, 6), (f_quant, 1, 2), (f_quant, 2, 4)] + halves(r_quant, 0) + [(weigh, 2, 4, 0, 2), (weigh, 2, 4, 2, 3)])
-        vector.extend([(sub, 3, 3), (sub, 4, 0), (weigh, 2, 4, 3, 4), (sub, 4, 1), (sub, 5, 0), (x_amp, 6), (sub, 5, 1)] + right(sub, 4)[:3])
-        vector.extend([(x_quant, 6, 7), (f_quant, 4, 6), (f_quant, 6, 8)] + halves(r_quant, 1))
+        vector.extend(right(sub, 0)[:2] + [(x_amp, 4)] + right(sub, 0)[2:] + [(weigh, 0, 2, 2, 4), (x_amp, 5)] + left(sub, 2) + right(sub, 2)[:3])
+        vector.extend([(x_quant, 4, 6), (f_quant, 1, 2), (f_quant, 2, 3), (f_quant, 3, 4)] + [(r_quant, 0, 1), (r_quant, 0, 0)] + [(weigh, 2, 4, 0, 2), (weigh, 2, 4, 2, 3)])
+        vector.extend([(sub, 3, 3), (sub, 4, 0), (weigh, 2, 4, 3, 4), (sub, 4, 1), (add, 0, 0), (sub, 5, 0), (x_amp, 6), (sub, 5, 1)] + right(sub, 4)[:3])
+        vector.extend([(x_quant, 6, 7), (f_quant, 4, 5), (f_quant, 5, 6), (f_quant, 6, 7), (f_quant, 7, 8)] + [(r_quant, 1, 1), (r_quant, 1, 0)])
         vector.extend([(weigh, 4, 6, 0, 2), (weigh, 4, 6, 2, 3)])
         vector.extend([(sub, 5, 3), (sub, 6, 0), (x_amp, 7), (add, 1, 2, 4), (weigh, 4, 6, 3, 4), (sub, 6, 2), (sub, 6, 3), (add, 2, 0), (add, 2, 1), (sub, 6, 1)])
         vector.extend([(x_quant, 7, 8), (weigh, 6, 7, 0, 2), (add, 3, 0), (weigh, 6, 7, 2, 4), (sub, 7, 0), (sub, 7, 1)])
-        vector.extend(halves(r_quant, 2) + [(weigh, 7, 8, 0, 2), (sub, 7, 2), (sub, 7, 3), (add, 3, 1), (weigh, 7, 8, 2, 4)])
-        vector.extend([(r_quant, 3, 0), (add, 4, 0), (add, 4, 1), (late_add, 0, 0, 0), (add, 5, 0), (r_quant, 3, 1), (add, 5, 1), (add, 6, 0), (late_add, 1, 0, 2)])
-        vector.extend([(add, 6, 1), (late_add, 0, 1, 3), (add, LAST, 0), (add, LAST, 2, 3), (add, LAST, 3, 4)])
+        vector.extend([(r_quant, 2, 1), (r_quant, 2, 0)] + [(weigh, 7, 8, 0, 2), (sub, 7, 2), (sub, 7, 3), (add, 3, 1), (weigh, 7, 8, 2, 4)])
+        vector.extend([(r_quant, 3, 0), (add, 4, 0), (add, 4, 1), (late_add, 1, 0, 0), (add, 5, 0), (r_quant, 3, 1), (add, 5, 1), (add, 6, 0), (late_add, 0, 1, 2)])
+        vector.extend([(add, 6, 1), (add, LAST, 0), (add, LAST, 2, 3), (add, LAST, 3, 4)])
 
-        tensor = [(x_turn, 0, 0, 1), (x_turn, 0, 1, 2), (amp_turn,), (v_col_turn, 3), (x_turn, 1), (x_turn, 2), (v_turn, 0), (x_turn, 3), (v_turn, 1)]
-        tensor.extend(left(first, 0) + [(x_turn, 4), (x_turn, 5)] + right(first, 0) + left(first, 2) + across(r_turn, 0)[:2] + right(first, 2))
+        tensor = [(x_turn, 0, 0, 1), (amp_turn,), (x_turn, 0, 1, 2), (x_turn, 1), (x_turn, 2), (x_turn, 3)] + halves(first, 0)
+        tensor.extend([(v_turn, 0), (v_turn, 1)] + halves(first, 1) + [(x_turn, 4), (x_turn, 5)] + right(first, 0) + left(first, 2) + right(first, 2)[:2])
+        tensor.extend(across(r_turn, 0)[:2] + [(v_col_turn, 3)] + right(first, 2)[2:])
         tensor.extend([(x_turn, 6)] + across(r_turn, 0)[2:] + halves(first, 4) + [(second, 0, 0)] + halves(first, 5) + right(first, 4)[:2])
         tensor.extend([(x_turn, 7)] + right(first, 4)[2:])
         tensor.extend(across(r_turn, 2)[:2] + [(second, 1, 0)] + across(r_turn, 2)[2:] + [(first, 6, 0)])
@@ -380,10 +380,9 @@ def tile_ftn_residual_turn_s9_kernel(tc, lam, amp, h_words, h_scales, y, v, f, o
         tensor.extend([(second, 3, 1)] + across(r_turn, 4)[2:] + [(first, 7, b) for b in range(NG)] + halves(r_turn, 6))
         tensor.extend(left(second, 4)[:3] + halves(r_turn, 7) + [(second, 5, 1)] + left(second, 6)[:3] + [(second, LAST, 2, 3), (second, LAST, 3, 4)])
 
-        scalar = [(x_tanh, 0, 0, 1), (x_tanh, 0, 1, 2), (x_tanh, 1), (x_tanh, 2), (v_copy, 0), (x_tanh, 3)] + halves(f_copy, 0)
-        scalar.extend([(v_copy, 1), (x_tanh, 4), (x_tanh, 5)] + left(f_copy, 1) + across(r_copy, 0)[:2] + halves(f_copy, 3))
-        scalar.extend([(x_tanh, 6)] + across(r_copy, 0)[2:] + left(f_copy, 4)[:3] + [(park, 0, 0), (f_copy, 5, 1)] + left(f_copy, 6)[:3])
-        scalar.extend(across(r_copy, 2)[:2] + [(f_copy, 7, 1)] + across(r_copy, 2)[2:])
+        scalar = [(x_tanh, 0, 0, 1), (x_tanh, 0, 1, 2), (x_tanh, 1), (x_tanh, 2), (x_tanh, 3), (f_copy, 0), (v_copy, 0), (v_copy, 1)]
+        scalar.extend([(x_tanh, 4), (x_tanh, 5), (f_copy, 1), (f_copy, 2)] + across(r_copy, 0)[:2] + [(f_copy, 3), (x_tanh, 6)] + across(r_copy, 0)[2:])
+        scalar.extend([(f_copy, 4), (f_copy, 5), (f_copy, 6), (f_copy, 7, 0, 1)] + across(r_copy, 2)[:2] + [(f_copy, 7, 1, 2)] + across(r_copy, 2)[2:])
         scalar.extend([(x_tanh, 7), (park, 1, 0), (park, 0, 1)] + across(r_copy, 4)[:2] + across(r_copy, 4)[2:] + left(r_copy, 6))
 
         windows = [x for x in vector if x[0] == weigh]
@@ -393,19 +392,19 @@ def tile_ftn_residual_turn_s9_kernel(tc, lam, amp, h_words, h_scales, y, v, f, o
             if call == x_tanh:
                 return [(x_turn, *step[1:])] + [(x_amp, k) if k else (x_amp, 0, 1, 2) for k in (i - XF_BUFS,) if k >= 0]
             if call == x_amp:
-                return [(x_tanh, *step[1:]), (v_col_turn, 3)]
+                return [(x_tanh, *step[1:]), (amp_turn,)]
             if call == first:
                 return [x for x in quants if x[0] == x_quant and x[1] <= i < x[2]]
             if call == weigh:
                 return [(v_copy, 1)] + [(v_col_turn, 2)][: i // (LAST - 1)]
             if call == v_col_turn:
-                return [(x_amp, LAST), (weigh, 4, 6, 3, 4)] if i == 2 else []
+                return [(x_amp, LAST), (weigh, 4, 6, 3, 4)] if i == 2 else [(x_amp, 5)]
             if call == r_turn:
                 return [w for w in windows if w[1] <= i < w[2] and w[3] < 2 * step[2] + 2 and w[4] > 2 * step[2]]
             if call == f_copy:
                 return [x for x in quants if x[0] == f_quant and x[1] <= i - F_BUFS < x[2]] + across(r_turn, 0)[: 2 * (i == F_BUFS)]
             if call == f_quant:
-                return [(f_copy, step[2] - 1, 1)]
+                return [(f_copy, step[2] - 1) if step[2] < 2 * NG else (f_copy, 7, 1, 2)]
             if call == second:
                 h = step[5] - 1 if len(step) > 4 else 1
                 kh = step[2] // 2 if len(step) > 3 else step[2]

@@ -202,7 +202,7 @@ def tile_ftn_residual_turn_s9_kernel(tc, lam, amp, h_words, h_scales, y, v, f, o
         def f_words(c, count=1):
             return f_ring[:, 2048 * (c % F_BUFS) : 2048 * (c % F_BUFS + count)]
 
-        def r_space(i, j, b0):
+        def r_space(i, b0):
             if i == 0:
                 return f_words(0) if b0 == 0 else stage[0][:, :N]
             if i == LAST - 1:
@@ -214,7 +214,7 @@ def tile_ftn_residual_turn_s9_kernel(tc, lam, amp, h_words, h_scales, y, v, f, o
         def weigh(i, j, b0, b1):
             tiles, groups = j - i, b1 - b0
             width = 512 * tiles * groups
-            dst = r_space(i, j, b0)[:, :width]
+            dst = r_space(i, b0)[:, :width]
             for b in range(b0, b1):
                 for a in range(tiles):
                     c = 512 * (tiles * (b - b0) + a)
@@ -266,8 +266,8 @@ def tile_ftn_residual_turn_s9_kernel(tc, lam, amp, h_words, h_scales, y, v, f, o
 
         def f_copy(c, q0=0, q1=2):
             nc.scalar.copy(
-                out=f_words(c)[:, 1024 * q0 : 1024 * q1].rearrange("p (c i t) -> p c t i", i=4, t=4),
-                in_=f_raw[c][:, :, 256 * q0 : 256 * q1].rearrange("p t (c i) -> p c t i", i=4),
+                out=f_words(c)[:, 1024 * q0 : 1024 * q1].rearrange("p (c i t) -> p c t i", i=2, t=4),
+                in_=f_raw[c][:, :, 256 * q0 : 256 * q1].rearrange("p t (c i) -> p c t i", i=2),
             )
 
         def f_quant(c0, c1):
@@ -383,7 +383,7 @@ def tile_ftn_residual_turn_s9_kernel(tc, lam, amp, h_words, h_scales, y, v, f, o
         scalar = [(x_tanh, 0, 0, 1), (x_tanh, 0, 1, 2), (x_tanh, 1), (x_tanh, 2), (x_tanh, 3), (f_copy, 0), (v_copy, 0), (v_copy, 1)]
         scalar.extend([(x_tanh, 4), (x_tanh, 5), (f_copy, 1), (f_copy, 2)] + across(r_copy, 0)[:2] + [(f_copy, 3), (x_tanh, 6)] + across(r_copy, 0)[2:])
         scalar.extend([(f_copy, 4), (f_copy, 5), (f_copy, 6), (f_copy, 7, 0, 1)] + across(r_copy, 2)[:2] + [(f_copy, 7, 1, 2)] + across(r_copy, 2)[2:])
-        scalar.extend([(x_tanh, 7), (park, 1, 0), (park, 0, 1)] + across(r_copy, 4)[:2] + across(r_copy, 4)[2:] + left(r_copy, 6))
+        scalar.extend([(x_tanh, 7), (park, 1, 0), (park, 0, 1)] + across(r_copy, 4) + left(r_copy, 6))
 
         windows = [x for x in vector if x[0] == weigh]
 

from contextlib import ExitStack

import concourse.mybir as mybir
from concourse.masks import make_identity

F32 = mybir.dt.float32
BF16 = mybir.dt.bfloat16
I32 = mybir.dt.int32
U32 = mybir.dt.uint32
U8 = mybir.dt.uint8
E4M3X4 = mybir.dt.float8_e4m3fn_x4
E5M2X4 = mybir.dt.float8_e5m2_x4
E2M1X4 = mybir.dt.float4_e2m1fn_x4
ALU = mybir.AluOpType
TANH = mybir.ActivationFunctionType.Tanh

M, K, N = 1024, 1024, 2048
P = 128
FLOPS = 2 * M * K * N * 2
TILES = M // P
KG = K // 512
NG = N // 512
LAST = TILES - 1
PAIRS = TILES // 2
BANKS = 7
XF_BUFS = 2
F_BUFS = 4


def tile_ftn_residual_turn_s9_kernel(tc, lam, amp, h_words, h_scales, y, v, f, out):
    nc = tc.nc
    with ExitStack() as ctx:
        keep = ctx.enter_context(tc.tile_pool(name="keep", bufs=1))
        work = ctx.enter_context(tc.tile_pool(name="work", bufs=2))
        psum = ctx.enter_context(tc.psum_pool(name="psum", bufs=1))
        ctx.enter_context(tc.manual_schedule())

        amp_rows = keep.tile([P, 256], F32, name="amp_rows", align_bytes=64)
        nc.vector.memset(amp_rows[:], 0.0)
        hs = keep.tile([P, KG, N], U8, name="hs", align_bytes=64)
        nc.vector.memset(hs[:].rearrange("p g n -> p (g n)").bitcast(I32), 0)
        ident = keep.tile([P, P], F32, name="ident", align_bytes=64)
        make_identity(nc, ident[:])

        v_in = keep.tile([P, 16], BF16, name="v_in", align_bytes=64)
        v_col = {}
        lam_t, y_t, f_raw, hw = {}, {}, {}, {}

        def load_lam(i, parts=1):
            lam_t[i] = work.tile([P, K], BF16, name="lam_in", bufs=TILES, align_bytes=64)
            for c in range(parts):
                cols = slice(K // parts * c, K // parts * (c + 1))
                nc.sync.dma_start(out=lam_t[i][:, cols], in_=lam[P * i : P * (i + 1), cols])

        def load_y(pair, half, j0=0, j1=2):
            if j0 == 0:
                y_t[pair, half] = work.tile([P, 2, K], BF16, name="y_in", bufs=TILES, align_bytes=64)
            rows = y[P * (2 * pair + j0) : P * (2 * pair + j1), K * half : K * (half + 1)]
            nc.sync.dma_start(out=y_t[pair, half][:, j0:j1], in_=rows.rearrange("(j p) c -> p j c", p=P))

        def load_f(c):
            kh, g = divmod(c, NG)
            f_raw[c] = work.tile([P, 4, 512], BF16, name="f_raw", bufs=2 * NG, align_bytes=64)
            nc.sync.dma_start(
                out=f_raw[c][:],
                in_=f[512 * g : 512 * (g + 1), 512 * kh : 512 * (kh + 1)].rearrange("(p j) k -> p j k", j=4),
            )

        def load_h(half):
            hw[half] = work.tile([P, KG, N], U8, name="hw", bufs=2, align_bytes=64)
            nc.sync.dma_start(
                out=hw[half][:].bitcast(I32),
                in_=h_words[:, :, N * half : N * (half + 1)].rearrange("g p c -> p g c").bitcast(I32),
            )

        def load_scales():
            for r in range(4):
                nc.sync.dma_start(
                    out=hs[r:P:32].bitcast(I32),
                    in_=h_scales[:, r:16:4].rearrange("g q n -> q g n").bitcast(I32),
                )

        def load_v_col(g, queue):
            v_col[g] = work.tile([P, 4], BF16, name="v_col", bufs=2, align_bytes=64)
            queue.dma_start(out=v_col[g][:], in_=v[512 * g : 512 * (g + 1)].rearrange("(q c) -> q c", c=4))

        xf_t = {}
        xb_two = keep.tile([P, 2 * K], BF16, name="xb_two", align_bytes=64)
        xb_one = keep.tile([P, K], BF16, name="xb_one", align_bytes=64)
        x_codes = keep.tile([P, TILES * KG * P], U32, name="x_codes", align_bytes=64)
        x_scales = keep.tile([P, TILES * KG * P], U8, name="x_scales", align_bytes=64)
        t_t, r_at, rc_t, rs_t = {}, {}, {}, {}
        bank_of, free = {}, list(range(BANKS))

        def take(key):
            k = free.pop(0)
            bank_of[key] = (k, psum.tile([P, 4, P], F32, name="bank", tag="bank%d" % k, bufs=1))
            return bank_of[key][1]

        def give(key):
            k, bank = bank_of[key]
            free.append(k)
            return bank

        factors = psum.tile([P, 512], F32, name="factors", tag="factors", bufs=1)
        amp_col = keep.tile([P, 4], F32, name="amp_col", align_bytes=64)

        def amp_turn():
            for u in range(2):
                nc.tensor.transpose(factors[:, u:256:2], amp_rows[:, u:256:2], ident[:])

        def v_col_turn(g):
            words = v_col[g][:].bitcast(F32)
            for u in range(2):
                c = 256 * (g - 2) + P * u
                nc.tensor.transpose(factors[:, c : c + P], words[:, u : u + 1].to_broadcast([P, P]), ident[:])

        def amp_copy():
            nc.vector.tensor_copy(out=amp_col[:], in_=factors[:, 0:4])

        def x_turn(i, g0=0, g1=KG):
            bank = take(("x", i, g0))
            words = lam_t[i][:].bitcast(F32)
            for g in range(g0, g1):
                for u in range(2):
                    nc.tensor.transpose(bank[:, 2 * g + u, :], words[:, 256 * g + u : 256 * (g + 1) : 2], ident[:])

        def x_tanh(i, g0=0, g1=KG):
            if g0 == 0:
                xf_t[i] = work.tile([P, KG, P, 4], F32, name="xf", bufs=XF_BUFS, align_bytes=64)
            bank = give(("x", i, g0))
            for g in range(g0, g1):
                nc.scalar.activation(
                    out=xf_t[i][:, g].rearrange("p m (u e) -> p m u e", u=2),
                    in_=bank[:, 2 * g : 2 * g + 2, :].bitcast(BF16).rearrange("p u (m e) -> p m u e", e=2),
                    func=TANH,
                )

        def xb_of(i):
            return xb_one[:] if i in (0, 6, 7) else xb_two[:, K * (i in (2, 5)) :]

        def x_amp(i, g0=0, g1=KG):
            engine, words = (nc.gpsimd, amp_col[:]) if i == 3 else (nc.vector, factors[:, 0:4])
            factor = words.bitcast(BF16).rearrange("p (g t) -> p g t", g=KG)[:, g0:g1]
            engine.tensor_tensor(
                out=xb_of(i)[:, :K].rearrange("p (g m t) -> p g m t", g=KG, t=4)[:, g0:g1],
                in0=xf_t[i][:, g0:g1],
                in1=factor.unsqueeze(2).to_broadcast([P, g1 - g0, P, 4]),
                op=ALU.mult,
            )

        def x_quant(i, j):
            cols = slice(KG * P * i, KG * P * j)
            nc.vector.quantize_mx(out=x_codes[:, cols].bitcast(E4M3X4), scales=x_scales[:, cols], in_=xb_of(i)[:, : K * (j - i)])

        def first(i, b):
            z = take(("z", i, b))
            half, c = divmod(b, 2)
            for g in range(KG):
                nc.tensor.matmul_mx(
                    out=z[:].rearrange("p a m -> p (a m)"),
                    lhsT=x_codes[:, P * (KG * i + g) : P * (KG * i + g + 1)].bitcast(E4M3X4),
                    lhsT_scale=x_scales[:, P * (KG * i + g) : P * (KG * i + g + 1)],
                    rhs=hw[half][:, g, 1024 * c : 1024 * (c + 1)].bitcast(E2M1X4),
                    rhs_scale=hs[:, g, 512 * b : 512 * (b + 1)],
                    start=(g == 0),
                    stop=(g == KG - 1),
                )

        def t_col(i, b):
            pair, j = divmod(i, 2)
            return 512 * (NG * j + b if pair == PAIRS - 1 else 2 * b + j)

        def sub(i, b):
            if i // 2 not in t_t:
                t_t[i // 2] = work.tile([P, 2 * N], F32, name="t", bufs=2, align_bytes=64)
            c = t_col(i, b)
            nc.vector.tensor_sub(
                out=t_t[i // 2][:, c : c + 512].rearrange("p (u q e) -> p u q e", u=2, e=2),
                in0=y_t[i // 2, b // 2][:, i % 2, 512 * (b % 2) : 512 * (b % 2 + 1)].rearrange("p (q u e) -> p u q e", u=2, e=2),
                in1=give(("z", i, b))[:].rearrange("p a (q u e) -> p u (a q) e", u=2, e=2),
            )

        v_rows = keep.tile([P, NG * 256], F32, name="v_rows", align_bytes=64)

        def v_turn(u):
            bank = take(("v", u))
            words = v_in[:].bitcast(F32)
            for i in range(4):
                w = 2 * i + u
                nc.tensor.transpose(bank[:, i, :], words[:, w : w + 1].to_broadcast([P, P]), ident[:])

        def v_copy(u):
            nc.scalar.copy(
                out=v_rows[:].rearrange("p (g u q i) -> p g u q i", g=NG, u=2, i=4)[:, :, u],
                in_=give(("v", u))[:].rearrange("p i (g q) -> p g q i", g=NG),
            )

        stage = [keep.tile([P, 2 * N], BF16, name="stage_a", align_bytes=64), keep.tile([P, 2 * N], BF16, name="stage_b", align_bytes=64)]
        f_ring = keep.tile([P, F_BUFS * 2048], BF16, name="f_ring", align_bytes=64)

        def f_words(c, count=1):
            return f_ring[:, 2048 * (c % F_BUFS) : 2048 * (c % F_BUFS + count)]

        def r_space(i, b0):
            if i == 0:
                return f_words(0) if b0 == 0 else stage[0][:, :N]
            if i == LAST - 1:
                return f_words(2 * NG - 1)[:, 512 * b0 :]
            if i == LAST:
                return stage[1][:, 512 * b0 : 512 * b0 + 1024]
            return stage[i // 2 % 2][:, 1024 * b0 :]

        def weigh(i, j, b0, b1):
            tiles, groups = j - i, b1 - b0
            width = 512 * tiles * groups
            dst = r_space(i, b0)[:, :width]
            for b in range(b0, b1):
                for a in range(tiles):
                    c = 512 * (tiles * (b - b0) + a)
                    r_at[i + a, b] = dst[:, c : c + 512]
            by_vector = b1 == NG and i > 0
            if by_vector:
                engine, rows = nc.vector, factors[:].bitcast(BF16)[:, 512 * (b0 - 2) :]
            else:
                engine, rows = nc.gpsimd, v_rows[:].bitcast(BF16)[:, 512 * b0 : 512 * b1]
            c = t_col(i, b0)
            src = t_t[i // 2][:, c : c + width]
            if tiles > 1:
                rows = rows.rearrange("p (g c) -> p g c", c=512).unsqueeze(2).to_broadcast([P, groups, tiles, 512])
                src = src.rearrange("p (g a c) -> p g a c", a=tiles, c=512)
                dst = dst.rearrange("p (g a c) -> p g a c", a=tiles, c=512)
            engine.tensor_tensor(out=dst, in0=src, in1=rows, op=ALU.mult)

        def r_turn(i, half):
            bank = take(("r", i, half))
            for a in range(4):
                g, u = divmod(a, 2)
                nc.tensor.transpose(bank[:, a, :], r_at[i, 2 * half + g][:, 256 * u : 256 * (u + 1)].bitcast(F32), ident[:])

        def r_slot(i, half):
            return 2 * (1 - half) + i % 2 if i < LAST - 1 else 2 * (i % 2) + half

        def r_words(i, half):
            slot = r_slot(i, half)
            return stage[(i // 2 + 1) % 2][:, 1024 * slot : 1024 * (slot + 1)]

        def r_copy(i, half):
            nc.scalar.copy(
                out=r_words(i, half).bitcast(F32).rearrange("p (g m u) -> p g m u", m=P, u=2),
                in_=give(("r", i, half))[:].rearrange("p (g u) m -> p g m u", u=2),
            )

        def r_quant(pair, part):
            if pair not in rc_t:
                rc_t[pair] = work.tile([P, 2 * NG * P], U32, name="rc", bufs=PAIRS, align_bytes=64)
                rs_t[pair] = work.tile([P, 2 * NG * P], U8, name="rs", bufs=PAIRS, align_bytes=64)
            nc.vector.quantize_mx(
                out=rc_t[pair][:, 512 * part : 512 * (part + 1)].bitcast(E5M2X4),
                scales=rs_t[pair][:, 512 * part : 512 * (part + 1)],
                in_=stage[(pair + 1) % 2][:, N * part : N * (part + 1)],
            )

        f_codes = keep.tile([P, 2 * NG * 512], U32, name="f_codes", align_bytes=64)
        f_scales = keep.tile([P, 2 * NG * 512], U8, name="f_scales", align_bytes=64)

        def f_copy(c, q0=0, q1=2):
            nc.scalar.copy(
                out=f_words(c)[:, 1024 * q0 : 1024 * q1].rearrange("p (c i t) -> p c t i", i=2, t=4),
                in_=f_raw[c][:, :, 256 * q0 : 256 * q1].rearrange("p t (c i) -> p c t i", i=2),
            )

        def f_quant(c0, c1):
            nc.vector.quantize_mx(
                out=f_codes[:, 512 * c0 : 512 * c1].bitcast(E4M3X4),
                scales=f_scales[:, 512 * c0 : 512 * c1],
                in_=f_words(c0, c1 - c0),
            )

        def second(i, c0, c1=None, h0=0, h1=2):
            c0, c1 = (2 * c0, 2 * c0 + 2) if c1 is None else (c0, c1)
            d = take(("d", i, c0)) if h0 == 0 else bank_of["d", i, c0][1]
            kh, q = divmod(c0, 2)
            width = 256 * (c1 - c0)
            for g in range(2 * h0, 2 * h1):
                c = 512 * (NG * kh + g) + 256 * q
                a = 256 * r_slot(i, g // 2) + P * (g % 2)
                nc.tensor.matmul_mx(
                    out=d[:].rearrange("p a m -> p (a m)")[:, :width],
                    lhsT=rc_t[i // 2][:, a : a + P].bitcast(E5M2X4),
                    lhsT_scale=rs_t[i // 2][:, a : a + P],
                    rhs=f_codes[:, c : c + width].bitcast(E4M3X4),
                    rhs_scale=f_scales[:, c : c + width],
                    start=(g == 0),
                    stop=(g == NG - 1),
                )

        def add(i, c0, c1=None):
            c0, c1 = (2 * c0, 2 * c0 + 2) if c1 is None else (c0, c1)
            width = 256 * (c1 - c0)
            d = give(("d", i, c0))[:].rearrange("p a m -> p (a m)")
            cols = slice(256 * c0, 256 * c1)
            o = y_t[i // 2, c0 // 2][:, i % 2].bitcast(F32)[:, 256 * (c0 % 2) : 256 * (c0 % 2) + width]
            nc.vector.tensor_add(out=o, in0=d[:, :width], in1=lam_t[i][:, cols])
            nc.sync.dma_start(out=out[P * i : P * (i + 1), cols], in_=o)

        parked = {}

        def park(i, kh):
            parked[i, kh] = work.tile([P, 512], F32, name="parked", bufs=3, align_bytes=64)
            nc.scalar.copy(out=parked[i, kh][:], in_=give(("d", i, 2 * kh))[:].rearrange("p a m -> p (a m)"))

        def late_add(i, kh, slot):
            o = stage[0][:, 1024 * slot : 1024 * (slot + 1)].bitcast(F32)
            cols = slice(512 * kh, 512 * (kh + 1))
            nc.gpsimd.tensor_tensor(out=o, in0=parked[i, kh][:], in1=lam_t[i][:, cols], op=ALU.add)
            nc.sync.dma_start(out=out[P * i : P * (i + 1), cols], in_=o)

        nc.scalar.dma_start(out=v_in[:], in_=v.rearrange("(q c) -> q c", c=16))
        load_v_col(3, nc.scalar)
        load_lam(0, 2)
        nc.sync.dma_start(out=amp_rows[0:KG, :].bitcast(BF16), in_=amp.rearrange("(g c) -> g c", g=KG))
        for i in range(1, 4):
            load_lam(i)
        load_scales()
        load_h(0)
        load_f(0)
        load_y(0, 0, 0, 1)
        load_y(0, 0, 1, 2)
        load_lam(4)
        load_lam(5)
        load_h(1)
        load_y(0, 1)
        load_f(1)
        for half in range(2):
            load_f(2 + half)
            load_y(1, half)
        for half in range(2):
            load_lam(6 + half)
            load_f(4 + 2 * half)
            load_y(2, half)
            load_f(5 + 2 * half)
        load_y(3, 0)
        load_y(3, 1)
        load_v_col(2, nc.sync)

        def halves(call, i):
            return [(call, i, 0), (call, i, 1)]

        def left(call, i):
            return [(call, i, 0), (call, i, 1), (call, i + 1, 0), (call, i + 1, 1)]

        def right(call, i):
            return [(call, i, 2), (call, i + 1, 2), (call, i, 3), (call, i + 1, 3)]

        def across(call, i):
            return [(call, i, 0), (call, i + 1, 0), (call, i, 1), (call, i + 1, 1)]

        vector = [(x_amp, 0, 0, 1), (x_amp, 0, 1, 2), (amp_copy,), (x_quant, 0, 1), (x_amp, 1), (x_amp, 2), (x_quant, 1, 2), (x_quant, 2, 3), (x_amp, 3)]
        vector.extend(left(sub, 0) + [(f_quant, 0, 1), (x_quant, 3, 4), (weigh, 0, 2, 0, 2)])
        vector.extend(right(sub, 0)[:2] + [(x_amp, 4)] + right(sub, 0)[2:] + [(weigh, 0, 2, 2, 4), (x_amp, 5)] + left(sub, 2) + right(sub, 2)[:3])
        vector.extend([(x_quant, 4, 6), (f_quant, 1, 2), (f_quant, 2, 3), (f_quant, 3, 4)] + [(r_quant, 0, 1), (r_quant, 0, 0)] + [(weigh, 2, 4, 0, 2), (weigh, 2, 4, 2, 3)])
        vector.extend([(sub, 3, 3), (sub, 4, 0), (weigh, 2, 4, 3, 4), (sub, 4, 1), (add, 0, 0), (sub, 5, 0), (x_amp, 6), (sub, 5, 1)] + right(sub, 4)[:3])
        vector.extend([(x_quant, 6, 7), (f_quant, 4, 5), (f_quant, 5, 6), (f_quant, 6, 7), (f_quant, 7, 8)] + [(r_quant, 1, 1), (r_quant, 1, 0)])
        vector.extend([(weigh, 4, 6, 0, 2), (weigh, 4, 6, 2, 3)])
        vector.extend([(sub, 5, 3), (sub, 6, 0), (x_amp, 7), (add, 1, 2, 4), (weigh, 4, 6, 3, 4), (sub, 6, 2), (sub, 6, 3), (add, 2, 0), (add, 2, 1), (sub, 6, 1)])
        vector.extend([(x_quant, 7, 8), (weigh, 6, 7, 0, 2), (add, 3, 0), (weigh, 6, 7, 2, 4), (sub, 7, 0), (sub, 7, 1)])
        vector.extend([(r_quant, 2, 1), (r_quant, 2, 0)] + [(weigh, 7, 8, 0, 2), (sub, 7, 2), (sub, 7, 3), (add, 3, 1), (weigh, 7, 8, 2, 4)])
        vector.extend([(r_quant, 3, 0), (add, 4, 0), (add, 4, 1), (late_add, 1, 0, 0), (add, 5, 0), (r_quant, 3, 1), (add, 5, 1), (add, 6, 0), (late_add, 0, 1, 2)])
        vector.extend([(add, 6, 1), (add, LAST, 0), (add, LAST, 2, 3), (add, LAST, 3, 4)])

        tensor = [(x_turn, 0, 0, 1), (amp_turn,), (x_turn, 0, 1, 2), (x_turn, 1), (x_turn, 2), (x_turn, 3)] + halves(first, 0)
        tensor.extend([(v_turn, 0), (v_turn, 1)] + halves(first, 1) + [(x_turn, 4), (x_turn, 5)] + right(first, 0) + left(first, 2) + right(first, 2)[:2])
        tensor.extend(across(r_turn, 0)[:2] + [(v_col_turn, 3)] + right(first, 2)[2:])
        tensor.extend([(x_turn, 6)] + across(r_turn, 0)[2:] + halves(first, 4) + [(second, 0, 0)] + halves(first, 5) + right(first, 4)[:2])
        tensor.extend([(x_turn, 7)] + right(first, 4)[2:])
        tensor.extend(across(r_turn, 2)[:2] + [(second, 1, 0)] + across(r_turn, 2)[2:] + [(first, 6, 0)])
        tensor.extend([(second, i, 2, 4, h, h + 1) for h in range(2) for i in range(2)])
        tensor.extend([(first, 6, 2), (first, 6, 3), (second, 2, 0), (second, 2, 1), (first, 6, 1), (second, 3, 0), (v_col_turn, 2)] + across(r_turn, 4)[:2])
        tensor.extend([(second, 3, 1)] + across(r_turn, 4)[2:] + [(first, 7, b) for b in range(NG)] + halves(r_turn, 6))
        tensor.extend(left(second, 4)[:3] + halves(r_turn, 7) + [(second, 5, 1)] + left(second, 6)[:3] + [(second, LAST, 2, 3), (second, LAST, 3, 4)])

        scalar = [(x_tanh, 0, 0, 1), (x_tanh, 0, 1, 2), (x_tanh, 1), (x_tanh, 2), (x_tanh, 3), (f_copy, 0), (v_copy, 0), (v_copy, 1)]
        scalar.extend([(x_tanh, 4), (x_tanh, 5), (f_copy, 1), (f_copy, 2)] + across(r_copy, 0)[:2] + [(f_copy, 3), (x_tanh, 6)] + across(r_copy, 0)[2:])
        scalar.extend([(f_copy, 4), (f_copy, 5), (f_copy, 6), (f_copy, 7, 0, 1)] + across(r_copy, 2)[:2] + [(f_copy, 7, 1, 2)] + across(r_copy, 2)[2:])
        scalar.extend([(x_tanh, 7), (park, 1, 0), (park, 0, 1)] + across(r_copy, 4) + left(r_copy, 6))

        windows = [x for x in vector if x[0] == weigh]

        def needs(step):
            call, i = step[0], step[1] if len(step) > 1 else 0
            if call == x_tanh:
                return [(x_turn, *step[1:])] + [(x_amp, k) if k else (x_amp, 0, 1, 2) for k in (i - XF_BUFS,) if k >= 0]
            if call == x_amp:
                return [(x_tanh, *step[1:]), (amp_turn,)]
            if call == first:
                return [x for x in quants if x[0] == x_quant and x[1] <= i < x[2]]
            if call == weigh:
                return [(v_copy, 1)] + [(v_col_turn, 2)][: i // (LAST - 1)]
            if call == v_col_turn:
                return [(x_amp, LAST), (weigh, 4, 6, 3, 4)] if i == 2 else [(x_amp, 5)]
            if call == r_turn:
                return [w for w in windows if w[1] <= i < w[2] and w[3] < 2 * step[2] + 2 and w[4] > 2 * step[2]]
            if call == f_copy:
                return [x for x in quants if x[0] == f_quant and x[1] <= i - F_BUFS < x[2]] + across(r_turn, 0)[: 2 * (i == F_BUFS)]
            if call == f_quant:
                return [(f_copy, step[2] - 1) if step[2] < 2 * NG else (f_copy, 7, 1, 2)]
            if call == second:
                h = step[5] - 1 if len(step) > 4 else 1
                kh = step[2] // 2 if len(step) > 3 else step[2]
                return [(r_quant, i // 2, r_slot(i, h) // 2)] + [x for x in quants if x[0] == f_quant and x[2] == NG * kh + 2 * h + 2]
            if call == add:
                return [x for x in tensor_all if x[: len(step)] == (second, *step[1:])]
            if call == park:
                return [x for x in tensor_all if x[:3] == (second, *step[1:]) or x[:4] == (second, i, 2 * step[2], 2 * step[2] + 2)]
            if call == late_add:
                return [(park, i, step[2])]
            if call == r_quant:
                return [(r_copy, a, h) for a in (2 * i, 2 * i + 1) for h in range(2) if r_slot(a, h) // 2 == step[2]]
            producer = {sub: first, v_copy: v_turn, r_copy: r_turn}
            return [(producer[call], *step[1:])] if call in producer else []

        tensor_all = list(tensor)
        quants = [x for x in vector if x[0] in (x_quant, f_quant)]
        queue_of = {}
        for queue in (tensor, scalar, vector):
            for step in queue:
                queue_of[step] = queue
        written = set()

        def write(step):
            queue = queue_of[step]
            while step not in written:
                head = queue[0]
                for other in needs(head):
                    write(other)
                if head not in written:
                    head[0](*head[1:])
                    written.add(queue.pop(0))
                if scalar and all(other in written for other in needs(scalar[0])):
                    write(scalar[0])

        for step in list(vector):
            write(step)
